import numpy as np
import ml_dtypes


def mxq(x, axis, fmt="e4m3"):
    dtype, down = {"e4m3": (ml_dtypes.float8_e4m3fn, 7), "e5m2": (ml_dtypes.float8_e5m2, 14)}[fmt]
    v = np.moveaxis(np.asarray(x, np.float32).astype(ml_dtypes.bfloat16).astype(np.float64), axis, -1)
    blocks = v.reshape(v.shape[:-1] + (-1, 32))
    amax = np.abs(blocks).max(-1, keepdims=True)
    byte = np.maximum(np.where(amax > 0, np.frexp(amax)[1] - 1 + 127, 0) - down, 1)
    scale = np.exp2(byte - 127.0)
    codes = (blocks / scale).astype(np.float32).astype(dtype).astype(np.float64)
    return np.moveaxis((codes * scale).reshape(v.shape), -1, axis)


WIDE = False


def mx_kscale(k):
    if not WIDE:
        return np.ones(k)
    levels = np.array([10, -10, 5, -5, 0])
    if k % 512:
        return np.exp2(np.random.permutation(np.resize(levels, k // 32))).repeat(32)
    a = np.empty((k // 512, 16))
    for p in range(k // 512):
        a[p, :8] = np.random.permutation(np.resize(levels, 8))
        for g in range(8):
            far = levels[np.abs(levels - a[p, g]) >= 10]
            a[p, g + 8] = far[np.random.randint(len(far))]
    return np.exp2(a.ravel()).repeat(32)


BF16 = ml_dtypes.bfloat16


def bf(x):
    return np.asarray(x, np.float32).astype(BF16)


def f64(x):
    return np.asarray(x).astype(np.float64)


E2M1 = np.array([0.0, 0.5, 1.0, 1.5, 2.0, 3.0, 4.0, 6.0, -0.0, -0.5, -1.0, -1.5, -2.0, -3.0, -4.0, -6.0])


def pack_weight(w, fmt):
    k, n = w.shape
    w = f64(bf(w)).reshape(k // 32, 32, n)
    amax = np.abs(w).max(1)
    if fmt == "e4m3":
        byte = np.frexp(amax)[1] - 1 + 127 - 7
    else:
        mant, ex = np.frexp(amax / 6.0)
        byte = np.where(mant > 0.5, ex, ex - 1) + 127
    byte = np.clip(np.where(amax > 0, byte, 1), 1, 254)
    scaled = (w * np.exp2(127.0 - byte)[:, None, :]).reshape(k, n).astype(np.float32)
    by_word = np.ascontiguousarray(scaled.reshape(k // 512, 128, 4, n).transpose(0, 1, 3, 2))
    if fmt == "e4m3":
        words = by_word.astype(ml_dtypes.float8_e4m3fn).view(np.uint8)
    else:
        c = by_word.astype(ml_dtypes.float4_e2m1fn).view(np.uint8) & 0xF
        words = c[..., 0::2] | (c[..., 1::2] << 4)
    return np.ascontiguousarray(words), np.ascontiguousarray(byte.astype(np.uint8).reshape(k // 512, 16, n))


def unpack_weight(words, scales, fmt):
    g, p, n, _ = words.shape
    if fmt == "e4m3":
        vals = np.ascontiguousarray(words).view(ml_dtypes.float8_e4m3fn).astype(np.float64)
    else:
        nib = np.empty((g, p, n, 4), np.uint8)
        nib[..., 0::2] = words & 0xF
        nib[..., 1::2] = words >> 4
        vals = E2M1[nib]
    vals = vals * np.repeat(np.exp2(scales.astype(np.float64) - 127.0), 8, axis=1)[..., None]
    return vals.transpose(0, 1, 3, 2).reshape(g * 512, n)
def pack4(w):
    words, scales = pack_weight(w, "e2m1")
    return words.reshape(words.shape[0], 128, -1), scales


def unpack4(words, scales):
    return unpack_weight(words.reshape(words.shape[0], 128, -1, 2), scales, "e2m1")


L, K, R, N, C = 1024, 2048, 1024, 1024, 2


def setup_inputs():
    s, t, v = mx_kscale(K), mx_kscale(R), mx_kscale(R)
    x = np.random.standard_normal((L, K)) * s
    comp = np.random.standard_normal((K, R)) / np.sqrt(K) / s[:, None] * t
    a = np.random.standard_normal((R, R)) / np.sqrt(R) * v[:, None] / t
    d = 4 * np.random.standard_normal((R, N)) / np.sqrt(R) / v[:, None]
    a_words, a_scales = pack4(a)
    d_words, d_scales = pack4(d)
    return {"x": bf(x),
            "comp": bf(comp),
            "gain": bf(1 + 0.1 * np.random.standard_normal(R)),
            "a_words": a_words, "a_scales": a_scales,
            "d_words": d_words, "d_scales": d_scales,
            "copy_gain": bf(1 + 0.1 * np.random.standard_normal((C, N))),
            "base": bf(np.random.standard_normal((L, C * N)))}


def reference(x, comp, gain, a_words, a_scales, d_words, d_scales, copy_gain, base):
    z = (mxq(f64(x), 1, "e4m3") @ mxq(f64(comp), 0, "e4m3")) * f64(gain)
    e = unpack4(a_words, a_scales).T @ unpack4(d_words, d_scales)
    y = mxq(z, 1, "e4m3") @ mxq(e, 0, "e4m3")
    out = f64(base).reshape(L, C, N) + y[:, None, :] * f64(copy_gain)
    return out.reshape(L, C * N)

@@ -1,0 +1,468 @@
+from contextlib import ExitStack
+
+import concourse.mybir as mybir
+from concourse.masks import make_identity
+
+F32 = mybir.dt.float32
+BF16 = mybir.dt.bfloat16
+I32 = mybir.dt.int32
+U32 = mybir.dt.uint32
+U8 = mybir.dt.uint8
+MXFP8 = mybir.dt.float8_e4m3fn_x4
+MXFP4 = mybir.dt.float4_e2m1fn_x4
+ADD = mybir.AluOpType.add
+MULT = mybir.AluOpType.mult
+COPY = mybir.ActivationFunctionType.Copy
+
+TOKENS, FEATURES, CHANNELS, COLUMNS, COPIES = 1024, 2048, 1024, 1024, 2
+FLOPS = 2 * TOKENS * FEATURES * CHANNELS + 2 * CHANNELS * CHANNELS * COLUMNS + 2 * TOKENS * CHANNELS * COLUMNS
+
+P = 128
+WORD = 4
+PASS = P * WORD
+FEATURE_PASSES = FEATURES // PASS
+CHANNEL_PASSES = CHANNELS // PASS
+RUN = 8
+PAIR = 2 * P
+WORDS = PASS // 2
+HALF = 512
+BLOCKS = HALF // P
+SCALE_ROWS = 4
+GAIN_COLUMNS = CHANNELS // P
+GAIN_ROWS = GAIN_COLUMNS + COPIES * (COLUMNS // P)
+
+
+def tile_mora_repeated_update_s12_kernel(
+    tc, x, comp, gain, a_words, a_scales, d_words, d_scales, copy_gain, base, out
+):
+    nc = tc.nc
+    with ExitStack() as ctx:
+        resident = ctx.enter_context(tc.tile_pool(name="resident", bufs=1))
+        rotating = ctx.enter_context(tc.tile_pool(name="rotating", bufs=2))
+        psum = ctx.enter_context(tc.psum_pool(name="psum", bufs=2))
+        ctx.enter_context(tc.manual_schedule())
+
+        a_codes_raw = resident.tile([P, CHANNEL_PASSES, 2 * CHANNELS], U8, name="a_codes_raw", align_bytes=64)
+        a_codes = resident.tile([P, CHANNEL_PASSES, 2 * CHANNELS], U8, name="a_codes", align_bytes=64)
+        d_codes = resident.tile([P, CHANNEL_PASSES, 2 * COLUMNS], U8, name="d_codes", align_bytes=64)
+        a_scales_raw = resident.tile([P, CHANNEL_PASSES, CHANNELS], U8, name="a_scales_raw", align_bytes=64)
+        a_scales_sb = resident.tile([P, CHANNEL_PASSES, CHANNELS], U8, name="a_scales_sb", align_bytes=64)
+        d_scales_sb = resident.tile([P, CHANNEL_PASSES, COLUMNS], U8, name="d_scales_sb", align_bytes=64)
+        comp_codes = resident.tile([P, FEATURE_PASSES, CHANNELS], U32, name="comp_codes", align_bytes=64)
+        comp_scales = resident.tile([P, FEATURE_PASSES, CHANNELS], U8, name="comp_scales", align_bytes=64)
+        e_codes = resident.tile([P, CHANNEL_PASSES, COLUMNS], U32, name="e_codes", align_bytes=64)
+        e_scales = resident.tile([P, CHANNEL_PASSES, COLUMNS], U8, name="e_scales", align_bytes=64)
+        copy_gain_sb = resident.tile([P, COPIES, COLUMNS], BF16, name="copy_gain_sb", align_bytes=64)
+        identity = resident.tile([P, P], F32, name="identity", align_bytes=64)
+        gain_rows = resident.tile([GAIN_ROWS, P], BF16, name="gain_rows", align_bytes=64)
+        gain_square = resident.tile([P, P], F32, name="gain_square", align_bytes=64)
+        gain_columns = resident.tile([P, GAIN_ROWS], F32, name="gain_columns", align_bytes=64)
+        dummy = resident.tile([P, 1], F32, name="dummy", align_bytes=64)
+
+        nc.vector.memset(a_scales_raw[:].rearrange("p g n -> p (g n)").bitcast(I32), 0)
+        nc.vector.memset(d_scales_sb[:].rearrange("p g n -> p (g n)").bitcast(I32), 0)
+        nc.vector.memset(dummy[:], 0.0)
+        nc.vector.memset(gain_square[:], 0.0)
+        make_identity(nc, identity[:])
+        nc.scalar.activation(out=dummy[:], in_=dummy[:], func=COPY)
+
+        x_rows, comp_rows, base_rows = {}, {}, {}
+
+        def load_x(i):
+            x_rows[i] = rotating.tile([P, FEATURES], BF16, name="x_rows", tag="token_rows", bufs=9, align_bytes=64)
+            nc.sync.dma_start(out=x_rows[i][:], in_=x[P * i : P * (i + 1), :])
+
+        def load_base(i):
+            base_rows[i] = rotating.tile(
+                [P, COPIES, COLUMNS], BF16, name="base_rows", tag="token_rows", bufs=9, align_bytes=64
+            )
+            nc.sync.dma_start(out=base_rows[i][:].rearrange("p c n -> p (c n)"), in_=base[P * i : P * (i + 1), :])
+
+        def load_comp(piece):
+            h, g = divmod(piece, FEATURE_PASSES)
+            comp_rows[piece] = rotating.tile(
+                [P, WORD, PASS], BF16, name="comp_rows", tag="four_kib", bufs=8, align_bytes=64
+            )
+            block = comp[PASS * g : PASS * (g + 1), PASS * h : PASS * (h + 1)]
+            nc.sync.dma_start(out=comp_rows[piece][:], in_=block.rearrange("(p v) r -> p v r", v=WORD))
+
+        def load_codes(tile, words):
+            nc.sync.dma_start(out=tile[:].bitcast(I32), in_=words.rearrange("g p n -> p g n").bitcast(I32))
+
+        def load_scales(tile, scales):
+            for quadrant in range(4):
+                rows = slice(SCALE_ROWS * quadrant, SCALE_ROWS * (quadrant + 1))
+                nc.sync.dma_start(
+                    out=tile[32 * quadrant : 32 * quadrant + SCALE_ROWS, :, :].bitcast(I32),
+                    in_=scales[:, rows, :].rearrange("g r n -> r g n").bitcast(I32),
+                )
+
+        def load_gains():
+            for h in range(CHANNEL_PASSES):
+                nc.sync.dma_start(
+                    out=gain_rows[WORD * h : WORD * (h + 1), :].rearrange("t (q e) -> t q e", e=RUN),
+                    in_=gain[PASS * h : PASS * (h + 1)].rearrange("(q t e) -> t q e", t=WORD, e=RUN),
+                )
+            for c in range(COPIES):
+                first = GAIN_COLUMNS + c * (COLUMNS // P)
+                nc.sync.dma_start(
+                    out=gain_rows[first : first + COLUMNS // P, :],
+                    in_=copy_gain[c, :].rearrange("(b p) -> b p", p=P),
+                )
+
+        x_grouped, x_mx = {}, {}
+
+        def x_transpose(i):
+            s, place = divmod(i, 2)
+            if place == 0:
+                x_grouped[s] = rotating.tile([P, FEATURE_PASSES, PAIR, 2], F32, name="x_grouped", align_bytes=64)
+            words = x_rows[i][:].bitcast(F32)
+            for g0 in range(0, FEATURE_PASSES, 2):
+                bank = psum.tile([P, 4, P], F32, name="turned_ps", bufs=2)
+                for g in (g0, g0 + 1):
+                    for u in range(2):
+                        first = WORDS * g + u
+                        nc.tensor.transpose(bank[:, 2 * (g - g0) + u, :], words[:, first : first + WORDS - 1 : 2], identity[:])
+                nc.scalar.copy(
+                    out=x_grouped[s][:, g0 : g0 + 2, P * place : P * (place + 1), :],
+                    in_=bank[:].rearrange("p (g u) r -> p g r u", u=2),
+                )
+
+        def x_quantize(s):
+            codes = rotating.tile([P, FEATURE_PASSES, PAIR], U32, name="x_codes", bufs=3, align_bytes=64)
+            scales = rotating.tile([P, FEATURE_PASSES, PAIR], U8, name="x_scales", bufs=3, align_bytes=64)
+            nc.vector.quantize_mx(
+                out=codes[:].rearrange("p g r -> p (g r)").bitcast(MXFP8),
+                scales=scales[:].rearrange("p g r -> p (g r)"),
+                in_=x_grouped[s][:].rearrange("p g r u -> p (g r u)").bitcast(BF16),
+            )
+            x_mx[s] = (codes, scales)
+
+        comp_grouped = {}
+
+        def comp_group(piece):
+            comp_grouped[piece] = rotating.tile(
+                [P, WORD, P // RUN, RUN, WORD], BF16, name="comp_grouped", bufs=3, align_bytes=64
+            )
+            nc.vector.tensor_copy(
+                out=comp_grouped[piece][:],
+                in_=comp_rows[piece][:].rearrange("p v (q t e) -> p t q e v", t=WORD, e=RUN),
+            )
+
+        def comp_quantize(piece):
+            h, g = divmod(piece, FEATURE_PASSES)
+            columns = slice(PASS * h, PASS * (h + 1))
+            nc.vector.quantize_mx(
+                out=comp_codes[:, g, columns].bitcast(MXFP8),
+                scales=comp_scales[:, g, columns],
+                in_=comp_grouped[piece][:].rearrange("p t q e v -> p (t q e v)"),
+            )
+
+        def turn_gains():
+            nc.vector.tensor_copy(out=gain_square[0:GAIN_ROWS, :], in_=gain_rows[:])
+            bank = psum.tile([P, 4, P], F32, name="direct_ps", bufs=2)
+            nc.tensor.transpose(bank[:, 0, :], gain_square[:], identity[:])
+            nc.vector.tensor_copy(out=gain_columns[:], in_=bank[:, 0, 0:GAIN_ROWS])
+
+        e_grouped = {}
+
+        def permute_a():
+            for g in range(CHANNEL_PASSES):
+                for target, source, ints in ((a_codes, a_codes_raw, 4), (a_scales_sb, a_scales_raw, 2)):
+                    nc.vector.tensor_copy(
+                        out=target[:, g, :].bitcast(I32).rearrange(
+                            "p (h t q i) -> p h t q i", h=CHANNEL_PASSES, t=WORD, i=ints
+                        ),
+                        in_=source[:, g, :].bitcast(I32).rearrange(
+                            "p (h q t i) -> p h t q i", h=CHANNEL_PASSES, t=WORD, i=ints
+                        ),
+                    )
+
+        def e_matmul(part, side):
+            j, h = divmod(part, CHANNEL_PASSES)
+            if side == 0:
+                e_grouped[part] = rotating.tile([P, HALF, WORD], BF16, name="e_grouped", bufs=4, align_bytes=64)
+            for b in (2 * side, 2 * side + 1):
+                n = HALF * j + P * b
+                bank = psum.tile([P, WORD, P], F32, name="sums_ps", bufs=4)
+                for t in range(WORD):
+                    m = PASS * h + P * t
+                    for g in range(CHANNEL_PASSES):
+                        nc.tensor.matmul_mx(
+                            out=bank[:, t, :],
+                            lhsT=a_codes[:, g, 2 * m : 2 * (m + P)].bitcast(MXFP4),
+                            lhsT_scale=a_scales_sb[:, g, m : m + P],
+                            rhs=d_codes[:, g, 2 * n : 2 * (n + P)].bitcast(MXFP4),
+                            rhs_scale=d_scales_sb[:, g, n : n + P],
+                            start=(g == 0),
+                            stop=(g == CHANNEL_PASSES - 1),
+                        )
+                nc.scalar.copy(
+                    out=e_grouped[part][:, P * b : P * (b + 1), :], in_=bank[:].rearrange("p t n -> p n t")
+                )
+
+        def e_quantize(part):
+            j, h = divmod(part, CHANNEL_PASSES)
+            columns = slice(HALF * j, HALF * (j + 1))
+            nc.vector.quantize_mx(
+                out=e_codes[:, h, columns].bitcast(MXFP8),
+                scales=e_scales[:, h, columns],
+                in_=e_grouped[part][:].rearrange("p n t -> p (n t)"),
+            )
+
+        z_rounded, z_grouped, z_mx = {}, {}, {}
+
+        def z_matmul(s, h):
+            codes, scales = x_mx[s]
+            z_rounded[(s, h)] = rotating.tile([P, WORD, PAIR], BF16, name="z_rounded", bufs=3, align_bytes=64)
+            for i in range(WORD // 2):
+                bank = psum.tile([P, 2, PAIR], F32, name="sums_ps", bufs=4)
+                for t in (2 * i, 2 * i + 1):
+                    m = PASS * h + P * t
+                    for g in range(FEATURE_PASSES):
+                        nc.tensor.matmul_mx(
+                            out=bank[:, t - 2 * i, :],
+                            lhsT=comp_codes[:, g, m : m + P].bitcast(MXFP8),
+                            lhsT_scale=comp_scales[:, g, m : m + P],
+                            rhs=codes[:, g, :].bitcast(MXFP8),
+                            rhs_scale=scales[:, g, :],
+                            start=(g == 0),
+                            stop=(g == FEATURE_PASSES - 1),
+                        )
+                for t in (2 * i, 2 * i + 1):
+                    column = WORD * h + t
+                    nc.scalar.activation(
+                        out=z_rounded[(s, h)][:, t, :],
+                        in_=bank[:, t - 2 * i, :],
+                        func=COPY,
+                        scale=gain_columns[:, column : column + 1],
+                    )
+
+        def z_group(s, h, copy):
+            z_grouped[(s, h)] = rotating.tile([P, PAIR, WORD], BF16, name="z_grouped", bufs=4, align_bytes=64)
+            copy(
+                out=z_grouped[(s, h)][:].rearrange("p (k i) t -> p k t i", i=4),
+                in_=z_rounded[(s, h)][:].rearrange("p t (k i) -> p k t i", i=4),
+            )
+
+        def z_quantize(s, h):
+            codes = rotating.tile([P, PAIR], U32, name="z_codes", bufs=8, align_bytes=64)
+            scales = rotating.tile([P, PAIR], U8, name="z_scales", bufs=8, align_bytes=64)
+            nc.vector.quantize_mx(
+                out=codes[:].bitcast(MXFP8),
+                scales=scales[:],
+                in_=z_grouped[(s, h)][:].rearrange("p r t -> p (r t)"),
+            )
+            z_mx[(s, h)] = (codes, scales)
+
+        products = {}
+
+        def y_direct(i, j):
+            s, place = divmod(i, 2)
+            columns = slice(HALF * j, HALF * (j + 1))
+            bank = psum.tile([P, HALF], F32, name="direct_ps", bufs=2)
+            for h in range(CHANNEL_PASSES):
+                codes, scales = z_mx[(s, h)]
+                nc.tensor.matmul_mx(
+                    out=bank[:],
+                    lhsT=codes[:, P * place : P * (place + 1)].bitcast(MXFP8),
+                    lhsT_scale=scales[:, P * place : P * (place + 1)],
+                    rhs=e_codes[:, h, columns].bitcast(MXFP8),
+                    rhs_scale=e_scales[:, h, columns],
+                    start=(h == 0),
+                    stop=(h == CHANNEL_PASSES - 1),
+                )
+            products[(i, j)] = rotating.tile(
+                [P, COPIES, HALF], F32, name="product", tag="four_kib", bufs=8, align_bytes=64
+            )
+            nc.vector.tensor_tensor(
+                out=products[(i, j)][:],
+                in0=bank[:].unsqueeze(1).to_broadcast([P, COPIES, HALF]),
+                in1=copy_gain_sb[:, :, columns],
+                op=MULT,
+            )
+
+        def add_base(i, j):
+            columns = slice(HALF * j, HALF * (j + 1))
+            product = products[(i, j)]
+            nc.vector.tensor_tensor(out=product[:], in0=product[:], in1=base_rows[i][:, :, columns], op=ADD)
+            rows = out[P * i : P * (i + 1), :].rearrange("p (c n) -> p c n", c=COPIES)
+            nc.sync.dma_start(out=rows[:, :, columns], in_=product[:])
+
+        turned_products = {}
+
+        def y_transposed(s, j):
+            banks = []
+            for b in range(BLOCKS):
+                if b % 2 == 0:
+                    banks.append(psum.tile([P, 2, PAIR], F32, name="sums_ps", bufs=4))
+                columns = slice(HALF * j + P * b, HALF * j + P * (b + 1))
+                for h in range(CHANNEL_PASSES):
+                    codes, scales = z_mx[(s, h)]
+                    nc.tensor.matmul_mx(
+                        out=banks[b // 2][:, b % 2, :],
+                        lhsT=e_codes[:, h, columns].bitcast(MXFP8),
+                        lhsT_scale=e_scales[:, h, columns],
+                        rhs=codes[:].bitcast(MXFP8),
+                        rhs_scale=scales[:],
+                        start=(h == 0),
+                        stop=(h == CHANNEL_PASSES - 1),
+                    )
+            turned = rotating.tile([P, COPIES, BLOCKS, PAIR], F32, name="turned", align_bytes=64)
+            for c in range(COPIES):
+                for b in range(BLOCKS):
+                    column = GAIN_COLUMNS + c * (COLUMNS // P) + BLOCKS * j + b
+                    nc.scalar.activation(
+                        out=turned[:, c, b, :],
+                        in_=banks[b // 2][:, b % 2, :],
+                        func=COPY,
+                        scale=gain_columns[:, column : column + 1],
+                    )
+            turned_products[(s, j)] = turned
+
+        def turn_back(i, j, c):
+            s, place = divmod(i, 2)
+            bank = psum.tile([P, BLOCKS, P], F32, name="turned_ps", bufs=2)
+            for b in range(BLOCKS):
+                nc.tensor.transpose(
+                    bank[:, b, :], turned_products[(s, j)][:, c, b, P * place : P * (place + 1)], identity[:]
+                )
+            total = rotating.tile([P, HALF], F32, name="total", bufs=8, align_bytes=64)
+            nc.vector.tensor_tensor(
+                out=total[:],
+                in0=bank[:].rearrange("p b n -> p (b n)"),
+                in1=base_rows[i][:, c, HALF * j : HALF * (j + 1)],
+                op=ADD,
+            )
+            first = COLUMNS * c + HALF * j
+            nc.sync.dma_start(out=out[P * i : P * (i + 1), first : first + HALF], in_=total[:])
+
+        load_comp(0)
+        load_scales(a_scales_raw, a_scales)
+        load_x(0)
+        load_codes(a_codes_raw, a_words)
+        load_codes(d_codes, d_words)
+        load_scales(d_scales_sb, d_scales)
+        load_comp(1)
+        load_x(1)
+        load_comp(2)
+        load_x(2)
+        load_gains()
+        load_x(3)
+        for piece in range(3, 7):
+            load_comp(piece)
+        load_x(4)
+        load_comp(7)
+        for i in range(5, 8):
+            load_x(i)
+        nc.sync.dma_start(
+            out=copy_gain_sb[:].rearrange("p c n -> p (c n)"),
+            in_=copy_gain.rearrange("c n -> (c n)").partition_broadcast(P),
+        )
+        for i in range(TOKENS // P):
+            load_base(i)
+
+        comp_group(0)
+        permute_a()
+        x_transpose(0)
+        comp_quantize(0)
+        e_matmul(0, 0)
+        e_matmul(0, 1)
+        x_transpose(1)
+        comp_group(1)
+        e_matmul(1, 0)
+        comp_quantize(1)
+        comp_group(2)
+        x_transpose(2)
+        e_quantize(0)
+        e_matmul(1, 1)
+        x_transpose(3)
+        e_matmul(2, 0)
+        x_quantize(0)
+        comp_quantize(2)
+        e_matmul(2, 1)
+        e_matmul(3, 0)
+        x_transpose(4)
+        for piece in range(3, 6):
+            comp_group(piece)
+        for piece in range(3, 6):
+            comp_quantize(piece)
+
+        turn_gains()
+        comp_group(6)
+        z_matmul(0, 0)
+        x_transpose(5)
+        comp_group(7)
+        z_group(0, 0, nc.scalar.copy)
+        comp_quantize(6)
+        comp_quantize(7)
+        e_quantize(1)
+        x_quantize(1)
+        e_matmul(3, 1)
+        x_quantize(2)
+        e_quantize(2)
+        z_matmul(0, 1)
+        x_transpose(6)
+        e_quantize(3)
+        z_group(0, 1, nc.vector.tensor_copy)
+        z_matmul(1, 0)
+        z_quantize(0, 0)
+        z_quantize(0, 1)
+
+        y_direct(0, 0)
+        z_group(1, 0, nc.scalar.copy)
+        y_direct(1, 0)
+        x_transpose(7)
+        add_base(0, 0)
+        z_matmul(2, 0)
+        x_quantize(3)
+        z_quantize(1, 0)
+        y_direct(0, 1)
+        z_group(2, 0, nc.scalar.copy)
+        z_matmul(1, 1)
+        z_group(1, 1, nc.scalar.copy)
+        add_base(1, 0)
+        z_quantize(2, 0)
+        add_base(0, 1)
+        z_matmul(2, 1)
+        z_quantize(1, 1)
+        z_group(2, 1, nc.scalar.copy)
+        y_direct(1, 1)
+        z_matmul(3, 1)
+        add_base(1, 1)
+        z_group(3, 1, nc.scalar.copy)
+        z_quantize(2, 1)
+        y_direct(2, 0)
+        y_direct(3, 0)
+
+        y_transposed(2, 0)
+        add_base(2, 0)
+        y_direct(2, 1)
+        y_transposed(2, 1)
+        y_direct(3, 1)
+        turn_back(4, 0, 0)
+        z_matmul(3, 0)
+        add_base(3, 0)
+        turn_back(4, 0, 1)
+        turn_back(5, 0, 0)
+        z_group(3, 0, nc.scalar.copy)
+        z_quantize(3, 1)
+        turn_back(5, 0, 1)
+        turn_back(4, 1, 0)
+        z_quantize(3, 0)
+        turn_back(4, 1, 1)
+        turn_back(5, 1, 0)
+        add_base(2, 1)
+        y_transposed(3, 0)
+        turn_back(5, 1, 1)
+        add_base(3, 1)
+
+        turn_back(6, 0, 0)
+        y_transposed(3, 1)
+        turn_back(6, 0, 1)
+        turn_back(7, 0, 0)
+        turn_back(7, 0, 1)
+        turn_back(6, 1, 0)
+        turn_back(6, 1, 1)
+        turn_back(7, 1, 0)
+        turn_back(7, 1, 1)

@@ -28,8 +28,10 @@ WORDS = PASS // 2
 HALF = 512
 BLOCKS = HALF // P
 SCALE_ROWS = 4
-GAIN_COLUMNS = CHANNELS // P
-GAIN_ROWS = GAIN_COLUMNS + COPIES * (COLUMNS // P)
+GAIN_ROWS = WORD + COPIES * (COLUMNS // P)
+SPREAD = COPIES * COLUMNS // P
+ROW_BUFS, E_BUFS = 12, 6
+SUM_BANKS, TURN_BANKS, DIRECT_BANKS = 4, 2, 2
 
 
 def tile_mora_repeated_update_s12_kernel(
@@ -42,39 +44,44 @@ def tile_mora_repeated_update_s12_kernel(
         psum = ctx.enter_context(tc.psum_pool(name="psum", bufs=2))
         ctx.enter_context(tc.manual_schedule())
 
-        a_codes_raw = resident.tile([P, CHANNEL_PASSES, 2 * CHANNELS], U8, name="a_codes_raw", align_bytes=64)
-        a_codes = resident.tile([P, CHANNEL_PASSES, 2 * CHANNELS], U8, name="a_codes", align_bytes=64)
-        d_codes = resident.tile([P, CHANNEL_PASSES, 2 * COLUMNS], U8, name="d_codes", align_bytes=64)
+        halves = range(2)
+        a_codes_raw = [
+            resident.tile([P, CHANNEL_PASSES, 2 * PASS], U8, name="a_codes_raw%d" % h, align_bytes=64) for h in halves
+        ]
+        a_codes = [resident.tile([P, CHANNEL_PASSES, 2 * PASS], U8, name="a_codes%d" % h, align_bytes=64) for h in halves]
+        d_codes = [resident.tile([P, CHANNEL_PASSES, 2 * HALF], U8, name="d_codes%d" % j, align_bytes=64) for j in halves]
         a_scales_raw = resident.tile([P, CHANNEL_PASSES, CHANNELS], U8, name="a_scales_raw", align_bytes=64)
-        a_scales_sb = resident.tile([P, CHANNEL_PASSES, CHANNELS], U8, name="a_scales_sb", align_bytes=64)
+        a_scales_sb = [resident.tile([P, CHANNEL_PASSES, PASS], U8, name="a_scales_sb%d" % h, align_bytes=64) for h in halves]
         d_scales_sb = resident.tile([P, CHANNEL_PASSES, COLUMNS], U8, name="d_scales_sb", align_bytes=64)
         comp_codes = resident.tile([P, FEATURE_PASSES, CHANNELS], U32, name="comp_codes", align_bytes=64)
         comp_scales = resident.tile([P, FEATURE_PASSES, CHANNELS], U8, name="comp_scales", align_bytes=64)
         e_codes = resident.tile([P, CHANNEL_PASSES, COLUMNS], U32, name="e_codes", align_bytes=64)
         e_scales = resident.tile([P, CHANNEL_PASSES, COLUMNS], U8, name="e_scales", align_bytes=64)
-        copy_gain_sb = resident.tile([P, COPIES, COLUMNS], BF16, name="copy_gain_sb", align_bytes=64)
+        copy_gain_sb = resident.tile([P, COPIES, COLUMNS], F32, name="copy_gain_sb", align_bytes=64)
+        copy_gain_runs = resident.tile([P, SPREAD], BF16, name="copy_gain_runs", align_bytes=64)
+        copy_gain_wide = resident.tile([P, SPREAD], F32, name="copy_gain_wide", align_bytes=64)
         identity = resident.tile([P, P], F32, name="identity", align_bytes=64)
-        gain_rows = resident.tile([GAIN_ROWS, P], BF16, name="gain_rows", align_bytes=64)
-        gain_square = resident.tile([P, P], F32, name="gain_square", align_bytes=64)
-        gain_columns = resident.tile([P, GAIN_ROWS], F32, name="gain_columns", align_bytes=64)
+        gain_rows = resident.tile([P, CHANNEL_PASSES, P], BF16, name="gain_rows", align_bytes=64)
+        gain_square = resident.tile([P, CHANNEL_PASSES, P], F32, name="gain_square", align_bytes=64)
+        gain_columns = resident.tile([P, CHANNEL_PASSES, GAIN_ROWS], F32, name="gain_columns", align_bytes=64)
         dummy = resident.tile([P, 1], F32, name="dummy", align_bytes=64)
 
         nc.vector.memset(a_scales_raw[:].rearrange("p g n -> p (g n)").bitcast(I32), 0)
         nc.vector.memset(d_scales_sb[:].rearrange("p g n -> p (g n)").bitcast(I32), 0)
         nc.vector.memset(dummy[:], 0.0)
-        nc.vector.memset(gain_square[:], 0.0)
+        nc.vector.memset(gain_rows[:], 0.0)
         make_identity(nc, identity[:])
         nc.scalar.activation(out=dummy[:], in_=dummy[:], func=COPY)
 
         x_rows, comp_rows, base_rows = {}, {}, {}
 
         def load_x(i):
-            x_rows[i] = rotating.tile([P, FEATURES], BF16, name="x_rows", tag="token_rows", bufs=9, align_bytes=64)
+            x_rows[i] = rotating.tile([P, FEATURES], BF16, name="x_rows", tag="token_rows", bufs=ROW_BUFS, align_bytes=64)
             nc.sync.dma_start(out=x_rows[i][:], in_=x[P * i : P * (i + 1), :])
 
         def load_base(i):
             base_rows[i] = rotating.tile(
-                [P, COPIES, COLUMNS], BF16, name="base_rows", tag="token_rows", bufs=9, align_bytes=64
+                [P, COPIES, COLUMNS], BF16, name="base_rows", tag="token_rows", bufs=ROW_BUFS, align_bytes=64
             )
             nc.sync.dma_start(out=base_rows[i][:].rearrange("p c n -> p (c n)"), in_=base[P * i : P * (i + 1), :])
 
@@ -86,8 +93,9 @@ def tile_mora_repeated_update_s12_kernel(
             block = comp[PASS * g : PASS * (g + 1), PASS * h : PASS * (h + 1)]
             nc.sync.dma_start(out=comp_rows[piece][:], in_=block.rearrange("(p v) r -> p v r", v=WORD))
 
-        def load_codes(tile, words):
-            nc.sync.dma_start(out=tile[:].bitcast(I32), in_=words.rearrange("g p n -> p g n").bitcast(I32))
+        def load_codes(tiles, words, half):
+            columns = words[:, :, 2 * HALF * half : 2 * HALF * (half + 1)]
+            nc.sync.dma_start(out=tiles[half][:].bitcast(I32), in_=columns.rearrange("g p n -> p g n").bitcast(I32))
 
         def load_scales(tile, scales):
             for quadrant in range(4):
@@ -98,27 +106,26 @@ def tile_mora_repeated_update_s12_kernel(
                 )
 
         def load_gains():
-            for h in range(CHANNEL_PASSES):
-                nc.sync.dma_start(
-                    out=gain_rows[WORD * h : WORD * (h + 1), :].rearrange("t (q e) -> t q e", e=RUN),
-                    in_=gain[PASS * h : PASS * (h + 1)].rearrange("(q t e) -> t q e", t=WORD, e=RUN),
-                )
-            for c in range(COPIES):
-                first = GAIN_COLUMNS + c * (COLUMNS // P)
-                nc.sync.dma_start(
-                    out=gain_rows[first : first + COLUMNS // P, :],
-                    in_=copy_gain[c, :].rearrange("(b p) -> b p", p=P),
-                )
+            nc.sync.dma_start(
+                out=gain_rows[0:WORD, :, :].rearrange("t h (q e) -> t (h q) e", e=RUN),
+                in_=gain.rearrange("(hq t e) -> t hq e", t=WORD, e=RUN),
+            )
+            nc.sync.dma_start(
+                out=gain_rows[WORD:GAIN_ROWS, 0, :], in_=copy_gain.rearrange("c (b p) -> (c b) p", p=P)
+            )
+
+        def load_copy_gain():
+            nc.sync.dma_start(out=copy_gain_runs[:], in_=copy_gain.rearrange("c (p m) -> (c p) m", m=SPREAD))
 
         x_grouped, x_mx = {}, {}
 
         def x_transpose(i):
             s, place = divmod(i, 2)
             if place == 0:
-                x_grouped[s] = rotating.tile([P, FEATURE_PASSES, PAIR, 2], F32, name="x_grouped", align_bytes=64)
+                x_grouped[s] = rotating.tile([P, FEATURE_PASSES, PAIR, 2], F32, name="x_grouped", tag="eight_kib", bufs=3, align_bytes=64)
             words = x_rows[i][:].bitcast(F32)
             for g0 in range(0, FEATURE_PASSES, 2):
-                bank = psum.tile([P, 4, P], F32, name="turned_ps", bufs=2)
+                bank = psum.tile([P, 4, P], F32, name="turned_ps", bufs=TURN_BANKS)
                 for g in (g0, g0 + 1):
                     for u in range(2):
                         first = WORDS * g + u
@@ -140,11 +147,11 @@ def tile_mora_repeated_update_s12_kernel(
 
         comp_grouped = {}
 
-        def comp_group(piece):
+        def comp_group(piece, copy):
             comp_grouped[piece] = rotating.tile(
                 [P, WORD, P // RUN, RUN, WORD], BF16, name="comp_grouped", bufs=3, align_bytes=64
             )
-            nc.vector.tensor_copy(
+            copy(
                 out=comp_grouped[piece][:],
                 in_=comp_rows[piece][:].rearrange("p v (q t e) -> p t q e v", t=WORD, e=RUN),
             )
@@ -158,48 +165,58 @@ def tile_mora_repeated_update_s12_kernel(
                 in_=comp_grouped[piece][:].rearrange("p t q e v -> p (t q e v)"),
             )
 
+        def spread_copy_gain():
+            nc.vector.tensor_copy(out=copy_gain_wide[:], in_=copy_gain_runs[:])
+            target = copy_gain_sb[:].rearrange("p c (n m) -> p (c n) m", m=SPREAD)
+            for first in range(0, SPREAD, 4):
+                bank = psum.tile([P, 4, P], F32, name="sums_ps", bufs=SUM_BANKS)
+                for m in range(first, first + 4):
+                    column = copy_gain_wide[:, m : m + 1].to_broadcast([P, P])
+                    nc.tensor.transpose(bank[:, m - first, :], column, identity[:])
+                nc.scalar.copy(out=target[:, :, first : first + 4], in_=bank[:].rearrange("p m n -> p n m"))
+
+        def widen_gains():
+            nc.scalar.copy(out=gain_square[:], in_=gain_rows[:])
+
         def turn_gains():
-            nc.vector.tensor_copy(out=gain_square[0:GAIN_ROWS, :], in_=gain_rows[:])
-            bank = psum.tile([P, 4, P], F32, name="direct_ps", bufs=2)
-            nc.tensor.transpose(bank[:, 0, :], gain_square[:], identity[:])
-            nc.vector.tensor_copy(out=gain_columns[:], in_=bank[:, 0, 0:GAIN_ROWS])
+            bank = psum.tile([P, 4, P], F32, name="direct_ps", bufs=DIRECT_BANKS)
+            for h in range(CHANNEL_PASSES):
+                nc.tensor.transpose(bank[:, h, :], gain_square[:, h, :], identity[:])
+            nc.scalar.copy(out=gain_columns[:], in_=bank[:, 0:CHANNEL_PASSES, 0:GAIN_ROWS])
 
         e_grouped = {}
 
-        def permute_a():
-            for g in range(CHANNEL_PASSES):
-                for target, source, ints in ((a_codes, a_codes_raw, 4), (a_scales_sb, a_scales_raw, 2)):
-                    nc.vector.tensor_copy(
-                        out=target[:, g, :].bitcast(I32).rearrange(
-                            "p (h t q i) -> p h t q i", h=CHANNEL_PASSES, t=WORD, i=ints
-                        ),
-                        in_=source[:, g, :].bitcast(I32).rearrange(
-                            "p (h q t i) -> p h t q i", h=CHANNEL_PASSES, t=WORD, i=ints
-                        ),
-                    )
-
-        def e_matmul(part, side):
-            j, h = divmod(part, CHANNEL_PASSES)
-            if side == 0:
-                e_grouped[part] = rotating.tile([P, HALF, WORD], BF16, name="e_grouped", bufs=4, align_bytes=64)
-            for b in (2 * side, 2 * side + 1):
-                n = HALF * j + P * b
-                bank = psum.tile([P, WORD, P], F32, name="sums_ps", bufs=4)
-                for t in range(WORD):
-                    m = PASS * h + P * t
-                    for g in range(CHANNEL_PASSES):
-                        nc.tensor.matmul_mx(
-                            out=bank[:, t, :],
-                            lhsT=a_codes[:, g, 2 * m : 2 * (m + P)].bitcast(MXFP4),
-                            lhsT_scale=a_scales_sb[:, g, m : m + P],
-                            rhs=d_codes[:, g, 2 * n : 2 * (n + P)].bitcast(MXFP4),
-                            rhs_scale=d_scales_sb[:, g, n : n + P],
-                            start=(g == 0),
-                            stop=(g == CHANNEL_PASSES - 1),
-                        )
-                nc.scalar.copy(
-                    out=e_grouped[part][:, P * b : P * (b + 1), :], in_=bank[:].rearrange("p t n -> p n t")
+        def permute_a(h):
+            scale_columns = a_scales_raw[:, :, PASS * h : PASS * (h + 1)]
+            for target, source, ints in ((a_codes[h][:], a_codes_raw[h][:], 4), (a_scales_sb[h][:], scale_columns, 2)):
+                nc.vector.tensor_copy(
+                    out=target.bitcast(I32).rearrange("p g (t q i) -> p g t q i", t=WORD, i=ints),
+                    in_=source.bitcast(I32).rearrange("p g (q t i) -> p g t q i", t=WORD, i=ints),
                 )
+
+        def e_matmul(part, b):
+            j, h = divmod(part, CHANNEL_PASSES)
+            if b == 0:
+                e_grouped[part] = rotating.tile([P, HALF, WORD], BF16, name="e_grouped", tag="e_then_sums", bufs=E_BUFS, align_bytes=64)
+            n = P * b
+            bank = psum.tile([P, WORD, P], F32, name="sums_ps", bufs=SUM_BANKS)
+            for t in range(WORD):
+                m = P * t
+                for g in range(CHANNEL_PASSES):
+                    nc.tensor.matmul_mx(
+                        out=bank[:, t, :],
+                        lhsT=a_codes[h][:, g, 2 * m : 2 * (m + P)].bitcast(MXFP4),
+                        lhsT_scale=a_scales_sb[h][:, g, m : m + P],
+                        rhs=d_codes[j][:, g, 2 * n : 2 * (n + P)].bitcast(MXFP4),
+                        rhs_scale=d_scales_sb[:, g, HALF * j + n : HALF * j + n + P],
+                        start=(g == 0),
+                        stop=(g == CHANNEL_PASSES - 1),
+                    )
+            nc.scalar.copy(out=e_grouped[part][:, n : n + P, :], in_=bank[:].rearrange("p t n -> p n t"))
+
+        def e_part(part):
+            for b in range(BLOCKS):
+                e_matmul(part, b)
 
         def e_quantize(part):
             j, h = divmod(part, CHANNEL_PASSES)
@@ -214,9 +231,9 @@ def tile_mora_repeated_update_s12_kernel(
 
         def z_matmul(s, h):
             codes, scales = x_mx[s]
-            z_rounded[(s, h)] = rotating.tile([P, WORD, PAIR], BF16, name="z_rounded", bufs=3, align_bytes=64)
+            z_rounded[(s, h)] = rotating.tile([P, WORD, PAIR], BF16, name="z_rounded", bufs=2, align_bytes=64)
             for i in range(WORD // 2):
-                bank = psum.tile([P, 2, PAIR], F32, name="sums_ps", bufs=4)
+                bank = psum.tile([P, 2, PAIR], F32, name="sums_ps", bufs=SUM_BANKS)
                 for t in (2 * i, 2 * i + 1):
                     m = PASS * h + P * t
                     for g in range(FEATURE_PASSES):
@@ -230,37 +247,87 @@ def tile_mora_repeated_update_s12_kernel(
                             stop=(g == FEATURE_PASSES - 1),
                         )
                 for t in (2 * i, 2 * i + 1):
-                    column = WORD * h + t
                     nc.scalar.activation(
                         out=z_rounded[(s, h)][:, t, :],
                         in_=bank[:, t - 2 * i, :],
                         func=COPY,
-                        scale=gain_columns[:, column : column + 1],
+                        scale=gain_columns[:, h, t : t + 1],
                     )
 
+        def z_matmul_by_passes(s, h):
+            codes, scales = x_mx[s]
+            z_rounded[(s, h)] = rotating.tile([P, WORD, PAIR], BF16, name="z_rounded", bufs=2, align_bytes=64)
+            banks = [psum.tile([P, 2, PAIR], F32, name="sums_ps", bufs=SUM_BANKS) for i in range(WORD // 2)]
+            for g in range(FEATURE_PASSES):
+                for t in range(WORD):
+                    m = PASS * h + P * t
+                    nc.tensor.matmul_mx(
+                        out=banks[t // 2][:, t % 2, :],
+                        lhsT=comp_codes[:, g, m : m + P].bitcast(MXFP8),
+                        lhsT_scale=comp_scales[:, g, m : m + P],
+                        rhs=codes[:, g, :].bitcast(MXFP8),
+                        rhs_scale=scales[:, g, :],
+                        start=(g == 0 and t % 2 == 0),
+                        stop=(g == FEATURE_PASSES - 1 and t % 2 == 1),
+                    )
+            for t in range(WORD):
+                nc.scalar.activation(
+                    out=z_rounded[(s, h)][:, t, :],
+                    in_=banks[t // 2][:, t % 2, :],
+                    func=COPY,
+                    scale=gain_columns[:, h, t : t + 1],
+                )
+
         def z_group(s, h, copy):
-            z_grouped[(s, h)] = rotating.tile([P, PAIR, WORD], BF16, name="z_grouped", bufs=4, align_bytes=64)
+            z_grouped[(s, h)] = rotating.tile([P, PAIR, WORD], BF16, name="z_grouped", bufs=3, align_bytes=64)
             copy(
                 out=z_grouped[(s, h)][:].rearrange("p (k i) t -> p k t i", i=4),
                 in_=z_rounded[(s, h)][:].rearrange("p t (k i) -> p k t i", i=4),
             )
 
-        def z_quantize(s, h):
-            codes = rotating.tile([P, PAIR], U32, name="z_codes", bufs=8, align_bytes=64)
-            scales = rotating.tile([P, PAIR], U8, name="z_scales", bufs=8, align_bytes=64)
-            nc.vector.quantize_mx(
-                out=codes[:].bitcast(MXFP8),
-                scales=scales[:],
-                in_=z_grouped[(s, h)][:].rearrange("p r t -> p (r t)"),
+        def z_matmul_narrow(s, h, place):
+            codes, scales = x_mx[s]
+            tokens = slice(P * place, P * (place + 1))
+            if place == 0:
+                z_grouped[(s, h)] = rotating.tile([P, PAIR, WORD], BF16, name="z_grouped", bufs=3, align_bytes=64)
+            bank = psum.tile([P, WORD, P], F32, name="sums_ps", bufs=SUM_BANKS)
+            for t in range(WORD):
+                m = PASS * h + P * t
+                for g in range(FEATURE_PASSES):
+                    nc.tensor.matmul_mx(
+                        out=bank[:, t, :],
+                        lhsT=comp_codes[:, g, m : m + P].bitcast(MXFP8),
+                        lhsT_scale=comp_scales[:, g, m : m + P],
+                        rhs=codes[:, g, tokens].bitcast(MXFP8),
+                        rhs_scale=scales[:, g, tokens],
+                        start=(g == 0),
+                        stop=(g == FEATURE_PASSES - 1),
+                    )
+            nc.vector.tensor_tensor(
+                out=z_grouped[(s, h)][:, tokens, :],
+                in0=bank[:].rearrange("p t n -> p n t"),
+                in1=gain_columns[:, h, 0:WORD].unsqueeze(1).to_broadcast([P, P, WORD]),
+                op=MULT,
             )
-            z_mx[(s, h)] = (codes, scales)
 
-        products = {}
+        def z_quantize(s, h, tokens=slice(0, PAIR)):
+            if tokens.start == 0:
+                codes = rotating.tile([P, PAIR], U32, name="z_codes", bufs=8, align_bytes=64)
+                scales = rotating.tile([P, PAIR], U8, name="z_scales", bufs=8, align_bytes=64)
+                z_mx[(s, h)] = (codes, scales)
+            codes, scales = z_mx[(s, h)]
+            nc.vector.quantize_mx(
+                out=codes[:, tokens].bitcast(MXFP8),
+                scales=scales[:, tokens],
+                in_=z_grouped[(s, h)][:, tokens, :].rearrange("p r t -> p (r t)"),
+            )
+
+        y_banks, products = {}, {}
 
         def y_direct(i, j):
             s, place = divmod(i, 2)
             columns = slice(HALF * j, HALF * (j + 1))
-            bank = psum.tile([P, HALF], F32, name="direct_ps", bufs=2)
+            bank = psum.tile([P, HALF], F32, name="direct_ps", bufs=DIRECT_BANKS)
             for h in range(CHANNEL_PASSES):
                 codes, scales = z_mx[(s, h)]
                 nc.tensor.matmul_mx(
@@ -272,6 +339,11 @@ def tile_mora_repeated_update_s12_kernel(
                     start=(h == 0),
                     stop=(h == CHANNEL_PASSES - 1),
                 )
+            y_banks[(i, j)] = bank
+
+        def multiply(i, j):
+            columns = slice(HALF * j, HALF * (j + 1))
+            bank = y_banks[(i, j)]
             products[(i, j)] = rotating.tile(
                 [P, COPIES, HALF], F32, name="product", tag="four_kib", bufs=8, align_bytes=64
             )
@@ -282,10 +354,10 @@ def tile_mora_repeated_update_s12_kernel(
                 op=MULT,
             )
 
-        def add_base(i, j):
+        def add_base(i, j, engine):
             columns = slice(HALF * j, HALF * (j + 1))
             product = products[(i, j)]
-            nc.vector.tensor_tensor(out=product[:], in0=product[:], in1=base_rows[i][:, :, columns], op=ADD)
+            engine.tensor_tensor(out=product[:], in0=product[:], in1=base_rows[i][:, :, columns], op=ADD)
             rows = out[P * i : P * (i + 1), :].rearrange("p (c n) -> p c n", c=COPIES)
             nc.sync.dma_start(out=rows[:, :, columns], in_=product[:])
 
@@ -295,7 +367,7 @@ def tile_mora_repeated_update_s12_kernel(
             banks = []
             for b in range(BLOCKS):
                 if b % 2 == 0:
-                    banks.append(psum.tile([P, 2, PAIR], F32, name="sums_ps", bufs=4))
+                    banks.append(psum.tile([P, 2, PAIR], F32, name="sums_ps", bufs=SUM_BANKS))
                 columns = slice(HALF * j + P * b, HALF * j + P * (b + 1))
                 for h in range(CHANNEL_PASSES):
                     codes, scales = z_mx[(s, h)]
@@ -308,161 +380,187 @@ def tile_mora_repeated_update_s12_kernel(
                         start=(h == 0),
                         stop=(h == CHANNEL_PASSES - 1),
                     )
-            turned = rotating.tile([P, COPIES, BLOCKS, PAIR], F32, name="turned", align_bytes=64)
+            turned = rotating.tile([P, COPIES, BLOCKS, PAIR], F32, name="turned", tag="eight_kib", bufs=3, align_bytes=64)
             for c in range(COPIES):
                 for b in range(BLOCKS):
-                    column = GAIN_COLUMNS + c * (COLUMNS // P) + BLOCKS * j + b
+                    column = WORD + c * (COLUMNS // P) + BLOCKS * j + b
                     nc.scalar.activation(
                         out=turned[:, c, b, :],
                         in_=banks[b // 2][:, b % 2, :],
                         func=COPY,
-                        scale=gain_columns[:, column : column + 1],
+                        scale=gain_columns[:, 0, column : column + 1],
                     )
             turned_products[(s, j)] = turned
 
-        def turn_back(i, j, c):
+        back_banks, totals = {}, {}
+
+        def turn_back(i, j, c, tag="turned_ps", bufs=TURN_BANKS):
             s, place = divmod(i, 2)
-            bank = psum.tile([P, BLOCKS, P], F32, name="turned_ps", bufs=2)
+            bank = psum.tile([P, BLOCKS, P], F32, name=tag, bufs=bufs)
             for b in range(BLOCKS):
                 nc.tensor.transpose(
                     bank[:, b, :], turned_products[(s, j)][:, c, b, P * place : P * (place + 1)], identity[:]
                 )
-            total = rotating.tile([P, HALF], F32, name="total", bufs=8, align_bytes=64)
+            back_banks[(i, j, c)] = bank
+
+        def add_turned(i, j, c):
+            bank = back_banks[(i, j, c)]
+            if c == 0:
+                totals[(i, j)] = rotating.tile(
+                    [P, COPIES, HALF], F32, name="total", tag="e_then_sums", bufs=E_BUFS, align_bytes=64
+                )
+            total = totals[(i, j)][:, c, :]
             nc.vector.tensor_tensor(
-                out=total[:],
+                out=total,
                 in0=bank[:].rearrange("p b n -> p (b n)"),
                 in1=base_rows[i][:, c, HALF * j : HALF * (j + 1)],
                 op=ADD,
             )
             first = COLUMNS * c + HALF * j
-            nc.sync.dma_start(out=out[P * i : P * (i + 1), first : first + HALF], in_=total[:])
+            nc.sync.dma_start(out=out[P * i : P * (i + 1), first : first + HALF], in_=total)
 
+        V, S = nc.vector.tensor_copy, nc.scalar.copy
+        load_copy_gain()
         load_comp(0)
         load_scales(a_scales_raw, a_scales)
-        load_x(0)
-        load_codes(a_codes_raw, a_words)
-        load_codes(d_codes, d_words)
+        load_codes(a_codes_raw, a_words, 0)
+        load_codes(d_codes, d_words, 0)
         load_scales(d_scales_sb, d_scales)
         load_comp(1)
-        load_x(1)
+        load_codes(a_codes_raw, a_words, 1)
         load_comp(2)
-        load_x(2)
         load_gains()
-        load_x(3)
-        for piece in range(3, 7):
-            load_comp(piece)
-        load_x(4)
+        load_comp(3)
+        load_x(0)
+        load_comp(4)
+        load_codes(d_codes, d_words, 1)
+        load_comp(5)
+        load_x(1)
+        load_comp(6)
+        load_x(2)
         load_comp(7)
-        for i in range(5, 8):
-            load_x(i)
-        nc.sync.dma_start(
-            out=copy_gain_sb[:].rearrange("p c n -> p (c n)"),
-            in_=copy_gain.rearrange("c n -> (c n)").partition_broadcast(P),
-        )
-        for i in range(TOKENS // P):
+        load_x(3)
+        load_x(4)
+        load_base(0)
+        load_x(5)
+        load_base(1)
+        load_x(6)
+        load_x(7)
+        for i in range(2, 8):
             load_base(i)
 
-        comp_group(0)
-        permute_a()
-        x_transpose(0)
+        spread_copy_gain()
+        comp_group(0, V)
+        permute_a(0)
         comp_quantize(0)
-        e_matmul(0, 0)
-        e_matmul(0, 1)
-        x_transpose(1)
-        comp_group(1)
+        e_part(0)
+        comp_group(1, V)
+        permute_a(1)
         e_matmul(1, 0)
-        comp_quantize(1)
-        comp_group(2)
-        x_transpose(2)
-        e_quantize(0)
         e_matmul(1, 1)
-        x_transpose(3)
-        e_matmul(2, 0)
-        x_quantize(0)
-        comp_quantize(2)
-        e_matmul(2, 1)
-        e_matmul(3, 0)
-        x_transpose(4)
-        for piece in range(3, 6):
-            comp_group(piece)
-        for piece in range(3, 6):
-            comp_quantize(piece)
-
+        widen_gains()
+        e_matmul(1, 2)
+        e_matmul(1, 3)
+        x_transpose(0)
         turn_gains()
-        comp_group(6)
+        e_part(2)
+        x_transpose(1)
+        for piece in range(2, 7):
+            comp_group(piece, V)
+            comp_quantize(piece - 1)
+        x_quantize(0)
+        e_matmul(3, 0)
+        x_transpose(2)
+        e_matmul(3, 1)
         z_matmul(0, 0)
-        x_transpose(5)
-        comp_group(7)
-        z_group(0, 0, nc.scalar.copy)
+        comp_group(7, V)
         comp_quantize(6)
         comp_quantize(7)
+        z_matmul_by_passes(0, 1)
+        e_quantize(0)
         e_quantize(1)
-        x_quantize(1)
-        e_matmul(3, 1)
-        x_quantize(2)
+        z_group(0, 0, V)
         e_quantize(2)
-        z_matmul(0, 1)
-        x_transpose(6)
-        e_quantize(3)
-        z_group(0, 1, nc.vector.tensor_copy)
-        z_matmul(1, 0)
         z_quantize(0, 0)
+        x_transpose(3)
+        e_matmul(3, 2)
+        e_matmul(3, 3)
+        z_group(0, 1, V)
         z_quantize(0, 1)
-
+        x_quantize(1)
+        x_transpose(4)
         y_direct(0, 0)
-        z_group(1, 0, nc.scalar.copy)
         y_direct(1, 0)
-        x_transpose(7)
-        add_base(0, 0)
-        z_matmul(2, 0)
-        x_quantize(3)
-        z_quantize(1, 0)
-        y_direct(0, 1)
-        z_group(2, 0, nc.scalar.copy)
+        z_matmul(1, 0)
+
+        def finish(s, j, c):
+            turn_back(2 * s, j, c)
+            add_turned(2 * s, j, c)
+            turn_back(2 * s + 1, j, c, "direct_ps", DIRECT_BANKS)
+            add_turned(2 * s + 1, j, c)
+        def mul2(s, j):
+            multiply(2 * s, j)
+            multiply(2 * s + 1, j)
+        def add2(s, j):
+            add_base(2 * s, j, nc.vector)
+            add_base(2 * s + 1, j, nc.vector)
+        def y2(s, j):
+            y_direct(2 * s, j)
+            y_direct(2 * s + 1, j)
+        e_quantize(3)
+        mul2(0, 0)
+        y2(0, 1)
+        z_group(1, 0, S)
+        x_transpose(5)
+        add2(0, 0)
+        mul2(0, 1)
         z_matmul(1, 1)
-        z_group(1, 1, nc.scalar.copy)
-        add_base(1, 0)
-        z_quantize(2, 0)
-        add_base(0, 1)
-        z_matmul(2, 1)
+        x_quantize(2)
+        z_quantize(1, 0)
+        z_group(1, 1, S)
+        x_transpose(6)
+        add_base(0, 1, nc.vector)
         z_quantize(1, 1)
-        z_group(2, 1, nc.scalar.copy)
-        y_direct(1, 1)
-        z_matmul(3, 1)
-        add_base(1, 1)
-        z_group(3, 1, nc.scalar.copy)
-        z_quantize(2, 1)
-        y_direct(2, 0)
-        y_direct(3, 0)
-
-        y_transposed(2, 0)
-        add_base(2, 0)
-        y_direct(2, 1)
-        y_transposed(2, 1)
-        y_direct(3, 1)
-        turn_back(4, 0, 0)
+        add_base(1, 1, nc.vector)
+        z_matmul(2, 0)
+        y2(1, 0)
+        z_group(2, 0, S)
+        x_transpose(7)
+        mul2(1, 0)
+        y2(1, 1)
+        z_matmul(2, 1)
+        add_base(2, 0, nc.vector)
+        x_quantize(3)
+        z_quantize(2, 0)
+        add_base(3, 0, nc.vector)
+        multiply(2, 1)
+        z_group(2, 1, S)
         z_matmul(3, 0)
-        add_base(3, 0)
-        turn_back(4, 0, 1)
-        turn_back(5, 0, 0)
-        z_group(3, 0, nc.scalar.copy)
-        z_quantize(3, 1)
-        turn_back(5, 0, 1)
-        turn_back(4, 1, 0)
+        multiply(3, 1)
+        z_quantize(2, 1)
+        y2(2, 0)
+        add_base(2, 1, nc.vector)
+        z_group(3, 0, S)
+        z_matmul(3, 1)
+        y_transposed(2, 1)
+        add_base(3, 1, nc.vector)
+        multiply(4, 0)
         z_quantize(3, 0)
-        turn_back(4, 1, 1)
+        multiply(5, 0)
+        z_group(3, 1, V)
+        add_base(4, 0, nc.vector)
+        z_quantize(3, 1)
+        turn_back(4, 1, 0)
         turn_back(5, 1, 0)
-        add_base(2, 1)
         y_transposed(3, 0)
-        turn_back(5, 1, 1)
-        add_base(3, 1)
-
-        turn_back(6, 0, 0)
+        add_base(5, 0, nc.vector)
+        add_turned(4, 1, 0)
+        add_turned(5, 1, 0)
+        turn_back(4, 1, 1, "direct_ps", DIRECT_BANKS)
+        turn_back(5, 1, 1, "direct_ps", DIRECT_BANKS)
         y_transposed(3, 1)
-        turn_back(6, 0, 1)
-        turn_back(7, 0, 0)
-        turn_back(7, 0, 1)
-        turn_back(6, 1, 0)
-        turn_back(6, 1, 1)
-        turn_back(7, 1, 0)
-        turn_back(7, 1, 1)
+        add_turned(4, 1, 1)
+        add_turned(5, 1, 1)
+        for j in range(2):
+            for c in range(2):
+                finish(3, j, c)

@@ -30,8 +30,9 @@ BLOCKS = HALF // P
 SCALE_ROWS = 4
 GAIN_ROWS = WORD + COPIES * (COLUMNS // P)
 SPREAD = COPIES * COLUMNS // P
-ROW_BUFS, E_BUFS = 12, 6
+ROW_BUFS, E_BUFS = 12, 3
 SUM_BANKS, TURN_BANKS, DIRECT_BANKS = 4, 2, 2
+POOL_WIDTH = 512
 
 
 def tile_mora_repeated_update_s12_kernel(
@@ -55,11 +56,10 @@ def tile_mora_repeated_update_s12_kernel(
         d_scales_sb = resident.tile([P, CHANNEL_PASSES, COLUMNS], U8, name="d_scales_sb", align_bytes=64)
         comp_codes = resident.tile([P, FEATURE_PASSES, CHANNELS], U32, name="comp_codes", align_bytes=64)
         comp_scales = resident.tile([P, FEATURE_PASSES, CHANNELS], U8, name="comp_scales", align_bytes=64)
-        e_codes = resident.tile([P, CHANNEL_PASSES, COLUMNS], U32, name="e_codes", align_bytes=64)
-        e_scales = resident.tile([P, CHANNEL_PASSES, COLUMNS], U8, name="e_scales", align_bytes=64)
-        copy_gain_sb = resident.tile([P, COPIES, COLUMNS], F32, name="copy_gain_sb", align_bytes=64)
+        e_codes = resident.tile([P, 2, CHANNEL_PASSES, HALF], U32, name="e_codes", align_bytes=64)
+        e_scales = resident.tile([P, 2, CHANNEL_PASSES, HALF], U8, name="e_scales", align_bytes=64)
+        copy_gain_sb = resident.tile([P, COPIES, COLUMNS], BF16, name="copy_gain_sb", align_bytes=64)
         copy_gain_runs = resident.tile([P, SPREAD], BF16, name="copy_gain_runs", align_bytes=64)
-        copy_gain_wide = resident.tile([P, SPREAD], F32, name="copy_gain_wide", align_bytes=64)
         identity = resident.tile([P, P], F32, name="identity", align_bytes=64)
         gain_rows = resident.tile([P, CHANNEL_PASSES, P], BF16, name="gain_rows", align_bytes=64)
         gain_square = resident.tile([P, CHANNEL_PASSES, P], F32, name="gain_square", align_bytes=64)
@@ -85,13 +85,12 @@ def tile_mora_repeated_update_s12_kernel(
             )
             nc.sync.dma_start(out=base_rows[i][:].rearrange("p c n -> p (c n)"), in_=base[P * i : P * (i + 1), :])
 
-        def load_comp(piece):
-            h, g = divmod(piece, FEATURE_PASSES)
-            comp_rows[piece] = rotating.tile(
-                [P, WORD, PASS], BF16, name="comp_rows", tag="four_kib", bufs=8, align_bytes=64
+        def load_comp(g):
+            comp_rows[g] = rotating.tile(
+                [P, WORD, CHANNELS], BF16, name="comp_rows", tag="comp_then_products", bufs=4, align_bytes=64
             )
-            block = comp[PASS * g : PASS * (g + 1), PASS * h : PASS * (h + 1)]
-            nc.sync.dma_start(out=comp_rows[piece][:], in_=block.rearrange("(p v) r -> p v r", v=WORD))
+            rows = comp[PASS * g : PASS * (g + 1), :]
+            nc.sync.dma_start(out=comp_rows[g][:], in_=rows.rearrange("(p v) r -> p v r", v=WORD))
 
         def load_codes(tiles, words, half):
             columns = words[:, :, 2 * HALF * half : 2 * HALF * (half + 1)]
@@ -147,32 +146,31 @@ def tile_mora_repeated_update_s12_kernel(
 
         comp_grouped = {}
 
-        def comp_group(piece, copy):
-            comp_grouped[piece] = rotating.tile(
-                [P, WORD, P // RUN, RUN, WORD], BF16, name="comp_grouped", bufs=3, align_bytes=64
-            )
-            copy(
-                out=comp_grouped[piece][:],
-                in_=comp_rows[piece][:].rearrange("p v (q t e) -> p t q e v", t=WORD, e=RUN),
+        def comp_group(g, first, count):
+            if first == 0:
+                comp_grouped[g] = rotating.tile(
+                    [P, WORD, CHANNELS // (WORD * RUN), RUN, WORD], BF16, name="comp_grouped", align_bytes=64
+                )
+            source = comp_rows[g][:].rearrange("p v (hq t e) -> p t hq e v", t=WORD, e=RUN)
+            nc.vector.tensor_copy(
+                out=comp_grouped[g][:, first : first + count], in_=source[:, first : first + count]
             )
 
-        def comp_quantize(piece):
-            h, g = divmod(piece, FEATURE_PASSES)
-            columns = slice(PASS * h, PASS * (h + 1))
+        def comp_quantize(g, first, count):
+            columns = slice(2 * P * first, 2 * P * (first + count))
             nc.vector.quantize_mx(
                 out=comp_codes[:, g, columns].bitcast(MXFP8),
                 scales=comp_scales[:, g, columns],
-                in_=comp_grouped[piece][:].rearrange("p t q e v -> p (t q e v)"),
+                in_=comp_grouped[g][:, first : first + count].rearrange("p t hq e v -> p (t hq e v)"),
             )
 
         def spread_copy_gain():
-            nc.vector.tensor_copy(out=copy_gain_wide[:], in_=copy_gain_runs[:])
-            target = copy_gain_sb[:].rearrange("p c (n m) -> p (c n) m", m=SPREAD)
-            for first in range(0, SPREAD, 4):
+            words = copy_gain_runs[:].bitcast(F32)
+            target = copy_gain_sb[:].rearrange("p c n -> p (c n)").bitcast(F32).rearrange("p (n m) -> p n m", n=P)
+            for first in range(0, SPREAD // 2, 4):
                 bank = psum.tile([P, 4, P], F32, name="sums_ps", bufs=SUM_BANKS)
                 for m in range(first, first + 4):
-                    column = copy_gain_wide[:, m : m + 1].to_broadcast([P, P])
-                    nc.tensor.transpose(bank[:, m - first, :], column, identity[:])
+                    nc.tensor.transpose(bank[:, m - first, :], words[:, m : m + 1].to_broadcast([P, P]), identity[:])
                 nc.scalar.copy(out=target[:, :, first : first + 4], in_=bank[:].rearrange("p m n -> p n m"))
 
         def widen_gains():
@@ -194,12 +192,14 @@ def tile_mora_repeated_update_s12_kernel(
                     in_=source.bitcast(I32).rearrange("p g (q t i) -> p g t q i", t=WORD, i=ints),
                 )
 
-        def e_matmul(part, b):
+        def e_matmul(part, b, tag="sums_ps", bufs=SUM_BANKS):
             j, h = divmod(part, CHANNEL_PASSES)
-            if b == 0:
-                e_grouped[part] = rotating.tile([P, HALF, WORD], BF16, name="e_grouped", tag="e_then_sums", bufs=E_BUFS, align_bytes=64)
+            if b == 0 and h == 0:
+                e_grouped[j] = rotating.tile(
+                    [P, CHANNEL_PASSES, HALF, WORD], BF16, name="e_grouped", tag="e_then_sums", bufs=E_BUFS, align_bytes=64
+                )
             n = P * b
-            bank = psum.tile([P, WORD, P], F32, name="sums_ps", bufs=SUM_BANKS)
+            bank = psum.tile([P, WORD, P], F32, name=tag, bufs=bufs)
             for t in range(WORD):
                 m = P * t
                 for g in range(CHANNEL_PASSES):
@@ -212,22 +212,20 @@ def tile_mora_repeated_update_s12_kernel(
                         start=(g == 0),
                         stop=(g == CHANNEL_PASSES - 1),
                     )
-            nc.scalar.copy(out=e_grouped[part][:, n : n + P, :], in_=bank[:].rearrange("p t n -> p n t"))
+            nc.scalar.copy(out=e_grouped[j][:, h, n : n + P, :], in_=bank[:].rearrange("p t n -> p n t"))
 
         def e_part(part):
             for b in range(BLOCKS):
                 e_matmul(part, b)
 
-        def e_quantize(part):
-            j, h = divmod(part, CHANNEL_PASSES)
-            columns = slice(HALF * j, HALF * (j + 1))
+        def e_quantize(j):
             nc.vector.quantize_mx(
-                out=e_codes[:, h, columns].bitcast(MXFP8),
-                scales=e_scales[:, h, columns],
-                in_=e_grouped[part][:].rearrange("p n t -> p (n t)"),
+                out=e_codes[:, j].rearrange("p h n -> p (h n)").bitcast(MXFP8),
+                scales=e_scales[:, j].rearrange("p h n -> p (h n)"),
+                in_=e_grouped[j][:].rearrange("p h n t -> p (h n t)"),
             )
 
-        z_rounded, z_grouped, z_mx = {}, {}, {}
+        z_rounded, z_grouped, z_mx, z_tile = {}, {}, {}, {}
 
         def z_matmul(s, h):
             codes, scales = x_mx[s]
@@ -235,7 +233,7 @@ def tile_mora_repeated_update_s12_kernel(
             for i in range(WORD // 2):
                 bank = psum.tile([P, 2, PAIR], F32, name="sums_ps", bufs=SUM_BANKS)
                 for t in (2 * i, 2 * i + 1):
-                    m = PASS * h + P * t
+                    m = 2 * P * t + P * h
                     for g in range(FEATURE_PASSES):
                         nc.tensor.matmul_mx(
                             out=bank[:, t - 2 * i, :],
@@ -254,88 +252,88 @@ def tile_mora_repeated_update_s12_kernel(
                         scale=gain_columns[:, h, t : t + 1],
                     )
 
-        def z_matmul_by_passes(s, h):
-            codes, scales = x_mx[s]
-            z_rounded[(s, h)] = rotating.tile([P, WORD, PAIR], BF16, name="z_rounded", bufs=2, align_bytes=64)
-            banks = [psum.tile([P, 2, PAIR], F32, name="sums_ps", bufs=SUM_BANKS) for i in range(WORD // 2)]
-            for g in range(FEATURE_PASSES):
-                for t in range(WORD):
-                    m = PASS * h + P * t
-                    nc.tensor.matmul_mx(
-                        out=banks[t // 2][:, t % 2, :],
-                        lhsT=comp_codes[:, g, m : m + P].bitcast(MXFP8),
-                        lhsT_scale=comp_scales[:, g, m : m + P],
-                        rhs=codes[:, g, :].bitcast(MXFP8),
-                        rhs_scale=scales[:, g, :],
-                        start=(g == 0 and t % 2 == 0),
-                        stop=(g == FEATURE_PASSES - 1 and t % 2 == 1),
-                    )
-            for t in range(WORD):
-                nc.scalar.activation(
-                    out=z_rounded[(s, h)][:, t, :],
-                    in_=banks[t // 2][:, t % 2, :],
-                    func=COPY,
-                    scale=gain_columns[:, h, t : t + 1],
-                )
+        open_banks = {}
 
-        def z_group(s, h, copy):
-            z_grouped[(s, h)] = rotating.tile([P, PAIR, WORD], BF16, name="z_grouped", bufs=3, align_bytes=64)
-            copy(
-                out=z_grouped[(s, h)][:].rearrange("p (k i) t -> p k t i", i=4),
-                in_=z_rounded[(s, h)][:].rearrange("p t (k i) -> p k t i", i=4),
-            )
-
-        def z_matmul_narrow(s, h, place):
+        def z_pass(s, g):
             codes, scales = x_mx[s]
-            tokens = slice(P * place, P * (place + 1))
-            if place == 0:
-                z_grouped[(s, h)] = rotating.tile([P, PAIR, WORD], BF16, name="z_grouped", bufs=3, align_bytes=64)
-            bank = psum.tile([P, WORD, P], F32, name="sums_ps", bufs=SUM_BANKS)
-            for t in range(WORD):
-                m = PASS * h + P * t
-                for g in range(FEATURE_PASSES):
-                    nc.tensor.matmul_mx(
-                        out=bank[:, t, :],
-                        lhsT=comp_codes[:, g, m : m + P].bitcast(MXFP8),
-                        lhsT_scale=comp_scales[:, g, m : m + P],
-                        rhs=codes[:, g, tokens].bitcast(MXFP8),
-                        rhs_scale=scales[:, g, tokens],
-                        start=(g == 0),
-                        stop=(g == FEATURE_PASSES - 1),
-                    )
+            for place in range(2):
+                tokens = slice(P * place, P * (place + 1))
+                for h in range(CHANNEL_PASSES):
+                    if g == 0:
+                        open_banks[(place, h)] = psum.tile([P, WORD, P], F32, name="sums_ps", bufs=SUM_BANKS)
+                    for t in range(WORD):
+                        m = 2 * P * t + P * h
+                        nc.tensor.matmul_mx(
+                            out=open_banks[(place, h)][:, t, :],
+                            lhsT=comp_codes[:, g, m : m + P].bitcast(MXFP8),
+                            lhsT_scale=comp_scales[:, g, m : m + P],
+                            rhs=codes[:, g, tokens].bitcast(MXFP8),
+                            rhs_scale=scales[:, g, tokens],
+                            start=(g == 0 and t == 0),
+                            stop=(g == FEATURE_PASSES - 1 and t == WORD - 1),
+                        )
+
+        tile_grouped = {}
+
+        def z_leave_bank(i, h):
+            if h == 0:
+                tile_grouped[i] = rotating.tile([P, CHANNEL_PASSES, P, WORD], BF16, name="z_rounded", bufs=2, align_bytes=64)
             nc.vector.tensor_tensor(
-                out=z_grouped[(s, h)][:, tokens, :],
-                in0=bank[:].rearrange("p t n -> p n t"),
+                out=tile_grouped[i][:, h],
+                in0=open_banks[(i % 2, h)][:].rearrange("p t n -> p n t"),
                 in1=gain_columns[:, h, 0:WORD].unsqueeze(1).to_broadcast([P, P, WORD]),
                 op=MULT,
             )
 
-        def z_quantize(s, h, tokens=slice(0, PAIR)):
-            if tokens.start == 0:
-                codes = rotating.tile([P, PAIR], U32, name="z_codes", bufs=8, align_bytes=64)
-                scales = rotating.tile([P, PAIR], U8, name="z_scales", bufs=8, align_bytes=64)
-                z_mx[(s, h)] = (codes, scales)
-            codes, scales = z_mx[(s, h)]
+        def z_quantize_tile(i):
+            codes = rotating.tile([P, CHANNEL_PASSES, P], U32, name="z_codes", bufs=5, align_bytes=64)
+            scales = rotating.tile([P, CHANNEL_PASSES, P], U8, name="z_scales", bufs=5, align_bytes=64)
             nc.vector.quantize_mx(
-                out=codes[:, tokens].bitcast(MXFP8),
-                scales=scales[:, tokens],
-                in_=z_grouped[(s, h)][:, tokens, :].rearrange("p r t -> p (r t)"),
+                out=codes[:].rearrange("p h r -> p (h r)").bitcast(MXFP8),
+                scales=scales[:].rearrange("p h r -> p (h r)"),
+                in_=tile_grouped[i][:].rearrange("p h r t -> p (h r t)"),
             )
+            for h in range(CHANNEL_PASSES):
+                z_tile[(i, h)] = (codes[:, h], scales[:, h])
+
+        def z_group(s, h, copy):
+            if h == 0:
+                z_grouped[s] = rotating.tile([P, CHANNEL_PASSES, PAIR, WORD], BF16, name="z_grouped", align_bytes=64)
+            copy(
+                out=z_grouped[s][:, h].rearrange("p (k i) t -> p k t i", i=4),
+                in_=z_rounded[(s, h)][:].rearrange("p t (k i) -> p k t i", i=4),
+            )
+
+        z_codes, z_scales = {}, {}
+
+        def z_quantize(s, first, count):
+            if first == 0:
+                z_codes[s] = rotating.tile([P, CHANNEL_PASSES, PAIR], U32, name="z_codes", bufs=5, align_bytes=64)
+                z_scales[s] = rotating.tile([P, CHANNEL_PASSES, PAIR], U8, name="z_scales", bufs=5, align_bytes=64)
+            passes = slice(first, first + count)
+            nc.vector.quantize_mx(
+                out=z_codes[s][:, passes].rearrange("p h r -> p (h r)").bitcast(MXFP8),
+                scales=z_scales[s][:, passes].rearrange("p h r -> p (h r)"),
+                in_=z_grouped[s][:, passes].rearrange("p h r t -> p (h r t)"),
+            )
+            for h in range(first, first + count):
+                z_mx[(s, h)] = (z_codes[s][:, h], z_scales[s][:, h])
+                for place in range(2):
+                    tokens = slice(P * place, P * (place + 1))
+                    z_tile[(2 * s + place, h)] = (z_codes[s][:, h, tokens], z_scales[s][:, h, tokens])
 
         y_banks, products = {}, {}
 
         def y_direct(i, j):
-            s, place = divmod(i, 2)
-            columns = slice(HALF * j, HALF * (j + 1))
             bank = psum.tile([P, HALF], F32, name="direct_ps", bufs=DIRECT_BANKS)
             for h in range(CHANNEL_PASSES):
-                codes, scales = z_mx[(s, h)]
+                codes, scales = z_tile[(i, h)]
                 nc.tensor.matmul_mx(
                     out=bank[:],
-                    lhsT=codes[:, P * place : P * (place + 1)].bitcast(MXFP8),
-                    lhsT_scale=scales[:, P * place : P * (place + 1)],
-                    rhs=e_codes[:, h, columns].bitcast(MXFP8),
-                    rhs_scale=e_scales[:, h, columns],
+                    lhsT=codes.bitcast(MXFP8),
+                    lhsT_scale=scales,
+                    rhs=e_codes[:, j, h, :].bitcast(MXFP8),
+                    rhs_scale=e_scales[:, j, h, :],
                     start=(h == 0),
                     stop=(h == CHANNEL_PASSES - 1),
                 )
@@ -344,22 +342,35 @@ def tile_mora_repeated_update_s12_kernel(
         def multiply(i, j):
             columns = slice(HALF * j, HALF * (j + 1))
             bank = y_banks[(i, j)]
-            products[(i, j)] = rotating.tile(
-                [P, COPIES, HALF], F32, name="product", tag="four_kib", bufs=8, align_bytes=64
-            )
+            s, place = divmod(i, 2)
+            if place == 0:
+                products[(s, j)] = rotating.tile(
+                    [P, 2, COPIES, HALF], F32, name="product", tag="comp_then_products", bufs=4, align_bytes=64
+                )
             nc.vector.tensor_tensor(
-                out=products[(i, j)][:],
+                out=products[(s, j)][:, place],
                 in0=bank[:].unsqueeze(1).to_broadcast([P, COPIES, HALF]),
                 in1=copy_gain_sb[:, :, columns],
                 op=MULT,
             )
 
         def add_base(i, j, engine):
+            s, place = divmod(i, 2)
             columns = slice(HALF * j, HALF * (j + 1))
-            product = products[(i, j)]
-            engine.tensor_tensor(out=product[:], in0=product[:], in1=base_rows[i][:, :, columns], op=ADD)
+            product = products[(s, j)][:, place]
+            if engine is nc.vector:
+                engine.tensor_tensor(out=product, in0=product, in1=base_rows[i][:, :, columns], op=ADD)
+            else:
+                for c in range(COPIES):
+                    for first in range(0, HALF, POOL_WIDTH):
+                        part = product[:, c, first : first + POOL_WIDTH]
+                        start = HALF * j + first
+                        engine.tensor_tensor(out=part, in0=part, in1=base_rows[i][:, c, start : start + POOL_WIDTH], op=ADD)
+
+        def store(i, j):
+            s, place = divmod(i, 2)
             rows = out[P * i : P * (i + 1), :].rearrange("p (c n) -> p c n", c=COPIES)
-            nc.sync.dma_start(out=rows[:, :, columns], in_=product[:])
+            nc.sync.dma_start(out=rows[:, :, HALF * j : HALF * (j + 1)], in_=products[(s, j)][:, place])
 
         turned_products = {}
 
@@ -368,15 +379,15 @@ def tile_mora_repeated_update_s12_kernel(
             for b in range(BLOCKS):
                 if b % 2 == 0:
                     banks.append(psum.tile([P, 2, PAIR], F32, name="sums_ps", bufs=SUM_BANKS))
-                columns = slice(HALF * j + P * b, HALF * j + P * (b + 1))
+                columns = slice(P * b, P * (b + 1))
                 for h in range(CHANNEL_PASSES):
                     codes, scales = z_mx[(s, h)]
                     nc.tensor.matmul_mx(
                         out=banks[b // 2][:, b % 2, :],
-                        lhsT=e_codes[:, h, columns].bitcast(MXFP8),
-                        lhsT_scale=e_scales[:, h, columns],
-                        rhs=codes[:].bitcast(MXFP8),
-                        rhs_scale=scales[:],
+                        lhsT=e_codes[:, j, h, columns].bitcast(MXFP8),
+                        lhsT_scale=e_scales[:, j, h, columns],
+                        rhs=codes.bitcast(MXFP8),
+                        rhs_scale=scales,
                         start=(h == 0),
                         stop=(h == CHANNEL_PASSES - 1),
                     )
@@ -405,11 +416,12 @@ def tile_mora_repeated_update_s12_kernel(
 
         def add_turned(i, j, c):
             bank = back_banks[(i, j, c)]
-            if c == 0:
-                totals[(i, j)] = rotating.tile(
-                    [P, COPIES, HALF], F32, name="total", tag="e_then_sums", bufs=E_BUFS, align_bytes=64
+            s, place = divmod(i, 2)
+            if (s, j) not in totals:
+                totals[(s, j)] = rotating.tile(
+                    [P, 2, COPIES, HALF], F32, name="total", tag="e_then_sums", bufs=E_BUFS, align_bytes=64
                 )
-            total = totals[(i, j)][:, c, :]
+            total = totals[(s, j)][:, place, c, :]
             nc.vector.tensor_tensor(
                 out=total,
                 in0=bank[:].rearrange("p b n -> p (b n)"),
@@ -420,6 +432,8 @@ def tile_mora_repeated_update_s12_kernel(
             nc.sync.dma_start(out=out[P * i : P * (i + 1), first : first + HALF], in_=total)
 
         V, S = nc.vector.tensor_copy, nc.scalar.copy
+        VE = nc.vector
+        G = nc.gpsimd
         load_copy_gain()
         load_comp(0)
         load_scales(a_scales_raw, a_scales)
@@ -428,17 +442,13 @@ def tile_mora_repeated_update_s12_kernel(
         load_scales(d_scales_sb, d_scales)
         load_comp(1)
         load_codes(a_codes_raw, a_words, 1)
-        load_comp(2)
-        load_gains()
-        load_comp(3)
         load_x(0)
-        load_comp(4)
+        load_gains()
+        load_comp(2)
         load_codes(d_codes, d_words, 1)
-        load_comp(5)
         load_x(1)
-        load_comp(6)
+        load_comp(3)
         load_x(2)
-        load_comp(7)
         load_x(3)
         load_x(4)
         load_base(0)
@@ -450,47 +460,48 @@ def tile_mora_repeated_update_s12_kernel(
             load_base(i)
 
         spread_copy_gain()
-        comp_group(0, V)
+        comp_group(0, 0, 2)
         permute_a(0)
-        comp_quantize(0)
+        comp_group(0, 2, 2)
         e_part(0)
-        comp_group(1, V)
+        comp_quantize(0, 0, 4)
+        comp_group(1, 0, 2)
         permute_a(1)
-        e_matmul(1, 0)
-        e_matmul(1, 1)
-        widen_gains()
-        e_matmul(1, 2)
-        e_matmul(1, 3)
+        comp_group(1, 2, 2)
+        e_part(1)
         x_transpose(0)
-        turn_gains()
-        e_part(2)
+        widen_gains()
+        e_matmul(2, 0)
+        e_matmul(2, 1)
         x_transpose(1)
-        for piece in range(2, 7):
-            comp_group(piece, V)
-            comp_quantize(piece - 1)
-        x_quantize(0)
+        e_matmul(2, 2)
+        turn_gains()
+        e_matmul(2, 3)
         e_matmul(3, 0)
         x_transpose(2)
-        e_matmul(3, 1)
-        z_matmul(0, 0)
-        comp_group(7, V)
-        comp_quantize(6)
-        comp_quantize(7)
-        z_matmul_by_passes(0, 1)
+        comp_quantize(1, 0, 4)
+        comp_group(2, 0, 4)
+        comp_quantize(2, 0, 4)
+        comp_group(3, 0, 2)
+        x_quantize(0)
+        comp_group(3, 2, 2)
+        comp_quantize(3, 0, 4)
+        for g in range(4):
+            z_pass(0, g)
         e_quantize(0)
-        e_quantize(1)
-        z_group(0, 0, V)
-        e_quantize(2)
-        z_quantize(0, 0)
         x_transpose(3)
+        for i in range(2):
+            z_leave_bank(i, 0)
+            z_leave_bank(i, 1)
+        e_matmul(3, 1)
         e_matmul(3, 2)
+        z_quantize_tile(0)
+        z_quantize_tile(1)
+        y_direct(0, 0)
         e_matmul(3, 3)
-        z_group(0, 1, V)
-        z_quantize(0, 1)
+        y_direct(1, 0)
         x_quantize(1)
         x_transpose(4)
-        y_direct(0, 0)
-        y_direct(1, 0)
         z_matmul(1, 0)
 
         def finish(s, j, c):
@@ -501,66 +512,60 @@ def tile_mora_repeated_update_s12_kernel(
         def mul2(s, j):
             multiply(2 * s, j)
             multiply(2 * s + 1, j)
-        def add2(s, j):
-            add_base(2 * s, j, nc.vector)
-            add_base(2 * s + 1, j, nc.vector)
+        def add2(s, j, engine):
+            add_base(2 * s, j, engine)
+            store(2 * s, j)
+            add_base(2 * s + 1, j, engine)
+            store(2 * s + 1, j)
         def y2(s, j):
             y_direct(2 * s, j)
             y_direct(2 * s + 1, j)
-        e_quantize(3)
+        def add1(i, j, engine):
+            add_base(i, j, engine)
+            store(i, j)
         mul2(0, 0)
+        e_quantize(1)
         y2(0, 1)
         z_group(1, 0, S)
         x_transpose(5)
-        add2(0, 0)
-        mul2(0, 1)
+        add2(0, 0, VE)
         z_matmul(1, 1)
+        mul2(0, 1)
         x_quantize(2)
-        z_quantize(1, 0)
         z_group(1, 1, S)
         x_transpose(6)
-        add_base(0, 1, nc.vector)
-        z_quantize(1, 1)
-        add_base(1, 1, nc.vector)
+        add1(0, 1, VE)
+        z_quantize(1, 0, 2)
         z_matmul(2, 0)
+        add1(1, 1, VE)
         y2(1, 0)
         z_group(2, 0, S)
         x_transpose(7)
         mul2(1, 0)
-        y2(1, 1)
         z_matmul(2, 1)
-        add_base(2, 0, nc.vector)
+        y2(1, 1)
+        add1(2, 0, VE)
         x_quantize(3)
-        z_quantize(2, 0)
-        add_base(3, 0, nc.vector)
-        multiply(2, 1)
+        add1(3, 0, VE)
         z_group(2, 1, S)
         z_matmul(3, 0)
+        multiply(2, 1)
+        z_quantize(2, 0, 2)
         multiply(3, 1)
-        z_quantize(2, 1)
-        y2(2, 0)
-        add_base(2, 1, nc.vector)
-        z_group(3, 0, S)
         z_matmul(3, 1)
+        y_transposed(2, 0)
+        z_group(3, 0, V)
+        add1(2, 1, VE)
         y_transposed(2, 1)
-        add_base(3, 1, nc.vector)
-        multiply(4, 0)
-        z_quantize(3, 0)
-        multiply(5, 0)
         z_group(3, 1, V)
-        add_base(4, 0, nc.vector)
-        z_quantize(3, 1)
-        turn_back(4, 1, 0)
-        turn_back(5, 1, 0)
+        add1(3, 1, VE)
+        z_quantize(3, 0, 2)
+        finish(2, 0, 0)
+        finish(2, 0, 1)
         y_transposed(3, 0)
-        add_base(5, 0, nc.vector)
-        add_turned(4, 1, 0)
-        add_turned(5, 1, 0)
-        turn_back(4, 1, 1, "direct_ps", DIRECT_BANKS)
-        turn_back(5, 1, 1, "direct_ps", DIRECT_BANKS)
+        finish(2, 1, 0)
+        finish(2, 1, 1)
         y_transposed(3, 1)
-        add_turned(4, 1, 1)
-        add_turned(5, 1, 1)
         for j in range(2):
             for c in range(2):
                 finish(3, j, c)

@@ -151,10 +151,10 @@ def tile_mora_repeated_update_s12_kernel(
                 comp_grouped[g] = rotating.tile(
                     [P, WORD, CHANNELS // (WORD * RUN), RUN, WORD], BF16, name="comp_grouped", align_bytes=64
                 )
-            source = comp_rows[g][:].rearrange("p v (hq t e) -> p t hq e v", t=WORD, e=RUN)
-            nc.vector.tensor_copy(
-                out=comp_grouped[g][:, first : first + count], in_=source[:, first : first + count]
-            )
+            source = comp_rows[g][:].rearrange("p v (hq t e i) -> p t hq e v i", t=WORD, e=2, i=4)
+            target = comp_grouped[g][:].rearrange("p t hq (e i) v -> p t hq e v i", i=4)
+            for t in range(first, first + count):
+                nc.vector.tensor_copy(out=target[:, t], in_=source[:, t])
 
         def comp_quantize(g, first, count):
             columns = slice(2 * P * first, 2 * P * (first + count))

@@ -30,8 +30,8 @@ BLOCKS = HALF // P
 SCALE_ROWS = 4
 GAIN_ROWS = WORD + COPIES * (COLUMNS // P)
 SPREAD = COPIES * COLUMNS // P
-ROW_BUFS, E_BUFS = 12, 3
-SUM_BANKS, TURN_BANKS, DIRECT_BANKS = 4, 2, 2
+X_BUFS, BASE_BUFS, E_BUFS = 6, 3, 3
+SUM_BANKS, TURN_BANKS, DIRECT_BANKS = 2, 2, 4
 POOL_WIDTH = 512
 
 
@@ -73,17 +73,18 @@ def tile_mora_repeated_update_s12_kernel(
         make_identity(nc, identity[:])
         nc.scalar.activation(out=dummy[:], in_=dummy[:], func=COPY)
 
-        x_rows, comp_rows, base_rows = {}, {}, {}
+        x_rows, comp_rows, base_rows, base_pairs = {}, {}, {}, {}
 
         def load_x(i):
-            x_rows[i] = rotating.tile([P, FEATURES], BF16, name="x_rows", tag="token_rows", bufs=ROW_BUFS, align_bytes=64)
+            x_rows[i] = rotating.tile([P, FEATURES], BF16, name="x_rows", bufs=X_BUFS, align_bytes=64)
             nc.sync.dma_start(out=x_rows[i][:], in_=x[P * i : P * (i + 1), :])
 
-        def load_base(i):
-            base_rows[i] = rotating.tile(
-                [P, COPIES, COLUMNS], BF16, name="base_rows", tag="token_rows", bufs=ROW_BUFS, align_bytes=64
-            )
-            nc.sync.dma_start(out=base_rows[i][:].rearrange("p c n -> p (c n)"), in_=base[P * i : P * (i + 1), :])
+        def load_base(s):
+            base_pairs[s] = rotating.tile([P, 2, COPIES, COLUMNS], BF16, name="base_pair", bufs=BASE_BUFS, align_bytes=64)
+            rows = base[PAIR * s : PAIR * (s + 1), :].rearrange("(a p) n -> p a n", p=P)
+            nc.sync.dma_start(out=base_pairs[s][:].rearrange("p a c n -> p a (c n)"), in_=rows)
+            for place in range(2):
+                base_rows[2 * s + place] = base_pairs[s][:, place]
 
         def load_comp(g):
             comp_rows[g] = rotating.tile(
@@ -91,6 +92,13 @@ def tile_mora_repeated_update_s12_kernel(
             )
             rows = comp[PASS * g : PASS * (g + 1), :]
             nc.sync.dma_start(out=comp_rows[g][:], in_=rows.rearrange("(p v) r -> p v r", v=WORD))
+
+        half_rows = {}
+
+        def load_comp_half(h):
+            half_rows[h] = rotating.tile([P, WORD, PASS], BF16, name="x_rows", bufs=X_BUFS, align_bytes=64)
+            block = comp[0:PASS, PASS * h : PASS * (h + 1)]
+            nc.sync.dma_start(out=half_rows[h][:], in_=block.rearrange("(p v) r -> p v r", v=WORD))
 
         def load_codes(tiles, words, half):
             columns = words[:, :, 2 * HALF * half : 2 * HALF * (half + 1)]
@@ -116,22 +124,32 @@ def tile_mora_repeated_update_s12_kernel(
         def load_copy_gain():
             nc.sync.dma_start(out=copy_gain_runs[:], in_=copy_gain.rearrange("c (p m) -> (c p) m", m=SPREAD))
 
-        x_grouped, x_mx = {}, {}
+        x_grouped, x_mx, x_banks = {}, {}, {}
 
-        def x_transpose(i):
+        def x_transpose(i, tag="turned_ps", bufs=TURN_BANKS, leave=True):
             s, place = divmod(i, 2)
             if place == 0:
                 x_grouped[s] = rotating.tile([P, FEATURE_PASSES, PAIR, 2], F32, name="x_grouped", tag="eight_kib", bufs=3, align_bytes=64)
             words = x_rows[i][:].bitcast(F32)
+            banks = {}
             for g0 in range(0, FEATURE_PASSES, 2):
-                bank = psum.tile([P, 4, P], F32, name="turned_ps", bufs=TURN_BANKS)
+                bank = psum.tile([P, 4, P], F32, name=tag, bufs=bufs)
+                banks[g0] = bank
                 for g in (g0, g0 + 1):
                     for u in range(2):
                         first = WORDS * g + u
                         nc.tensor.transpose(bank[:, 2 * (g - g0) + u, :], words[:, first : first + WORDS - 1 : 2], identity[:])
+            x_banks[i] = banks
+            if leave:
+                x_leave(i)
+
+        def x_leave(i):
+            s, place = divmod(i, 2)
+            banks = x_banks[i]
+            for g0 in range(0, FEATURE_PASSES, 2):
                 nc.scalar.copy(
                     out=x_grouped[s][:, g0 : g0 + 2, P * place : P * (place + 1), :],
-                    in_=bank[:].rearrange("p (g u) r -> p g r u", u=2),
+                    in_=banks[g0][:].rearrange("p (g u) r -> p g r u", u=2),
                 )
 
         def x_quantize(s):
@@ -146,15 +164,36 @@ def tile_mora_repeated_update_s12_kernel(
 
         comp_grouped = {}
 
-        def comp_group(g, first, count):
-            if first == 0:
+        def first_column(g, h, t):
+            return PASS * h + P * t if g == 0 else 2 * P * t + P * h
+
+        def comp_group_half(h):
+            if h == 0:
+                comp_grouped[0] = rotating.tile(
+                    [P, CHANNEL_PASSES, WORD, P // RUN, RUN, WORD], BF16, name="comp_grouped", align_bytes=64
+                )
+            source = half_rows[h][:].rearrange("p v (q t e i) -> p t q e v i", t=WORD, e=2, i=4)
+            target = comp_grouped[0][:, h].rearrange("p t q (e i) v -> p t q e v i", i=4)
+            for t in range(WORD):
+                nc.vector.tensor_copy(out=target[:, t], in_=source[:, t])
+
+        def comp_quantize_half(h):
+            columns = slice(PASS * h, PASS * (h + 1))
+            nc.vector.quantize_mx(
+                out=comp_codes[:, 0, columns].bitcast(MXFP8),
+                scales=comp_scales[:, 0, columns],
+                in_=comp_grouped[0][:, h].rearrange("p t q e v -> p (t q e v)"),
+            )
+
+        def comp_group(g, first, count, copy):
+            if g not in comp_grouped:
                 comp_grouped[g] = rotating.tile(
                     [P, WORD, CHANNELS // (WORD * RUN), RUN, WORD], BF16, name="comp_grouped", align_bytes=64
                 )
             source = comp_rows[g][:].rearrange("p v (hq t e i) -> p t hq e v i", t=WORD, e=2, i=4)
             target = comp_grouped[g][:].rearrange("p t hq (e i) v -> p t hq e v i", i=4)
             for t in range(first, first + count):
-                nc.vector.tensor_copy(out=target[:, t], in_=source[:, t])
+                copy(out=target[:, t], in_=source[:, t])
 
         def comp_quantize(g, first, count):
             columns = slice(2 * P * first, 2 * P * (first + count))
@@ -168,7 +207,7 @@ def tile_mora_repeated_update_s12_kernel(
             words = copy_gain_runs[:].bitcast(F32)
             target = copy_gain_sb[:].rearrange("p c n -> p (c n)").bitcast(F32).rearrange("p (n m) -> p n m", n=P)
             for first in range(0, SPREAD // 2, 4):
-                bank = psum.tile([P, 4, P], F32, name="sums_ps", bufs=SUM_BANKS)
+                bank = psum.tile([P, 4, P], F32, name="direct_ps", bufs=DIRECT_BANKS)
                 for m in range(first, first + 4):
                     nc.tensor.transpose(bank[:, m - first, :], words[:, m : m + 1].to_broadcast([P, P]), identity[:])
                 nc.scalar.copy(out=target[:, :, first : first + 4], in_=bank[:].rearrange("p m n -> p n m"))
@@ -177,7 +216,7 @@ def tile_mora_repeated_update_s12_kernel(
             nc.scalar.copy(out=gain_square[:], in_=gain_rows[:])
 
         def turn_gains():
-            bank = psum.tile([P, 4, P], F32, name="direct_ps", bufs=DIRECT_BANKS)
+            bank = psum.tile([P, 4, P], F32, name="sums_ps", bufs=SUM_BANKS)
             for h in range(CHANNEL_PASSES):
                 nc.tensor.transpose(bank[:, h, :], gain_square[:, h, :], identity[:])
             nc.scalar.copy(out=gain_columns[:], in_=bank[:, 0:CHANNEL_PASSES, 0:GAIN_ROWS])
@@ -192,7 +231,7 @@ def tile_mora_repeated_update_s12_kernel(
                     in_=source.bitcast(I32).rearrange("p g (q t i) -> p g t q i", t=WORD, i=ints),
                 )
 
-        def e_matmul(part, b, tag="sums_ps", bufs=SUM_BANKS):
+        def e_matmul(part, b, tag="direct_ps", bufs=DIRECT_BANKS):
             j, h = divmod(part, CHANNEL_PASSES)
             if b == 0 and h == 0:
                 e_grouped[j] = rotating.tile(
@@ -227,14 +266,14 @@ def tile_mora_repeated_update_s12_kernel(
 
         z_rounded, z_grouped, z_mx, z_tile = {}, {}, {}, {}
 
-        def z_matmul(s, h):
+        def z_matmul(s, h, tag="sums_ps", bufs=SUM_BANKS):
             codes, scales = x_mx[s]
             z_rounded[(s, h)] = rotating.tile([P, WORD, PAIR], BF16, name="z_rounded", bufs=2, align_bytes=64)
             for i in range(WORD // 2):
-                bank = psum.tile([P, 2, PAIR], F32, name="sums_ps", bufs=SUM_BANKS)
+                bank = psum.tile([P, 2, PAIR], F32, name=tag, bufs=bufs)
                 for t in (2 * i, 2 * i + 1):
-                    m = 2 * P * t + P * h
                     for g in range(FEATURE_PASSES):
+                        m = first_column(g, h, t)
                         nc.tensor.matmul_mx(
                             out=bank[:, t - 2 * i, :],
                             lhsT=comp_codes[:, g, m : m + P].bitcast(MXFP8),
@@ -260,9 +299,9 @@ def tile_mora_repeated_update_s12_kernel(
                 tokens = slice(P * place, P * (place + 1))
                 for h in range(CHANNEL_PASSES):
                     if g == 0:
-                        open_banks[(place, h)] = psum.tile([P, WORD, P], F32, name="sums_ps", bufs=SUM_BANKS)
+                        open_banks[(place, h)] = psum.tile([P, WORD, P], F32, name="direct_ps", bufs=DIRECT_BANKS)
                     for t in range(WORD):
-                        m = 2 * P * t + P * h
+                        m = first_column(g, h, t)
                         nc.tensor.matmul_mx(
                             out=open_banks[(place, h)][:, t, :],
                             lhsT=comp_codes[:, g, m : m + P].bitcast(MXFP8),
@@ -273,10 +312,37 @@ def tile_mora_repeated_update_s12_kernel(
                             stop=(g == FEATURE_PASSES - 1 and t == WORD - 1),
                         )
 
+        def z_narrow(i, h):
+            s, place = divmod(i, 2)
+            codes, scales = x_mx[s]
+            tokens = slice(P * place, P * (place + 1))
+            open_banks[(place, h)] = psum.tile([P, WORD, P], F32, name="sums_ps", bufs=SUM_BANKS)
+            for t in range(WORD):
+                for g in range(FEATURE_PASSES):
+                    m = first_column(g, h, t)
+                    nc.tensor.matmul_mx(
+                        out=open_banks[(place, h)][:, t, :],
+                        lhsT=comp_codes[:, g, m : m + P].bitcast(MXFP8),
+                        lhsT_scale=comp_scales[:, g, m : m + P],
+                        rhs=codes[:, g, tokens].bitcast(MXFP8),
+                        rhs_scale=scales[:, g, tokens],
+                        start=(g == 0),
+                        stop=(g == FEATURE_PASSES - 1),
+                    )
+
+        def z_leave_narrow(i, h):
+            s, place = divmod(i, 2)
+            nc.vector.tensor_tensor(
+                out=z_grouped[s][:, h, P * place : P * (place + 1), :],
+                in0=open_banks[(place, h)][:].rearrange("p t n -> p n t"),
+                in1=gain_columns[:, h, 0:WORD].unsqueeze(1).to_broadcast([P, P, WORD]),
+                op=MULT,
+            )
+
         tile_grouped = {}
 
         def z_leave_bank(i, h):
-            if h == 0:
+            if i not in tile_grouped:
                 tile_grouped[i] = rotating.tile([P, CHANNEL_PASSES, P, WORD], BF16, name="z_rounded", bufs=2, align_bytes=64)
             nc.vector.tensor_tensor(
                 out=tile_grouped[i][:, h],
@@ -343,7 +409,7 @@ def tile_mora_repeated_update_s12_kernel(
             columns = slice(HALF * j, HALF * (j + 1))
             bank = y_banks[(i, j)]
             s, place = divmod(i, 2)
-            if place == 0:
+            if (s, j) not in products:
                 products[(s, j)] = rotating.tile(
                     [P, 2, COPIES, HALF], F32, name="product", tag="comp_then_products", bufs=4, align_bytes=64
                 )
@@ -367,6 +433,17 @@ def tile_mora_repeated_update_s12_kernel(
                         start = HALF * j + first
                         engine.tensor_tensor(out=part, in0=part, in1=base_rows[i][:, c, start : start + POOL_WIDTH], op=ADD)
 
+        def add_pair(s, j):
+            product = products[(s, j)][:]
+            nc.vector.tensor_tensor(out=product, in0=product, in1=base_pairs[s][:, :, :, HALF * j : HALF * (j + 1)], op=ADD)
+            store(2 * s, j)
+            store(2 * s + 1, j)
+
+        def add_copy(i, j, c, engine):
+            s, place = divmod(i, 2)
+            part = products[(s, j)][:, place, c, :]
+            engine.tensor_tensor(out=part, in0=part, in1=base_rows[i][:, c, HALF * j : HALF * (j + 1)], op=ADD)
+
         def store(i, j):
             s, place = divmod(i, 2)
             rows = out[P * i : P * (i + 1), :].rearrange("p (c n) -> p c n", c=COPIES)
@@ -374,11 +451,17 @@ def tile_mora_repeated_update_s12_kernel(
 
         turned_products = {}
 
+        turned_banks = {}
+
         def y_transposed(s, j):
+            y_transposed_mm(s, j)
+            turned_out(s, j)
+
+        def y_transposed_mm(s, j):
             banks = []
             for b in range(BLOCKS):
                 if b % 2 == 0:
-                    banks.append(psum.tile([P, 2, PAIR], F32, name="sums_ps", bufs=SUM_BANKS))
+                    banks.append(psum.tile([P, 2, PAIR], F32, name="direct_ps", bufs=DIRECT_BANKS))
                 columns = slice(P * b, P * (b + 1))
                 for h in range(CHANNEL_PASSES):
                     codes, scales = z_mx[(s, h)]
@@ -391,6 +474,10 @@ def tile_mora_repeated_update_s12_kernel(
                         start=(h == 0),
                         stop=(h == CHANNEL_PASSES - 1),
                     )
+            turned_banks[(s, j)] = banks
+
+        def turned_out(s, j):
+            banks = turned_banks[(s, j)]
             turned = rotating.tile([P, COPIES, BLOCKS, PAIR], F32, name="turned", tag="eight_kib", bufs=3, align_bytes=64)
             for c in range(COPIES):
                 for b in range(BLOCKS):
@@ -433,15 +520,15 @@ def tile_mora_repeated_update_s12_kernel(
 
         V, S = nc.vector.tensor_copy, nc.scalar.copy
         VE = nc.vector
-        G = nc.gpsimd
         load_copy_gain()
-        load_comp(0)
+        load_comp_half(0)
         load_scales(a_scales_raw, a_scales)
         load_codes(a_codes_raw, a_words, 0)
         load_codes(d_codes, d_words, 0)
         load_scales(d_scales_sb, d_scales)
-        load_comp(1)
+        load_comp_half(1)
         load_codes(a_codes_raw, a_words, 1)
+        load_comp(1)
         load_x(0)
         load_gains()
         load_comp(2)
@@ -453,21 +540,20 @@ def tile_mora_repeated_update_s12_kernel(
         load_x(4)
         load_base(0)
         load_x(5)
-        load_base(1)
         load_x(6)
         load_x(7)
-        for i in range(2, 8):
-            load_base(i)
+        load_base(1)
+        load_base(2)
 
         spread_copy_gain()
-        comp_group(0, 0, 2)
+        comp_group_half(0)
         permute_a(0)
-        comp_group(0, 2, 2)
+        comp_quantize_half(0)
         e_part(0)
-        comp_quantize(0, 0, 4)
-        comp_group(1, 0, 2)
+        comp_group_half(1)
         permute_a(1)
-        comp_group(1, 2, 2)
+        comp_quantize_half(1)
+        comp_group(1, 0, 4, V)
         e_part(1)
         x_transpose(0)
         widen_gains()
@@ -477,95 +563,96 @@ def tile_mora_repeated_update_s12_kernel(
         e_matmul(2, 2)
         turn_gains()
         e_matmul(2, 3)
-        e_matmul(3, 0)
-        x_transpose(2)
+        comp_group(2, 0, 2, V)
         comp_quantize(1, 0, 4)
-        comp_group(2, 0, 4)
-        comp_quantize(2, 0, 4)
-        comp_group(3, 0, 2)
+        comp_group(2, 2, 2, V)
+        comp_group(3, 0, 2, V)
+        comp_group(3, 2, 2, S)
+        e_matmul(3, 0, "sums_ps", SUM_BANKS)
+        e_matmul(3, 1, "sums_ps", SUM_BANKS)
         x_quantize(0)
-        comp_group(3, 2, 2)
+        comp_quantize(2, 0, 4)
+        e_quantize(0)
         comp_quantize(3, 0, 4)
+        x_transpose(2)
         for g in range(4):
             z_pass(0, g)
-        e_quantize(0)
         x_transpose(3)
         for i in range(2):
             z_leave_bank(i, 0)
             z_leave_bank(i, 1)
-        e_matmul(3, 1)
-        e_matmul(3, 2)
+        e_matmul(3, 2, "sums_ps", SUM_BANKS)
+        e_matmul(3, 3, "sums_ps", SUM_BANKS)
         z_quantize_tile(0)
         z_quantize_tile(1)
         y_direct(0, 0)
-        e_matmul(3, 3)
         y_direct(1, 0)
         x_quantize(1)
+        e_quantize(1)
         x_transpose(4)
         z_matmul(1, 0)
-
-        def finish(s, j, c):
-            turn_back(2 * s, j, c)
-            add_turned(2 * s, j, c)
-            turn_back(2 * s + 1, j, c, "direct_ps", DIRECT_BANKS)
-            add_turned(2 * s + 1, j, c)
-        def mul2(s, j):
-            multiply(2 * s, j)
-            multiply(2 * s + 1, j)
-        def add2(s, j, engine):
-            add_base(2 * s, j, engine)
-            store(2 * s, j)
-            add_base(2 * s + 1, j, engine)
-            store(2 * s + 1, j)
-        def y2(s, j):
-            y_direct(2 * s, j)
-            y_direct(2 * s + 1, j)
-        def add1(i, j, engine):
-            add_base(i, j, engine)
-            store(i, j)
-        mul2(0, 0)
-        e_quantize(1)
-        y2(0, 1)
+        y_direct(0, 1)
+        y_direct(1, 1)
+        G = nc.gpsimd
+        def finish(s, j):
+            for c in range(2):
+                turn_back(2 * s, j, c)
+                add_turned(2 * s, j, c)
+                turn_back(2 * s + 1, j, c, "sums_ps", SUM_BANKS)
+                add_turned(2 * s + 1, j, c)
+        def multiply_pair(s):
+            i = 2 * s
+            multiply(i, 0)
+            add_copy(i, 0, 0, G)
+            add_copy(i, 0, 1, G)
+            store(i, 0)
+            multiply(i + 1, 0)
+            add_copy(i + 1, 0, 0, G)
+            multiply(i, 1)
+            multiply(i + 1, 1)
+        multiply_pair(0)
         z_group(1, 0, S)
         x_transpose(5)
-        add2(0, 0, VE)
         z_matmul(1, 1)
-        mul2(0, 1)
+        add_copy(1, 0, 1, VE)
+        store(1, 0)
+        add_base(0, 1, VE)
+        store(0, 1)
         x_quantize(2)
         z_group(1, 1, S)
         x_transpose(6)
-        add1(0, 1, VE)
+        x_transpose(7, "sums_ps", SUM_BANKS)
+        z_matmul(2, 0, "direct_ps", DIRECT_BANKS)
         z_quantize(1, 0, 2)
-        z_matmul(2, 0)
-        add1(1, 1, VE)
-        y2(1, 0)
-        z_group(2, 0, S)
-        x_transpose(7)
-        mul2(1, 0)
-        z_matmul(2, 1)
-        y2(1, 1)
-        add1(2, 0, VE)
+        add_base(1, 1, VE)
+        store(1, 1)
+        load_base(3)
         x_quantize(3)
-        add1(3, 0, VE)
+        y_direct(2, 0)
+        y_direct(3, 0)
+        z_group(2, 0, S)
+        z_matmul(2, 1)
+        y_direct(2, 1)
+        y_direct(3, 1)
+        multiply_pair(1)
         z_group(2, 1, S)
         z_matmul(3, 0)
-        multiply(2, 1)
+        add_copy(3, 0, 1, VE)
+        store(3, 0)
         z_quantize(2, 0, 2)
-        multiply(3, 1)
+        add_base(2, 1, VE)
+        store(2, 1)
         z_matmul(3, 1)
         y_transposed(2, 0)
         z_group(3, 0, V)
-        add1(2, 1, VE)
+        add_base(3, 1, VE)
+        store(3, 1)
         y_transposed(2, 1)
         z_group(3, 1, V)
-        add1(3, 1, VE)
         z_quantize(3, 0, 2)
-        finish(2, 0, 0)
-        finish(2, 0, 1)
+        finish(2, 0)
         y_transposed(3, 0)
-        finish(2, 1, 0)
-        finish(2, 1, 1)
+        finish(2, 1)
         y_transposed(3, 1)
-        for j in range(2):
-            for c in range(2):
-                finish(3, j, c)
+        finish(3, 0)
+        finish(3, 1)

@@ -124,7 +124,7 @@ def tile_mora_repeated_update_s12_kernel(
         def load_copy_gain():
             nc.sync.dma_start(out=copy_gain_runs[:], in_=copy_gain.rearrange("c (p m) -> (c p) m", m=SPREAD))
 
-        x_grouped, x_mx, x_banks = {}, {}, {}
+        x_grouped, x_mx, x_banks, x_sorted, sorted_pairs = {}, {}, {}, {}, {}
 
         def x_transpose(i, tag="turned_ps", bufs=TURN_BANKS, leave=True):
             s, place = divmod(i, 2)
@@ -138,10 +138,17 @@ def tile_mora_repeated_update_s12_kernel(
                 for g in (g0, g0 + 1):
                     for u in range(2):
                         first = WORDS * g + u
-                        nc.tensor.transpose(bank[:, 2 * (g - g0) + u, :], words[:, first : first + WORDS - 1 : 2], identity[:])
+                        source = x_sorted[i][:, g, u, :] if i in x_sorted else words[:, first : first + WORDS - 1 : 2]
+                        nc.tensor.transpose(bank[:, 2 * (g - g0) + u, :], source, identity[:])
             x_banks[i] = banks
             if leave:
                 x_leave(i)
+
+        def x_sort(i, copy):
+            if i % 2 == 1:
+                sorted_pairs[i] = rotating.tile([P, 2, FEATURE_PASSES, 2, P], F32, name="comp_grouped", align_bytes=64)
+            x_sorted[i] = sorted_pairs[i - 1 + i % 2][:, 1 - i % 2]
+            copy(out=x_sorted[i], in_=x_rows[i][:].bitcast(F32).rearrange("r (g p u) -> r g u p", u=2, p=P))
 
         def x_leave(i):
             s, place = divmod(i, 2)
@@ -538,9 +545,9 @@ def tile_mora_repeated_update_s12_kernel(
         load_x(2)
         load_x(3)
         load_x(4)
-        load_base(0)
         load_x(5)
         load_x(6)
+        load_base(0)
         load_x(7)
         load_base(1)
         load_base(2)
@@ -575,6 +582,8 @@ def tile_mora_repeated_update_s12_kernel(
         e_quantize(0)
         comp_quantize(3, 0, 4)
         x_transpose(2)
+        x_sort(3, S)
+        x_sort(4, S)
         for g in range(4):
             z_pass(0, g)
         x_transpose(3)
@@ -583,6 +592,7 @@ def tile_mora_repeated_update_s12_kernel(
             z_leave_bank(i, 1)
         e_matmul(3, 2, "sums_ps", SUM_BANKS)
         e_matmul(3, 3, "sums_ps", SUM_BANKS)
+        x_sort(5, S)
         z_quantize_tile(0)
         z_quantize_tile(1)
         y_direct(0, 0)
@@ -636,7 +646,7 @@ def tile_mora_repeated_update_s12_kernel(
         y_direct(3, 1)
         multiply_pair(1)
         z_group(2, 1, S)
-        z_matmul(3, 0)
+        z_matmul(3, 0, "direct_ps", DIRECT_BANKS)
         add_copy(3, 0, 1, VE)
         store(3, 0)
         z_quantize(2, 0, 2)

@@ -617,18 +617,17 @@ def tile_mora_repeated_update_s12_kernel(
             add_copy(i, 0, 1, G)
             store(i, 0)
             multiply(i + 1, 0)
-            add_copy(i + 1, 0, 0, G)
             multiply(i, 1)
             multiply(i + 1, 1)
         multiply_pair(0)
         z_group(1, 0, S)
         x_transpose(5)
         z_matmul(1, 1)
-        add_copy(1, 0, 1, VE)
+        add_base(1, 0, VE)
         store(1, 0)
+        x_quantize(2)
         add_base(0, 1, VE)
         store(0, 1)
-        x_quantize(2)
         z_group(1, 1, S)
         x_transpose(6)
         x_transpose(7, "sums_ps", SUM_BANKS)
@@ -647,18 +646,18 @@ def tile_mora_repeated_update_s12_kernel(
         multiply_pair(1)
         z_group(2, 1, S)
         z_matmul(3, 0, "direct_ps", DIRECT_BANKS)
-        add_copy(3, 0, 1, VE)
+        add_base(3, 0, VE)
         store(3, 0)
         z_quantize(2, 0, 2)
         add_base(2, 1, VE)
         store(2, 1)
+        z_group(3, 0, S)
         z_matmul(3, 1)
         y_transposed(2, 0)
-        z_group(3, 0, V)
-        add_base(3, 1, VE)
-        store(3, 1)
         y_transposed(2, 1)
         z_group(3, 1, V)
+        add_base(3, 1, VE)
+        store(3, 1)
         z_quantize(3, 0, 2)
         finish(2, 0)
         y_transposed(3, 0)

@@ -145,9 +145,9 @@ def tile_mora_repeated_update_s12_kernel(
                 x_leave(i)
 
         def x_sort(i, copy):
-            if i % 2 == 1:
+            if i % 2 == 0:
                 sorted_pairs[i] = rotating.tile([P, 2, FEATURE_PASSES, 2, P], F32, name="comp_grouped", align_bytes=64)
-            x_sorted[i] = sorted_pairs[i - 1 + i % 2][:, 1 - i % 2]
+            x_sorted[i] = sorted_pairs[i - i % 2][:, i % 2]
             copy(out=x_sorted[i], in_=x_rows[i][:].bitcast(F32).rearrange("r (g p u) -> r g u p", u=2, p=P))
 
         def x_leave(i):
@@ -528,80 +528,81 @@ def tile_mora_repeated_update_s12_kernel(
         V, S = nc.vector.tensor_copy, nc.scalar.copy
         VE = nc.vector
         load_copy_gain()
-        load_comp_half(0)
         load_scales(a_scales_raw, a_scales)
         load_codes(a_codes_raw, a_words, 0)
         load_codes(d_codes, d_words, 0)
         load_scales(d_scales_sb, d_scales)
-        load_comp_half(1)
         load_codes(a_codes_raw, a_words, 1)
+        load_comp_half(0)
+        load_comp_half(1)
+        load_codes(d_codes, d_words, 1)
         load_comp(1)
         load_x(0)
         load_gains()
-        load_comp(2)
-        load_codes(d_codes, d_words, 1)
         load_x(1)
+        load_comp(2)
         load_comp(3)
         load_x(2)
         load_x(3)
         load_x(4)
         load_x(5)
         load_x(6)
-        load_base(0)
         load_x(7)
+        load_base(0)
         load_base(1)
         load_base(2)
 
         spread_copy_gain()
-        comp_group_half(0)
         permute_a(0)
-        comp_quantize_half(0)
         e_part(0)
-        comp_group_half(1)
         permute_a(1)
+        comp_group_half(0)
+        comp_group_half(1)
+        comp_quantize_half(0)
         comp_quantize_half(1)
-        comp_group(1, 0, 4, V)
         e_part(1)
+        e_part(2)
         x_transpose(0)
         widen_gains()
-        e_matmul(2, 0)
-        e_matmul(2, 1)
+        e_matmul(3, 0)
         x_transpose(1)
-        e_matmul(2, 2)
+        e_matmul(3, 1)
         turn_gains()
-        e_matmul(2, 3)
-        comp_group(2, 0, 2, V)
-        comp_quantize(1, 0, 4)
-        comp_group(2, 2, 2, V)
-        comp_group(3, 0, 2, V)
-        comp_group(3, 2, 2, S)
-        e_matmul(3, 0, "sums_ps", SUM_BANKS)
-        e_matmul(3, 1, "sums_ps", SUM_BANKS)
-        x_quantize(0)
-        comp_quantize(2, 0, 4)
+        e_matmul(3, 2)
+        e_matmul(3, 3)
+        comp_group(1, 0, 4, V)
         e_quantize(0)
+        comp_quantize(1, 0, 4)
+        comp_group(2, 0, 1, V)
+        x_quantize(0)
+        comp_group(2, 1, 3, V)
+        comp_group(3, 1, 3, S)
+        comp_group(3, 0, 1, V)
+        comp_quantize(2, 0, 4)
+        e_quantize(1)
+        x_sort(4, V)
         comp_quantize(3, 0, 4)
+        z_pass(0, 0)
+        z_pass(0, 1)
         x_transpose(2)
-        x_sort(3, S)
-        x_sort(4, S)
-        for g in range(4):
-            z_pass(0, g)
-        x_transpose(3)
+        x_transpose(3, "sums_ps", SUM_BANKS)
+        x_sort(5, S)
+        z_pass(0, 2)
+        x_transpose(4)
+        z_pass(0, 3)
+        x_transpose(5)
+        x_sort(6, S)
+        x_quantize(1)
         for i in range(2):
             z_leave_bank(i, 0)
             z_leave_bank(i, 1)
-        e_matmul(3, 2, "sums_ps", SUM_BANKS)
-        e_matmul(3, 3, "sums_ps", SUM_BANKS)
-        x_sort(5, S)
         z_quantize_tile(0)
         z_quantize_tile(1)
-        y_direct(0, 0)
-        y_direct(1, 0)
-        x_quantize(1)
-        e_quantize(1)
-        x_transpose(4)
         z_matmul(1, 0)
+        x_quantize(2)
+        y_direct(0, 0)
         y_direct(0, 1)
+        y_direct(1, 0)
         y_direct(1, 1)
         G = nc.gpsimd
         def finish(s, j):
@@ -616,16 +617,15 @@ def tile_mora_repeated_update_s12_kernel(
             add_copy(i, 0, 0, G)
             add_copy(i, 0, 1, G)
             store(i, 0)
-            multiply(i + 1, 0)
             multiply(i, 1)
+            multiply(i + 1, 0)
             multiply(i + 1, 1)
         multiply_pair(0)
         z_group(1, 0, S)
-        x_transpose(5)
+        x_sort(7, S)
         z_matmul(1, 1)
         add_base(1, 0, VE)
         store(1, 0)
-        x_quantize(2)
         add_base(0, 1, VE)
         store(0, 1)
         z_group(1, 1, S)
@@ -638,10 +638,10 @@ def tile_mora_repeated_update_s12_kernel(
         load_base(3)
         x_quantize(3)
         y_direct(2, 0)
-        y_direct(3, 0)
+        y_direct(2, 1)
         z_group(2, 0, S)
         z_matmul(2, 1)
-        y_direct(2, 1)
+        y_direct(3, 0)
         y_direct(3, 1)
         multiply_pair(1)
         z_group(2, 1, S)
@@ -655,9 +655,9 @@ def tile_mora_repeated_update_s12_kernel(
         z_matmul(3, 1)
         y_transposed(2, 0)
         y_transposed(2, 1)
-        z_group(3, 1, V)
         add_base(3, 1, VE)
         store(3, 1)
+        z_group(3, 1, V)
         z_quantize(3, 0, 2)
         finish(2, 0)
         y_transposed(3, 0)

@@ -145,8 +145,10 @@ def tile_mora_repeated_update_s12_kernel(
                 x_leave(i)
 
         def x_sort(i, copy):
-            if i % 2 == 0:
-                sorted_pairs[i] = rotating.tile([P, 2, FEATURE_PASSES, 2, P], F32, name="comp_grouped", align_bytes=64)
+            if i - i % 2 not in sorted_pairs:
+                sorted_pairs[i - i % 2] = rotating.tile(
+                    [P, 2, FEATURE_PASSES, 2, P], F32, name="comp_grouped", align_bytes=64
+                )
             x_sorted[i] = sorted_pairs[i - i % 2][:, i % 2]
             copy(out=x_sorted[i], in_=x_rows[i][:].bitcast(F32).rearrange("r (g p u) -> r g u p", u=2, p=P))
 
@@ -464,9 +466,9 @@ def tile_mora_repeated_update_s12_kernel(
             y_transposed_mm(s, j)
             turned_out(s, j)
 
-        def y_transposed_mm(s, j):
-            banks = []
-            for b in range(BLOCKS):
+        def y_transposed_mm(s, j, blocks=range(BLOCKS)):
+            banks = turned_banks.setdefault((s, j), [])
+            for b in blocks:
                 if b % 2 == 0:
                     banks.append(psum.tile([P, 2, PAIR], F32, name="direct_ps", bufs=DIRECT_BANKS))
                 columns = slice(P * b, P * (b + 1))
@@ -481,7 +483,6 @@ def tile_mora_repeated_update_s12_kernel(
                         start=(h == 0),
                         stop=(h == CHANNEL_PASSES - 1),
                     )
-            turned_banks[(s, j)] = banks
 
         def turned_out(s, j):
             banks = turned_banks[(s, j)]
@@ -528,8 +529,8 @@ def tile_mora_repeated_update_s12_kernel(
         V, S = nc.vector.tensor_copy, nc.scalar.copy
         VE = nc.vector
         load_copy_gain()
-        load_scales(a_scales_raw, a_scales)
         load_codes(a_codes_raw, a_words, 0)
+        load_scales(a_scales_raw, a_scales)
         load_codes(d_codes, d_words, 0)
         load_scales(d_scales_sb, d_scales)
         load_codes(a_codes_raw, a_words, 1)

@@ -64,14 +64,11 @@ def tile_mora_repeated_update_s12_kernel(
         gain_rows = resident.tile([P, CHANNEL_PASSES, P], BF16, name="gain_rows", align_bytes=64)
         gain_square = resident.tile([P, CHANNEL_PASSES, P], F32, name="gain_square", align_bytes=64)
         gain_columns = resident.tile([P, CHANNEL_PASSES, GAIN_ROWS], F32, name="gain_columns", align_bytes=64)
-        dummy = resident.tile([P, 1], F32, name="dummy", align_bytes=64)
 
         nc.vector.memset(a_scales_raw[:].rearrange("p g n -> p (g n)").bitcast(I32), 0)
         nc.vector.memset(d_scales_sb[:].rearrange("p g n -> p (g n)").bitcast(I32), 0)
-        nc.vector.memset(dummy[:], 0.0)
         nc.vector.memset(gain_rows[:], 0.0)
         make_identity(nc, identity[:])
-        nc.scalar.activation(out=dummy[:], in_=dummy[:], func=COPY)
 
         x_rows, comp_rows, base_rows, base_pairs = {}, {}, {}, {}
 

@@ -1,7 +1,6 @@
 from contextlib import ExitStack
 
 import concourse.mybir as mybir
-from concourse.masks import make_identity
 
 F32 = mybir.dt.float32
 BF16 = mybir.dt.bfloat16
@@ -29,10 +28,10 @@ HALF = 512
 BLOCKS = HALF // P
 SCALE_ROWS = 4
 GAIN_ROWS = WORD + COPIES * (COLUMNS // P)
-SPREAD = COPIES * COLUMNS // P
-X_BUFS, BASE_BUFS, E_BUFS = 6, 3, 3
+ROW_BUFS, E_BUFS, SMALL_BUFS = 10, 2, 9
 SUM_BANKS, TURN_BANKS, DIRECT_BANKS = 2, 2, 4
-POOL_WIDTH = 512
+RESULT_BUFS = 5
+TURNED_BUFS = 3
 
 
 def tile_mora_repeated_update_s12_kernel(
@@ -46,46 +45,55 @@ def tile_mora_repeated_update_s12_kernel(
         ctx.enter_context(tc.manual_schedule())
 
         halves = range(2)
-        a_codes_raw = [
-            resident.tile([P, CHANNEL_PASSES, 2 * PASS], U8, name="a_codes_raw%d" % h, align_bytes=64) for h in halves
-        ]
-        a_codes = [resident.tile([P, CHANNEL_PASSES, 2 * PASS], U8, name="a_codes%d" % h, align_bytes=64) for h in halves]
-        d_codes = [resident.tile([P, CHANNEL_PASSES, 2 * HALF], U8, name="d_codes%d" % j, align_bytes=64) for j in halves]
-        a_scales_raw = resident.tile([P, CHANNEL_PASSES, CHANNELS], U8, name="a_scales_raw", align_bytes=64)
+        def small(shape, dtype, name):
+            return rotating.tile(shape, dtype, name=name, tag="two_kib", bufs=SMALL_BUFS, align_bytes=64)
+
+        a_codes_raw = [small([P, CHANNEL_PASSES, 2 * PASS], U8, "a_codes_raw") for h in halves]
+        a_codes = [small([P, CHANNEL_PASSES, 2 * PASS], U8, "a_codes") for h in halves]
+        d_codes = [small([P, CHANNEL_PASSES, 2 * HALF], U8, "d_codes") for j in halves]
+        a_scales_raw = small([P, CHANNEL_PASSES, CHANNELS], U8, "a_scales_raw")
         a_scales_sb = [resident.tile([P, CHANNEL_PASSES, PASS], U8, name="a_scales_sb%d" % h, align_bytes=64) for h in halves]
-        d_scales_sb = resident.tile([P, CHANNEL_PASSES, COLUMNS], U8, name="d_scales_sb", align_bytes=64)
+        d_scales_sb = small([P, CHANNEL_PASSES, COLUMNS], U8, "d_scales_sb")
         comp_codes = resident.tile([P, FEATURE_PASSES, CHANNELS], U32, name="comp_codes", align_bytes=64)
         comp_scales = resident.tile([P, FEATURE_PASSES, CHANNELS], U8, name="comp_scales", align_bytes=64)
         e_codes = resident.tile([P, 2, CHANNEL_PASSES, HALF], U32, name="e_codes", align_bytes=64)
         e_scales = resident.tile([P, 2, CHANNEL_PASSES, HALF], U8, name="e_scales", align_bytes=64)
         copy_gain_sb = resident.tile([P, COPIES, COLUMNS], BF16, name="copy_gain_sb", align_bytes=64)
-        copy_gain_runs = resident.tile([P, SPREAD], BF16, name="copy_gain_runs", align_bytes=64)
         identity = resident.tile([P, P], F32, name="identity", align_bytes=64)
         gain_rows = resident.tile([P, CHANNEL_PASSES, P], BF16, name="gain_rows", align_bytes=64)
         gain_square = resident.tile([P, CHANNEL_PASSES, P], F32, name="gain_square", align_bytes=64)
         gain_columns = resident.tile([P, CHANNEL_PASSES, GAIN_ROWS], F32, name="gain_columns", align_bytes=64)
 
-        nc.vector.memset(a_scales_raw[:].rearrange("p g n -> p (g n)").bitcast(I32), 0)
         nc.vector.memset(d_scales_sb[:].rearrange("p g n -> p (g n)").bitcast(I32), 0)
-        nc.vector.memset(gain_rows[:], 0.0)
-        make_identity(nc, identity[:])
+
+        def fill_tiles():
+            for h in halves:
+                nc.vector.memset(a_scales_sb[h][:].rearrange("p g n -> p (g n)").bitcast(I32), 0)
+            nc.vector.memset(gain_rows[:], 0.0)
+            nc.vector.memset(identity[:], 0.0)
+            nc.gpsimd.affine_select(
+                out=identity[:],
+                in_=identity[:],
+                compare_op=mybir.AluOpType.not_equal,
+                fill=1.0,
+                base=0,
+                pattern=[[-1, P]],
+                channel_multiplier=1,
+            )
 
         x_rows, comp_rows, base_rows, base_pairs = {}, {}, {}, {}
 
         def load_x(i):
-            x_rows[i] = rotating.tile([P, FEATURES], BF16, name="x_rows", bufs=X_BUFS, align_bytes=64)
+            x_rows[i] = rotating.tile([P, FEATURES], BF16, name="x_rows", tag="rows", bufs=ROW_BUFS, align_bytes=64)
             nc.sync.dma_start(out=x_rows[i][:], in_=x[P * i : P * (i + 1), :])
 
-        def load_base(s):
-            base_pairs[s] = rotating.tile([P, 2, COPIES, COLUMNS], BF16, name="base_pair", bufs=BASE_BUFS, align_bytes=64)
-            rows = base[PAIR * s : PAIR * (s + 1), :].rearrange("(a p) n -> p a n", p=P)
-            nc.sync.dma_start(out=base_pairs[s][:].rearrange("p a c n -> p a (c n)"), in_=rows)
-            for place in range(2):
-                base_rows[2 * s + place] = base_pairs[s][:, place]
+        def load_base(i):
+            base_rows[i] = rotating.tile([P, COPIES, COLUMNS], BF16, name="base_rows", tag="rows", bufs=ROW_BUFS, align_bytes=64)
+            nc.sync.dma_start(out=base_rows[i][:].rearrange("p c n -> p (c n)"), in_=base[P * i : P * (i + 1), :])
 
         def load_comp(g):
             comp_rows[g] = rotating.tile(
-                [P, WORD, CHANNELS], BF16, name="comp_rows", tag="comp_then_products", bufs=4, align_bytes=64
+                [P, WORD, CHANNELS], BF16, name="comp_rows", tag="comp_then_products", bufs=RESULT_BUFS, align_bytes=64
             )
             rows = comp[PASS * g : PASS * (g + 1), :]
             nc.sync.dma_start(out=comp_rows[g][:], in_=rows.rearrange("(p v) r -> p v r", v=WORD))
@@ -93,7 +101,7 @@ def tile_mora_repeated_update_s12_kernel(
         half_rows = {}
 
         def load_comp_half(h):
-            half_rows[h] = rotating.tile([P, WORD, PASS], BF16, name="x_rows", bufs=X_BUFS, align_bytes=64)
+            half_rows[h] = rotating.tile([P, WORD, PASS], BF16, name="half_rows", tag="rows", bufs=ROW_BUFS, align_bytes=64)
             block = comp[0:PASS, PASS * h : PASS * (h + 1)]
             nc.sync.dma_start(out=half_rows[h][:], in_=block.rearrange("(p v) r -> p v r", v=WORD))
 
@@ -119,7 +127,10 @@ def tile_mora_repeated_update_s12_kernel(
             )
 
         def load_copy_gain():
-            nc.sync.dma_start(out=copy_gain_runs[:], in_=copy_gain.rearrange("c (p m) -> (c p) m", m=SPREAD))
+            nc.sync.dma_start(
+                out=copy_gain_sb[:].rearrange("p c n -> p (c n)"),
+                in_=copy_gain.rearrange("c n -> (c n)").partition_broadcast(P),
+            )
 
         x_grouped, x_mx, x_banks, x_sorted, sorted_pairs = {}, {}, {}, {}, {}
 
@@ -142,11 +153,7 @@ def tile_mora_repeated_update_s12_kernel(
                 x_leave(i)
 
         def x_sort(i, copy):
-            if i - i % 2 not in sorted_pairs:
-                sorted_pairs[i - i % 2] = rotating.tile(
-                    [P, 2, FEATURE_PASSES, 2, P], F32, name="comp_grouped", align_bytes=64
-                )
-            x_sorted[i] = sorted_pairs[i - i % 2][:, i % 2]
+            x_sorted[i] = rotating.tile([P, FEATURE_PASSES, 2, P], F32, name="x_sorted", bufs=2, align_bytes=64)[:]
             copy(out=x_sorted[i], in_=x_rows[i][:].bitcast(F32).rearrange("r (g p u) -> r g u p", u=2, p=P))
 
         def x_leave(i):
@@ -209,15 +216,6 @@ def tile_mora_repeated_update_s12_kernel(
                 in_=comp_grouped[g][:, first : first + count].rearrange("p t hq e v -> p (t hq e v)"),
             )
 
-        def spread_copy_gain():
-            words = copy_gain_runs[:].bitcast(F32)
-            target = copy_gain_sb[:].rearrange("p c n -> p (c n)").bitcast(F32).rearrange("p (n m) -> p n m", n=P)
-            for first in range(0, SPREAD // 2, 4):
-                bank = psum.tile([P, 4, P], F32, name="direct_ps", bufs=DIRECT_BANKS)
-                for m in range(first, first + 4):
-                    nc.tensor.transpose(bank[:, m - first, :], words[:, m : m + 1].to_broadcast([P, P]), identity[:])
-                nc.scalar.copy(out=target[:, :, first : first + 4], in_=bank[:].rearrange("p m n -> p n m"))
-
         def widen_gains():
             nc.scalar.copy(out=gain_square[:], in_=gain_rows[:])
 
@@ -229,13 +227,19 @@ def tile_mora_repeated_update_s12_kernel(
 
         e_grouped = {}
 
-        def permute_a(h):
-            scale_columns = a_scales_raw[:, :, PASS * h : PASS * (h + 1)]
-            for target, source, ints in ((a_codes[h][:], a_codes_raw[h][:], 4), (a_scales_sb[h][:], scale_columns, 2)):
+        def permute_a_scales(h):
+            for quadrant in range(4):
+                rows = slice(32 * quadrant, 32 * quadrant + SCALE_ROWS)
                 nc.vector.tensor_copy(
-                    out=target.bitcast(I32).rearrange("p g (t q i) -> p g t q i", t=WORD, i=ints),
-                    in_=source.bitcast(I32).rearrange("p g (q t i) -> p g t q i", t=WORD, i=ints),
+                    out=a_scales_sb[h][rows].bitcast(I32).rearrange("p g (t q i) -> p g t q i", t=WORD, i=2),
+                    in_=a_scales_raw[rows, :, PASS * h : PASS * (h + 1)].bitcast(I32).rearrange("p g (q t i) -> p g t q i", t=WORD, i=2),
                 )
+
+        def permute_a(h):
+            nc.vector.tensor_copy(
+                out=a_codes[h][:].bitcast(I32).rearrange("p g (t q i) -> p g t q i", t=WORD, i=4),
+                in_=a_codes_raw[h][:].bitcast(I32).rearrange("p g (q t i) -> p g t q i", t=WORD, i=4),
+            )
 
         def e_matmul(part, b, tag="direct_ps", bufs=DIRECT_BANKS):
             j, h = divmod(part, CHANNEL_PASSES)
@@ -272,10 +276,11 @@ def tile_mora_repeated_update_s12_kernel(
 
         z_rounded, z_grouped, z_mx, z_tile = {}, {}, {}, {}
 
-        def z_matmul(s, h, tag="sums_ps", bufs=SUM_BANKS):
+        def z_matmul(s, h, tag="sums_ps", bufs=SUM_BANKS, banks=range(WORD // 2)):
             codes, scales = x_mx[s]
-            z_rounded[(s, h)] = rotating.tile([P, WORD, PAIR], BF16, name="z_rounded", bufs=2, align_bytes=64)
-            for i in range(WORD // 2):
+            if (s, h) not in z_rounded:
+                z_rounded[(s, h)] = small([P, WORD, PAIR], BF16, "z_rounded")
+            for i in banks:
                 bank = psum.tile([P, 2, PAIR], F32, name=tag, bufs=bufs)
                 for t in (2 * i, 2 * i + 1):
                     for g in range(FEATURE_PASSES):
@@ -349,7 +354,7 @@ def tile_mora_repeated_update_s12_kernel(
 
         def z_leave_bank(i, h):
             if i not in tile_grouped:
-                tile_grouped[i] = rotating.tile([P, CHANNEL_PASSES, P, WORD], BF16, name="z_rounded", bufs=2, align_bytes=64)
+                tile_grouped[i] = small([P, CHANNEL_PASSES, P, WORD], BF16, "tile_grouped")
             nc.vector.tensor_tensor(
                 out=tile_grouped[i][:, h],
                 in0=open_banks[(i % 2, h)][:].rearrange("p t n -> p n t"),
@@ -358,8 +363,8 @@ def tile_mora_repeated_update_s12_kernel(
             )
 
         def z_quantize_tile(i):
-            codes = rotating.tile([P, CHANNEL_PASSES, P], U32, name="z_codes", bufs=5, align_bytes=64)
-            scales = rotating.tile([P, CHANNEL_PASSES, P], U8, name="z_scales", bufs=5, align_bytes=64)
+            codes = rotating.tile([P, CHANNEL_PASSES, P], U32, name="z_codes", bufs=4, align_bytes=64)
+            scales = rotating.tile([P, CHANNEL_PASSES, P], U8, name="z_scales", bufs=4, align_bytes=64)
             nc.vector.quantize_mx(
                 out=codes[:].rearrange("p h r -> p (h r)").bitcast(MXFP8),
                 scales=scales[:].rearrange("p h r -> p (h r)"),
@@ -367,6 +372,11 @@ def tile_mora_repeated_update_s12_kernel(
             )
             for h in range(CHANNEL_PASSES):
                 z_tile[(i, h)] = (codes[:, h], scales[:, h])
+
+        def z_group_pool(s, h):
+            if h == 0:
+                z_grouped[s] = rotating.tile([P, CHANNEL_PASSES, PAIR, WORD], BF16, name="z_grouped", align_bytes=64)
+            pool_copy(out=z_grouped[s][:, h], in_=z_rounded[(s, h)][:].rearrange("p t n -> p n t"))
 
         def z_group(s, h, copy):
             if h == 0:
@@ -380,8 +390,8 @@ def tile_mora_repeated_update_s12_kernel(
 
         def z_quantize(s, first, count):
             if first == 0:
-                z_codes[s] = rotating.tile([P, CHANNEL_PASSES, PAIR], U32, name="z_codes", bufs=5, align_bytes=64)
-                z_scales[s] = rotating.tile([P, CHANNEL_PASSES, PAIR], U8, name="z_scales", bufs=5, align_bytes=64)
+                z_codes[s] = rotating.tile([P, CHANNEL_PASSES, PAIR], U32, name="z_codes", bufs=4, align_bytes=64)
+                z_scales[s] = rotating.tile([P, CHANNEL_PASSES, PAIR], U8, name="z_scales", bufs=4, align_bytes=64)
             passes = slice(first, first + count)
             nc.vector.quantize_mx(
                 out=z_codes[s][:, passes].rearrange("p h r -> p (h r)").bitcast(MXFP8),
@@ -394,7 +404,7 @@ def tile_mora_repeated_update_s12_kernel(
                     tokens = slice(P * place, P * (place + 1))
                     z_tile[(2 * s + place, h)] = (z_codes[s][:, h, tokens], z_scales[s][:, h, tokens])
 
-        y_banks, products = {}, {}
+        y_banks, results = {}, {}
 
         def y_direct(i, j):
             bank = psum.tile([P, HALF], F32, name="direct_ps", bufs=DIRECT_BANKS)
@@ -411,63 +421,51 @@ def tile_mora_repeated_update_s12_kernel(
                 )
             y_banks[(i, j)] = bank
 
+        def result(i):
+            if i not in results:
+                results[i] = rotating.tile(
+                    [P, COPIES, COLUMNS], F32, name="result", tag="comp_then_products", bufs=RESULT_BUFS, align_bytes=64
+                )
+            return results[i]
+
         def multiply(i, j):
             columns = slice(HALF * j, HALF * (j + 1))
-            bank = y_banks[(i, j)]
-            s, place = divmod(i, 2)
-            if (s, j) not in products:
-                products[(s, j)] = rotating.tile(
-                    [P, 2, COPIES, HALF], F32, name="product", tag="comp_then_products", bufs=4, align_bytes=64
-                )
             nc.vector.tensor_tensor(
-                out=products[(s, j)][:, place],
-                in0=bank[:].unsqueeze(1).to_broadcast([P, COPIES, HALF]),
+                out=result(i)[:, :, columns],
+                in0=y_banks[(i, j)][:].unsqueeze(1).to_broadcast([P, COPIES, HALF]),
                 in1=copy_gain_sb[:, :, columns],
                 op=MULT,
             )
 
-        def add_base(i, j, engine):
-            s, place = divmod(i, 2)
+        def add_base(engine, i, c, first, count):
+            columns = slice(HALF * first, HALF * (first + count))
+            part = results[i][:, c, columns]
+            engine.tensor_tensor(out=part, in0=part, in1=base_rows[i][:, c, columns], op=ADD)
+
+        def add_half(i, j):
             columns = slice(HALF * j, HALF * (j + 1))
-            product = products[(s, j)][:, place]
-            if engine is nc.vector:
-                engine.tensor_tensor(out=product, in0=product, in1=base_rows[i][:, :, columns], op=ADD)
-            else:
-                for c in range(COPIES):
-                    for first in range(0, HALF, POOL_WIDTH):
-                        part = product[:, c, first : first + POOL_WIDTH]
-                        start = HALF * j + first
-                        engine.tensor_tensor(out=part, in0=part, in1=base_rows[i][:, c, start : start + POOL_WIDTH], op=ADD)
+            part = results[i][:, :, columns]
+            nc.vector.tensor_tensor(out=part, in0=part, in1=base_rows[i][:, :, columns], op=ADD)
 
-        def add_pair(s, j):
-            product = products[(s, j)][:]
-            nc.vector.tensor_tensor(out=product, in0=product, in1=base_pairs[s][:, :, :, HALF * j : HALF * (j + 1)], op=ADD)
-            store(2 * s, j)
-            store(2 * s + 1, j)
-
-        def add_copy(i, j, c, engine):
-            s, place = divmod(i, 2)
-            part = products[(s, j)][:, place, c, :]
-            engine.tensor_tensor(out=part, in0=part, in1=base_rows[i][:, c, HALF * j : HALF * (j + 1)], op=ADD)
-
-        def store(i, j):
-            s, place = divmod(i, 2)
+        def store(i, c, first=0, count=2):
+            columns = slice(HALF * first, HALF * (first + count))
             rows = out[P * i : P * (i + 1), :].rearrange("p (c n) -> p c n", c=COPIES)
-            nc.sync.dma_start(out=rows[:, :, HALF * j : HALF * (j + 1)], in_=products[(s, j)][:, place])
+            nc.sync.dma_start(out=rows[:, c, columns], in_=results[i][:, c, columns])
+
+        def store_half(i, j):
+            columns = slice(HALF * j, HALF * (j + 1))
+            rows = out[P * i : P * (i + 1), :].rearrange("p (c n) -> p c n", c=COPIES)
+            nc.sync.dma_start(out=rows[:, :, columns], in_=results[i][:, :, columns])
 
         turned_products = {}
 
         turned_banks = {}
 
-        def y_transposed(s, j):
-            y_transposed_mm(s, j)
-            turned_out(s, j)
-
-        def y_transposed_mm(s, j, blocks=range(BLOCKS)):
+        def y_transposed_mm(s, j, tag="direct_ps", bufs=DIRECT_BANKS, blocks=range(BLOCKS)):
             banks = turned_banks.setdefault((s, j), [])
             for b in blocks:
                 if b % 2 == 0:
-                    banks.append(psum.tile([P, 2, PAIR], F32, name="direct_ps", bufs=DIRECT_BANKS))
+                    banks.append(psum.tile([P, 2, PAIR], F32, name=tag, bufs=bufs))
                 columns = slice(P * b, P * (b + 1))
                 for h in range(CHANNEL_PASSES):
                     codes, scales = z_mx[(s, h)]
@@ -481,19 +479,18 @@ def tile_mora_repeated_update_s12_kernel(
                         stop=(h == CHANNEL_PASSES - 1),
                     )
 
-        def turned_out(s, j):
+        def turned_out(s, j, c):
             banks = turned_banks[(s, j)]
-            turned = rotating.tile([P, COPIES, BLOCKS, PAIR], F32, name="turned", tag="eight_kib", bufs=3, align_bytes=64)
-            for c in range(COPIES):
-                for b in range(BLOCKS):
-                    column = WORD + c * (COLUMNS // P) + BLOCKS * j + b
-                    nc.scalar.activation(
-                        out=turned[:, c, b, :],
-                        in_=banks[b // 2][:, b % 2, :],
-                        func=COPY,
-                        scale=gain_columns[:, 0, column : column + 1],
-                    )
-            turned_products[(s, j)] = turned
+            turned = rotating.tile([P, BLOCKS, PAIR], F32, name="turned", tag="rows", bufs=ROW_BUFS, align_bytes=64)
+            for b in range(BLOCKS):
+                column = WORD + c * (COLUMNS // P) + BLOCKS * j + b
+                nc.scalar.activation(
+                    out=turned[:, b, :],
+                    in_=banks[b // 2][:, b % 2, :],
+                    func=COPY,
+                    scale=gain_columns[:, 0, column : column + 1],
+                )
+            turned_products[(s, j, c)] = turned
 
         back_banks, totals = {}, {}
 
@@ -502,32 +499,28 @@ def tile_mora_repeated_update_s12_kernel(
             bank = psum.tile([P, BLOCKS, P], F32, name=tag, bufs=bufs)
             for b in range(BLOCKS):
                 nc.tensor.transpose(
-                    bank[:, b, :], turned_products[(s, j)][:, c, b, P * place : P * (place + 1)], identity[:]
+                    bank[:, b, :], turned_products[(s, j, c)][:, b, P * place : P * (place + 1)], identity[:]
                 )
             back_banks[(i, j, c)] = bank
 
         def add_turned(i, j, c):
-            bank = back_banks[(i, j, c)]
-            s, place = divmod(i, 2)
-            if (s, j) not in totals:
-                totals[(s, j)] = rotating.tile(
-                    [P, 2, COPIES, HALF], F32, name="total", tag="e_then_sums", bufs=E_BUFS, align_bytes=64
-                )
-            total = totals[(s, j)][:, place, c, :]
+            columns = slice(HALF * j, HALF * (j + 1))
             nc.vector.tensor_tensor(
-                out=total,
-                in0=bank[:].rearrange("p b n -> p (b n)"),
-                in1=base_rows[i][:, c, HALF * j : HALF * (j + 1)],
+                out=result(i)[:, c, columns],
+                in0=back_banks[(i, j, c)][:].rearrange("p b n -> p (b n)"),
+                in1=base_rows[i][:, c, columns],
                 op=ADD,
             )
-            first = COLUMNS * c + HALF * j
-            nc.sync.dma_start(out=out[P * i : P * (i + 1), first : first + HALF], in_=total)
 
+        def pool_copy(out, in_):
+            nc.gpsimd.tensor_scalar(out=out, in0=in_, scalar1=1.0, scalar2=0.0, op0=MULT, op1=ADD)
+
+
+        fill_tiles()
         V, S = nc.vector.tensor_copy, nc.scalar.copy
-        VE = nc.vector
-        load_copy_gain()
-        load_codes(a_codes_raw, a_words, 0)
+        VE, G = nc.vector, nc.gpsimd
         load_scales(a_scales_raw, a_scales)
+        load_codes(a_codes_raw, a_words, 0)
         load_codes(d_codes, d_words, 0)
         load_scales(d_scales_sb, d_scales)
         load_codes(a_codes_raw, a_words, 1)
@@ -540,126 +533,149 @@ def tile_mora_repeated_update_s12_kernel(
         load_x(1)
         load_comp(2)
         load_comp(3)
-        load_x(2)
-        load_x(3)
-        load_x(4)
-        load_x(5)
-        load_x(6)
-        load_x(7)
-        load_base(0)
-        load_base(1)
-        load_base(2)
+        for i in range(2, 8):
+            load_x(i)
+        load_copy_gain()
+        for i in range(8):
+            load_base(i)
 
-        spread_copy_gain()
+        permute_a_scales(0)
         permute_a(0)
+        permute_a_scales(1)
         e_part(0)
         permute_a(1)
         comp_group_half(0)
+        e_part(1)
         comp_group_half(1)
         comp_quantize_half(0)
         comp_quantize_half(1)
-        e_part(1)
         e_part(2)
+        comp_group(1, 0, 4, V)
         x_transpose(0)
+        x_transpose(1, "sums_ps", SUM_BANKS)
         widen_gains()
         e_matmul(3, 0)
-        x_transpose(1)
         e_matmul(3, 1)
         turn_gains()
         e_matmul(3, 2)
         e_matmul(3, 3)
-        comp_group(1, 0, 4, V)
         e_quantize(0)
         comp_quantize(1, 0, 4)
-        comp_group(2, 0, 1, V)
         x_quantize(0)
-        comp_group(2, 1, 3, V)
+        comp_group(2, 0, 4, V)
         comp_group(3, 1, 3, S)
         comp_group(3, 0, 1, V)
         comp_quantize(2, 0, 4)
         e_quantize(1)
-        x_sort(4, V)
         comp_quantize(3, 0, 4)
         z_pass(0, 0)
         z_pass(0, 1)
         x_transpose(2)
         x_transpose(3, "sums_ps", SUM_BANKS)
+        x_sort(4, V)
         x_sort(5, S)
         z_pass(0, 2)
-        x_transpose(4)
         z_pass(0, 3)
-        x_transpose(5)
-        x_sort(6, S)
+        x_transpose(4)
         x_quantize(1)
         for i in range(2):
             z_leave_bank(i, 0)
             z_leave_bank(i, 1)
         z_quantize_tile(0)
         z_quantize_tile(1)
-        z_matmul(1, 0)
+
+        x_transpose(5, "sums_ps", SUM_BANKS)
+        z_matmul(1, 0, "turned_ps", TURN_BANKS)
+        x_sort(6, S)
         x_quantize(2)
+        z_group_pool(1, 0)
         y_direct(0, 0)
-        y_direct(0, 1)
         y_direct(1, 0)
+        y_direct(0, 1)
         y_direct(1, 1)
-        G = nc.gpsimd
-        def finish(s, j):
-            for c in range(2):
-                turn_back(2 * s, j, c)
-                add_turned(2 * s, j, c)
-                turn_back(2 * s + 1, j, c, "sums_ps", SUM_BANKS)
-                add_turned(2 * s + 1, j, c)
         def multiply_pair(s):
             i = 2 * s
             multiply(i, 0)
-            add_copy(i, 0, 0, G)
-            add_copy(i, 0, 1, G)
-            store(i, 0)
-            multiply(i, 1)
+            add_base(G, i, 0, 0, 1)
+            add_base(G, i, 1, 0, 1)
+            store_half(i, 0)
             multiply(i + 1, 0)
+            multiply(i, 1)
             multiply(i + 1, 1)
+        def turned(s, j):
+            y_transposed_mm(s, j)
+            turned_out(s, j, 0)
+            turned_out(s, j, 1)
         multiply_pair(0)
-        z_group(1, 0, S)
         x_sort(7, S)
         z_matmul(1, 1)
-        add_base(1, 0, VE)
-        store(1, 0)
-        add_base(0, 1, VE)
-        store(0, 1)
+        add_half(1, 0)
+        store_half(1, 0)
+        add_half(0, 1)
+        store_half(0, 1)
         z_group(1, 1, S)
         x_transpose(6)
         x_transpose(7, "sums_ps", SUM_BANKS)
         z_matmul(2, 0, "direct_ps", DIRECT_BANKS)
         z_quantize(1, 0, 2)
-        add_base(1, 1, VE)
-        store(1, 1)
-        load_base(3)
+        add_half(1, 1)
+        store_half(1, 1)
         x_quantize(3)
         y_direct(2, 0)
-        y_direct(2, 1)
-        z_group(2, 0, S)
-        z_matmul(2, 1)
         y_direct(3, 0)
+        z_group_pool(2, 0)
+        z_matmul(2, 1)
+        y_direct(2, 1)
         y_direct(3, 1)
         multiply_pair(1)
         z_group(2, 1, S)
         z_matmul(3, 0, "direct_ps", DIRECT_BANKS)
-        add_base(3, 0, VE)
-        store(3, 0)
+        TU, SU, DI = ("turned_ps", TURN_BANKS), ("sums_ps", SUM_BANKS), ("direct_ps", DIRECT_BANKS)
+        def back(s, j, c, tags):
+            for i, tag in zip((2 * s, 2 * s + 1), tags):
+                turn_back(i, j, c, *tag)
+        def tadd(s, j, c):
+            for i in (2 * s, 2 * s + 1):
+                add_turned(i, j, c)
+                store(i, c, j, 1)
         z_quantize(2, 0, 2)
-        add_base(2, 1, VE)
-        store(2, 1)
+        add_half(3, 0)
+        store_half(3, 0)
+        add_half(2, 1)
+        store_half(2, 1)
         z_group(3, 0, S)
-        z_matmul(3, 1)
-        y_transposed(2, 0)
-        y_transposed(2, 1)
-        add_base(3, 1, VE)
-        store(3, 1)
-        z_group(3, 1, V)
+        z_narrow(6, 1)
+        y_transposed_mm(2, 0, *TU)
+        turned_out(2, 0, 0)
+        turned_out(2, 0, 1)
+        z_narrow(7, 1)
+        y_transposed_mm(2, 1)
+        turned_out(2, 1, 0)
+        turned_out(2, 1, 1)
+        add_half(3, 1)
+        store_half(3, 1)
+        z_leave_narrow(6, 1)
+        z_leave_narrow(7, 1)
         z_quantize(3, 0, 2)
-        finish(2, 0)
-        y_transposed(3, 0)
-        finish(2, 1)
-        y_transposed(3, 1)
-        finish(3, 0)
-        finish(3, 1)
+        back(2, 0, 0, (DI, DI))
+        back(2, 0, 1, (TU, TU))
+        tadd(2, 0, 0)
+        tadd(2, 0, 1)
+        y_transposed_mm(3, 0, *SU)
+        turned_out(3, 0, 0)
+        turned_out(3, 0, 1)
+        back(2, 1, 0, (DI, DI))
+        back(2, 1, 1, (TU, TU))
+        tadd(2, 1, 0)
+        tadd(2, 1, 1)
+        y_transposed_mm(3, 1)
+        turned_out(3, 1, 0)
+        turned_out(3, 1, 1)
+        back(3, 0, 0, (DI, DI))
+        back(3, 0, 1, (TU, TU))
+        tadd(3, 0, 0)
+        tadd(3, 0, 1)
+        back(3, 1, 0, (SU, SU))
+        back(3, 1, 1, (DI, DI))
+        tadd(3, 1, 0)
+        tadd(3, 1, 1)

@@ -81,6 +81,21 @@ def tile_mora_repeated_update_s12_kernel(
                 channel_multiplier=1,
             )
 
+        def warm_up(count):
+            zeros = resident.tile([P, P], BF16, name="warm_zeros", align_bytes=64)
+            codes = resident.tile([P, HALF], U32, name="warm_codes", align_bytes=64)
+            scales = resident.tile([P, HALF], U8, name="warm_scales", align_bytes=64)
+            nc.vector.memset(zeros[:], 0.0)
+            nc.vector.memset(codes[:], 0)
+            nc.vector.memset(scales[:].bitcast(I32), 0)
+            nc.vector.quantize_mx(out=codes[:, 0 : P // WORD].bitcast(MXFP8), scales=scales[:, 0 : P // WORD], in_=zeros[:])
+            bank = psum.tile([P, HALF], F32, name="sums_ps", bufs=SUM_BANKS)
+            for k in range(count):
+                nc.tensor.matmul_mx(
+                    out=bank[:], lhsT=codes[:, 0:P].bitcast(MXFP8), lhsT_scale=scales[:, 0:P],
+                    rhs=codes[:].bitcast(MXFP8), rhs_scale=scales[:], start=True, stop=True,
+                )
+
         x_rows, comp_rows, base_rows, base_pairs = {}, {}, {}, {}
 
         def load_x(i):
@@ -516,6 +531,7 @@ def tile_mora_repeated_update_s12_kernel(
             nc.gpsimd.tensor_scalar(out=out, in0=in_, scalar1=1.0, scalar2=0.0, op0=MULT, op1=ADD)
 
 
+        warm_up(5)
         fill_tiles()
         V, S = nc.vector.tensor_copy, nc.scalar.copy
         VE, G = nc.vector, nc.gpsimd

@@ -567,28 +567,29 @@ def tile_mora_repeated_update_s12_kernel(
         comp_quantize_half(1)
         e_part(2)
         comp_group(1, 0, 4, V)
+        e_matmul(3, 0)
         x_transpose(0)
         x_transpose(1, "sums_ps", SUM_BANKS)
-        widen_gains()
-        e_matmul(3, 0)
         e_matmul(3, 1)
-        turn_gains()
+        widen_gains()
         e_matmul(3, 2)
         e_matmul(3, 3)
+        turn_gains()
         e_quantize(0)
         comp_quantize(1, 0, 4)
         x_quantize(0)
-        comp_group(2, 0, 4, V)
-        comp_group(3, 1, 3, S)
-        comp_group(3, 0, 1, V)
+        comp_group(2, 0, 3, V)
+        comp_group(2, 3, 1, S)
+        comp_group(3, 2, 2, S)
+        comp_group(3, 0, 2, V)
         comp_quantize(2, 0, 4)
-        e_quantize(1)
         comp_quantize(3, 0, 4)
+        e_quantize(1)
         z_pass(0, 0)
         z_pass(0, 1)
         x_transpose(2)
         x_transpose(3, "sums_ps", SUM_BANKS)
-        x_sort(4, V)
+        x_sort(4, S)
         x_sort(5, S)
         z_pass(0, 2)
         z_pass(0, 3)

@@ -31,6 +31,7 @@ GAIN_ROWS = WORD + COPIES * (COLUMNS // P)
 ROW_BUFS, E_BUFS, SMALL_BUFS = 10, 2, 9
 SUM_BANKS, TURN_BANKS, DIRECT_BANKS = 2, 2, 4
 RESULT_BUFS = 5
+POOL_COLUMNS = 320
 TURNED_BUFS = 3
 
 
@@ -452,25 +453,14 @@ def tile_mora_repeated_update_s12_kernel(
                 op=MULT,
             )
 
-        def add_base(engine, i, c, first, count):
-            columns = slice(HALF * first, HALF * (first + count))
-            part = results[i][:, c, columns]
-            engine.tensor_tensor(out=part, in0=part, in1=base_rows[i][:, c, columns], op=ADD)
-
-        def add_half(i, j):
-            columns = slice(HALF * j, HALF * (j + 1))
-            part = results[i][:, :, columns]
-            nc.vector.tensor_tensor(out=part, in0=part, in1=base_rows[i][:, :, columns], op=ADD)
+        def add_base(engine, i, c, first, last):
+            part = results[i][:, c, first:last]
+            engine.tensor_tensor(out=part, in0=part, in1=base_rows[i][:, c, first:last], op=ADD)
 
         def store(i, c, first=0, count=2):
             columns = slice(HALF * first, HALF * (first + count))
             rows = out[P * i : P * (i + 1), :].rearrange("p (c n) -> p c n", c=COPIES)
             nc.sync.dma_start(out=rows[:, c, columns], in_=results[i][:, c, columns])
-
-        def store_half(i, j):
-            columns = slice(HALF * j, HALF * (j + 1))
-            rows = out[P * i : P * (i + 1), :].rearrange("p (c n) -> p c n", c=COPIES)
-            nc.sync.dma_start(out=rows[:, :, columns], in_=results[i][:, :, columns])
 
         turned_products = {}
 
@@ -584,12 +574,12 @@ def tile_mora_repeated_update_s12_kernel(
         comp_group(3, 0, 2, V)
         comp_quantize(2, 0, 4)
         comp_quantize(3, 0, 4)
+        x_sort(4, V)
         e_quantize(1)
         z_pass(0, 0)
         z_pass(0, 1)
         x_transpose(2)
         x_transpose(3, "sums_ps", SUM_BANKS)
-        x_sort(4, S)
         x_sort(5, S)
         z_pass(0, 2)
         z_pass(0, 3)
@@ -613,9 +603,8 @@ def tile_mora_repeated_update_s12_kernel(
         def multiply_pair(s):
             i = 2 * s
             multiply(i, 0)
-            add_base(G, i, 0, 0, 1)
-            add_base(G, i, 1, 0, 1)
-            store_half(i, 0)
+            add_base(G, i, 0, 0, HALF)
+            add_base(G, i, 1, 0, POOL_COLUMNS)
             multiply(i + 1, 0)
             multiply(i, 1)
             multiply(i + 1, 1)
@@ -626,17 +615,19 @@ def tile_mora_repeated_update_s12_kernel(
         multiply_pair(0)
         x_sort(7, S)
         z_matmul(1, 1)
-        add_half(1, 0)
-        store_half(1, 0)
-        add_half(0, 1)
-        store_half(0, 1)
+        add_base(VE, 0, 0, HALF, COLUMNS)
+        store(0, 0)
+        add_base(VE, 1, 0, 0, COLUMNS)
+        store(1, 0)
         z_group(1, 1, S)
         x_transpose(6)
         x_transpose(7, "sums_ps", SUM_BANKS)
         z_matmul(2, 0, "direct_ps", DIRECT_BANKS)
         z_quantize(1, 0, 2)
-        add_half(1, 1)
-        store_half(1, 1)
+        add_base(VE, 0, 1, POOL_COLUMNS, COLUMNS)
+        store(0, 1)
+        add_base(VE, 1, 1, 0, COLUMNS)
+        store(1, 1)
         x_quantize(3)
         y_direct(2, 0)
         y_direct(3, 0)
@@ -656,10 +647,12 @@ def tile_mora_repeated_update_s12_kernel(
                 add_turned(i, j, c)
                 store(i, c, j, 1)
         z_quantize(2, 0, 2)
-        add_half(3, 0)
-        store_half(3, 0)
-        add_half(2, 1)
-        store_half(2, 1)
+        add_base(VE, 3, 0, 0, COLUMNS)
+        store(3, 0)
+        add_base(VE, 2, 0, HALF, COLUMNS)
+        store(2, 0)
+        add_base(VE, 2, 1, POOL_COLUMNS, COLUMNS)
+        store(2, 1)
         z_group(3, 0, S)
         z_narrow(6, 1)
         y_transposed_mm(2, 0, *TU)
@@ -669,10 +662,11 @@ def tile_mora_repeated_update_s12_kernel(
         y_transposed_mm(2, 1)
         turned_out(2, 1, 0)
         turned_out(2, 1, 1)
-        add_half(3, 1)
-        store_half(3, 1)
+        add_base(VE, 3, 1, 0, HALF)
         z_leave_narrow(6, 1)
         z_leave_narrow(7, 1)
+        add_base(VE, 3, 1, HALF, COLUMNS)
+        store(3, 1)
         z_quantize(3, 0, 2)
         back(2, 0, 0, (DI, DI))
         back(2, 0, 1, (TU, TU))

@@ -30,9 +30,9 @@ SCALE_ROWS = 4
 GAIN_ROWS = WORD + COPIES * (COLUMNS // P)
 ROW_BUFS, E_BUFS, SMALL_BUFS = 10, 2, 9
 SUM_BANKS, TURN_BANKS, DIRECT_BANKS = 2, 2, 4
+WARM_PASSES = 4
 RESULT_BUFS = 5
 POOL_COLUMNS = 320
-TURNED_BUFS = 3
 
 
 def tile_mora_repeated_update_s12_kernel(
@@ -82,19 +82,27 @@ def tile_mora_repeated_update_s12_kernel(
                 channel_multiplier=1,
             )
 
-        def warm_up(count):
-            zeros = resident.tile([P, P], BF16, name="warm_zeros", align_bytes=64)
-            codes = resident.tile([P, HALF], U32, name="warm_codes", align_bytes=64)
-            scales = resident.tile([P, HALF], U8, name="warm_scales", align_bytes=64)
-            nc.vector.memset(zeros[:], 0.0)
-            nc.vector.memset(codes[:], 0)
-            nc.vector.memset(scales[:].bitcast(I32), 0)
-            nc.vector.quantize_mx(out=codes[:, 0 : P // WORD].bitcast(MXFP8), scales=scales[:, 0 : P // WORD], in_=zeros[:])
+        zeros = resident.tile([P, P], BF16, name="warm_zeros", align_bytes=64)
+        warm_codes = resident.tile([P, HALF], U32, name="warm_codes", align_bytes=64)
+        warm_scales = resident.tile([P, HALF], U8, name="warm_scales", align_bytes=64)
+        nc.vector.memset(zeros[:], 0.0)
+        nc.vector.memset(warm_codes[:], 0)
+        nc.vector.memset(warm_scales[:].bitcast(I32), 0)
+
+        def warm_up():
+            nc.vector.quantize_mx(
+                out=warm_codes[:, 0 : P // WORD].bitcast(MXFP8), scales=warm_scales[:, 0 : P // WORD], in_=zeros[:]
+            )
             bank = psum.tile([P, HALF], F32, name="sums_ps", bufs=SUM_BANKS)
-            for k in range(count):
+            for _ in range(WARM_PASSES):
                 nc.tensor.matmul_mx(
-                    out=bank[:], lhsT=codes[:, 0:P].bitcast(MXFP8), lhsT_scale=scales[:, 0:P],
-                    rhs=codes[:].bitcast(MXFP8), rhs_scale=scales[:], start=True, stop=True,
+                    out=bank[:],
+                    lhsT=warm_codes[:, 0:P].bitcast(MXFP8),
+                    lhsT_scale=warm_scales[:, 0:P],
+                    rhs=warm_codes[:].bitcast(MXFP8),
+                    rhs_scale=warm_scales[:],
+                    start=True,
+                    stop=True,
                 )
 
         x_rows, comp_rows, base_rows, base_pairs = {}, {}, {}, {}
@@ -243,8 +251,8 @@ def tile_mora_repeated_update_s12_kernel(
 
         e_grouped = {}
 
-        def permute_a_scales(h):
-            for quadrant in range(4):
+        def permute_a_scales(h, quadrants=range(4)):
+            for quadrant in quadrants:
                 rows = slice(32 * quadrant, 32 * quadrant + SCALE_ROWS)
                 nc.vector.tensor_copy(
                     out=a_scales_sb[h][rows].bitcast(I32).rearrange("p g (t q i) -> p g t q i", t=WORD, i=2),
@@ -457,6 +465,15 @@ def tile_mora_repeated_update_s12_kernel(
             part = results[i][:, c, first:last]
             engine.tensor_tensor(out=part, in0=part, in1=base_rows[i][:, c, first:last], op=ADD)
 
+        def add_aside(i, c, first, last, target):
+            nc.gpsimd.tensor_tensor(out=target, in0=results[i][:, c, first:last], in1=base_rows[i][:, c, first:last], op=ADD)
+
+        def store_aside(i, c, first, last, target):
+            nc.sync.dma_start(out=out[P * i : P * (i + 1), COLUMNS * c + first : COLUMNS * c + last], in_=target)
+
+        def store_columns(i, c, first, last):
+            store_aside(i, c, first, last, results[i][:, c, first:last])
+
         def store(i, c, first=0, count=2):
             columns = slice(HALF * first, HALF * (first + count))
             rows = out[P * i : P * (i + 1), :].rearrange("p (c n) -> p c n", c=COPIES)
@@ -521,7 +538,6 @@ def tile_mora_repeated_update_s12_kernel(
             nc.gpsimd.tensor_scalar(out=out, in0=in_, scalar1=1.0, scalar2=0.0, op0=MULT, op1=ADD)
 
 
-        warm_up(5)
         fill_tiles()
         V, S = nc.vector.tensor_copy, nc.scalar.copy
         VE, G = nc.vector, nc.gpsimd
@@ -545,7 +561,9 @@ def tile_mora_repeated_update_s12_kernel(
         for i in range(8):
             load_base(i)
 
-        permute_a_scales(0)
+        permute_a_scales(0, range(1))
+        warm_up()
+        permute_a_scales(0, range(1, 4))
         permute_a(0)
         permute_a_scales(1)
         e_part(0)
@@ -626,12 +644,15 @@ def tile_mora_repeated_update_s12_kernel(
         z_quantize(1, 0, 2)
         add_base(VE, 0, 1, POOL_COLUMNS, COLUMNS)
         store(0, 1)
-        add_base(VE, 1, 1, 0, COLUMNS)
-        store(1, 1)
+        add_base(VE, 1, 1, 0, HALF)
+        store_columns(1, 1, 0, HALF)
         x_quantize(3)
+        aside = x_grouped[3][:, 0].rearrange("p n t -> p (n t)").bitcast(F32)
+        add_aside(1, 1, HALF, COLUMNS, aside)
+        store_aside(1, 1, HALF, COLUMNS, aside)
         y_direct(2, 0)
         y_direct(3, 0)
-        z_group_pool(2, 0)
+        z_group(2, 0, S)
         z_matmul(2, 1)
         y_direct(2, 1)
         y_direct(3, 1)

@@ -555,10 +555,13 @@ def tile_mora_repeated_update_s12_kernel(
         load_x(1)
         load_comp(2)
         load_comp(3)
-        for i in range(2, 8):
+        for i in range(2, 6):
             load_x(i)
         load_copy_gain()
-        for i in range(8):
+        load_x(6)
+        load_base(0)
+        load_x(7)
+        for i in range(1, 8):
             load_base(i)
 
         permute_a_scales(0, range(1))
@@ -639,8 +642,8 @@ def tile_mora_repeated_update_s12_kernel(
         store(1, 0)
         z_group(1, 1, S)
         x_transpose(6)
-        x_transpose(7, "sums_ps", SUM_BANKS)
-        z_matmul(2, 0, "direct_ps", DIRECT_BANKS)
+        x_transpose(7, "direct_ps", DIRECT_BANKS)
+        z_matmul(2, 0)
         z_quantize(1, 0, 2)
         add_base(VE, 0, 1, POOL_COLUMNS, COLUMNS)
         store(0, 1)
@@ -653,10 +656,12 @@ def tile_mora_repeated_update_s12_kernel(
         y_direct(2, 0)
         y_direct(3, 0)
         z_group(2, 0, S)
-        z_matmul(2, 1)
+        z_matmul(2, 1, "turned_ps", TURN_BANKS)
         y_direct(2, 1)
         y_direct(3, 1)
         multiply_pair(1)
+        store_columns(2, 0, 0, HALF)
+        store_columns(2, 1, 0, POOL_COLUMNS)
         z_group(2, 1, S)
         z_matmul(3, 0, "direct_ps", DIRECT_BANKS)
         TU, SU, DI = ("turned_ps", TURN_BANKS), ("sums_ps", SUM_BANKS), ("direct_ps", DIRECT_BANKS)
@@ -668,12 +673,12 @@ def tile_mora_repeated_update_s12_kernel(
                 add_turned(i, j, c)
                 store(i, c, j, 1)
         z_quantize(2, 0, 2)
+        add_base(VE, 2, 0, HALF, COLUMNS)
+        store_columns(2, 0, HALF, COLUMNS)
         add_base(VE, 3, 0, 0, COLUMNS)
         store(3, 0)
-        add_base(VE, 2, 0, HALF, COLUMNS)
-        store(2, 0)
         add_base(VE, 2, 1, POOL_COLUMNS, COLUMNS)
-        store(2, 1)
+        store_columns(2, 1, POOL_COLUMNS, COLUMNS)
         z_group(3, 0, S)
         z_narrow(6, 1)
         y_transposed_mm(2, 0, *TU)
@@ -684,10 +689,11 @@ def tile_mora_repeated_update_s12_kernel(
         turned_out(2, 1, 0)
         turned_out(2, 1, 1)
         add_base(VE, 3, 1, 0, HALF)
+        store_columns(3, 1, 0, HALF)
         z_leave_narrow(6, 1)
         z_leave_narrow(7, 1)
         add_base(VE, 3, 1, HALF, COLUMNS)
-        store(3, 1)
+        store_columns(3, 1, HALF, COLUMNS)
         z_quantize(3, 0, 2)
         back(2, 0, 0, (DI, DI))
         back(2, 0, 1, (TU, TU))

from contextlib import ExitStack

import concourse.mybir as mybir

F32 = mybir.dt.float32
BF16 = mybir.dt.bfloat16
I32 = mybir.dt.int32
U32 = mybir.dt.uint32
U8 = mybir.dt.uint8
MXFP8 = mybir.dt.float8_e4m3fn_x4
MXFP4 = mybir.dt.float4_e2m1fn_x4
ADD = mybir.AluOpType.add
MULT = mybir.AluOpType.mult
COPY = mybir.ActivationFunctionType.Copy

TOKENS, FEATURES, CHANNELS, COLUMNS, COPIES = 1024, 2048, 1024, 1024, 2
FLOPS = 2 * TOKENS * FEATURES * CHANNELS + 2 * CHANNELS * CHANNELS * COLUMNS + 2 * TOKENS * CHANNELS * COLUMNS

P = 128
WORD = 4
PASS = P * WORD
FEATURE_PASSES = FEATURES // PASS
CHANNEL_PASSES = CHANNELS // PASS
RUN = 8
PAIR = 2 * P
WORDS = PASS // 2
HALF = 512
BLOCKS = HALF // P
SCALE_ROWS = 4
GAIN_ROWS = WORD + COPIES * (COLUMNS // P)
ROW_BUFS, E_BUFS, SMALL_BUFS = 10, 2, 9
SUM_BANKS, TURN_BANKS, DIRECT_BANKS = 2, 2, 4
WARM_PASSES = 4
RESULT_BUFS = 5
POOL_COLUMNS = 320


def tile_mora_repeated_update_s12_kernel(
    tc, x, comp, gain, a_words, a_scales, d_words, d_scales, copy_gain, base, out
):
    nc = tc.nc
    with ExitStack() as ctx:
        resident = ctx.enter_context(tc.tile_pool(name="resident", bufs=1))
        rotating = ctx.enter_context(tc.tile_pool(name="rotating", bufs=2))
        psum = ctx.enter_context(tc.psum_pool(name="psum", bufs=2))
        ctx.enter_context(tc.manual_schedule())

        halves = range(2)
        def small(shape, dtype, name):
            return rotating.tile(shape, dtype, name=name, tag="two_kib", bufs=SMALL_BUFS, align_bytes=64)

        a_codes_raw = [small([P, CHANNEL_PASSES, 2 * PASS], U8, "a_codes_raw") for h in halves]
        a_codes = [small([P, CHANNEL_PASSES, 2 * PASS], U8, "a_codes") for h in halves]
        d_codes = [small([P, CHANNEL_PASSES, 2 * HALF], U8, "d_codes") for j in halves]
        a_scales_raw = small([P, CHANNEL_PASSES, CHANNELS], U8, "a_scales_raw")
        a_scales_sb = [resident.tile([P, CHANNEL_PASSES, PASS], U8, name="a_scales_sb%d" % h, align_bytes=64) for h in halves]
        d_scales_sb = small([P, CHANNEL_PASSES, COLUMNS], U8, "d_scales_sb")
        comp_codes = resident.tile([P, FEATURE_PASSES, CHANNELS], U32, name="comp_codes", align_bytes=64)
        comp_scales = resident.tile([P, FEATURE_PASSES, CHANNELS], U8, name="comp_scales", align_bytes=64)
        e_codes = resident.tile([P, 2, CHANNEL_PASSES, HALF], U32, name="e_codes", align_bytes=64)
        e_scales = resident.tile([P, 2, CHANNEL_PASSES, HALF], U8, name="e_scales", align_bytes=64)
        copy_gain_sb = resident.tile([P, COPIES, COLUMNS], BF16, name="copy_gain_sb", align_bytes=64)
        identity = resident.tile([P, P], F32, name="identity", align_bytes=64)
        gain_rows = resident.tile([P, CHANNEL_PASSES, P], BF16, name="gain_rows", align_bytes=64)
        gain_square = resident.tile([P, CHANNEL_PASSES, P], F32, name="gain_square", align_bytes=64)
        gain_columns = resident.tile([P, CHANNEL_PASSES, GAIN_ROWS], F32, name="gain_columns", align_bytes=64)

        nc.vector.memset(d_scales_sb[:].rearrange("p g n -> p (g n)").bitcast(I32), 0)

        def fill_tiles():
            for h in halves:
                nc.vector.memset(a_scales_sb[h][:].rearrange("p g n -> p (g n)").bitcast(I32), 0)
            nc.vector.memset(gain_rows[:], 0.0)
            nc.vector.memset(identity[:], 0.0)
            nc.gpsimd.affine_select(
                out=identity[:],
                in_=identity[:],
                compare_op=mybir.AluOpType.not_equal,
                fill=1.0,
                base=0,
                pattern=[[-1, P]],
                channel_multiplier=1,
            )

        zeros = resident.tile([P, P], BF16, name="warm_zeros", align_bytes=64)
        warm_codes = resident.tile([P, HALF], U32, name="warm_codes", align_bytes=64)
        warm_scales = resident.tile([P, HALF], U8, name="warm_scales", align_bytes=64)
        nc.vector.memset(zeros[:], 0.0)
        nc.vector.memset(warm_codes[:], 0)
        nc.vector.memset(warm_scales[:].bitcast(I32), 0)

        def warm_up():
            nc.vector.quantize_mx(
                out=warm_codes[:, 0 : P // WORD].bitcast(MXFP8), scales=warm_scales[:, 0 : P // WORD], in_=zeros[:]
            )
            bank = psum.tile([P, HALF], F32, name="sums_ps", bufs=SUM_BANKS)
            for _ in range(WARM_PASSES):
                nc.tensor.matmul_mx(
                    out=bank[:],
                    lhsT=warm_codes[:, 0:P].bitcast(MXFP8),
                    lhsT_scale=warm_scales[:, 0:P],
                    rhs=warm_codes[:].bitcast(MXFP8),
                    rhs_scale=warm_scales[:],
                    start=True,
                    stop=True,
                )

        x_rows, comp_rows, base_rows, base_pairs = {}, {}, {}, {}

        def load_x(i):
            x_rows[i] = rotating.tile([P, FEATURES], BF16, name="x_rows", tag="rows", bufs=ROW_BUFS, align_bytes=64)
            nc.sync.dma_start(out=x_rows[i][:], in_=x[P * i : P * (i + 1), :])

        def load_base(i):
            base_rows[i] = rotating.tile([P, COPIES, COLUMNS], BF16, name="base_rows", tag="rows", bufs=ROW_BUFS, align_bytes=64)
            nc.sync.dma_start(out=base_rows[i][:].rearrange("p c n -> p (c n)"), in_=base[P * i : P * (i + 1), :])

        def load_comp(g):
            comp_rows[g] = rotating.tile(
                [P, WORD, CHANNELS], BF16, name="comp_rows", tag="comp_then_products", bufs=RESULT_BUFS, align_bytes=64
            )
            rows = comp[PASS * g : PASS * (g + 1), :]
            nc.sync.dma_start(out=comp_rows[g][:], in_=rows.rearrange("(p v) r -> p v r", v=WORD))

        half_rows = {}

        def load_comp_half(h):
            half_rows[h] = rotating.tile([P, WORD, PASS], BF16, name="half_rows", tag="rows", bufs=ROW_BUFS, align_bytes=64)
            block = comp[0:PASS, PASS * h : PASS * (h + 1)]
            nc.sync.dma_start(out=half_rows[h][:], in_=block.rearrange("(p v) r -> p v r", v=WORD))

        def load_codes(tiles, words, half):
            columns = words[:, :, 2 * HALF * half : 2 * HALF * (half + 1)]
            nc.sync.dma_start(out=tiles[half][:].bitcast(I32), in_=columns.rearrange("g p n -> p g n").bitcast(I32))

        def load_scales(tile, scales):
            for quadrant in range(4):
                rows = slice(SCALE_ROWS * quadrant, SCALE_ROWS * (quadrant + 1))
                nc.sync.dma_start(
                    out=tile[32 * quadrant : 32 * quadrant + SCALE_ROWS, :, :].bitcast(I32),
                    in_=scales[:, rows, :].rearrange("g r n -> r g n").bitcast(I32),
                )

        def load_gains():
            nc.sync.dma_start(
                out=gain_rows[0:WORD, :, :].rearrange("t h (q e) -> t (h q) e", e=RUN),
                in_=gain.rearrange("(hq t e) -> t hq e", t=WORD, e=RUN),
            )
            nc.sync.dma_start(
                out=gain_rows[WORD:GAIN_ROWS, 0, :], in_=copy_gain.rearrange("c (b p) -> (c b) p", p=P)
            )

        def load_copy_gain():
            nc.sync.dma_start(
                out=copy_gain_sb[:].rearrange("p c n -> p (c n)"),
                in_=copy_gain.rearrange("c n -> (c n)").partition_broadcast(P),
            )

        x_grouped, x_mx, x_banks, x_sorted, sorted_pairs = {}, {}, {}, {}, {}

        def x_transpose(i, tag="turned_ps", bufs=TURN_BANKS, leave=True):
            s, place = divmod(i, 2)
            if place == 0:
                x_grouped[s] = rotating.tile([P, FEATURE_PASSES, PAIR, 2], F32, name="x_grouped", tag="eight_kib", bufs=3, align_bytes=64)
            words = x_rows[i][:].bitcast(F32)
            banks = {}
            for g0 in range(0, FEATURE_PASSES, 2):
                bank = psum.tile([P, 4, P], F32, name=tag, bufs=bufs)
                banks[g0] = bank
                for g in (g0, g0 + 1):
                    for u in range(2):
                        first = WORDS * g + u
                        source = x_sorted[i][:, g, u, :] if i in x_sorted else words[:, first : first + WORDS - 1 : 2]
                        nc.tensor.transpose(bank[:, 2 * (g - g0) + u, :], source, identity[:])
            x_banks[i] = banks
            if leave:
                x_leave(i)

        def x_sort(i, copy):
            x_sorted[i] = rotating.tile([P, FEATURE_PASSES, 2, P], F32, name="x_sorted", bufs=2, align_bytes=64)[:]
            copy(out=x_sorted[i], in_=x_rows[i][:].bitcast(F32).rearrange("r (g p u) -> r g u p", u=2, p=P))

        def x_leave(i):
            s, place = divmod(i, 2)
            banks = x_banks[i]
            for g0 in range(0, FEATURE_PASSES, 2):
                nc.scalar.copy(
                    out=x_grouped[s][:, g0 : g0 + 2, P * place : P * (place + 1), :],
                    in_=banks[g0][:].rearrange("p (g u) r -> p g r u", u=2),
                )

        def x_quantize(s):
            codes = rotating.tile([P, FEATURE_PASSES, PAIR], U32, name="x_codes", bufs=3, align_bytes=64)
            scales = rotating.tile([P, FEATURE_PASSES, PAIR], U8, name="x_scales", bufs=3, align_bytes=64)
            nc.vector.quantize_mx(
                out=codes[:].rearrange("p g r -> p (g r)").bitcast(MXFP8),
                scales=scales[:].rearrange("p g r -> p (g r)"),
                in_=x_grouped[s][:].rearrange("p g r u -> p (g r u)").bitcast(BF16),
            )
            x_mx[s] = (codes, scales)

        comp_grouped = {}

        def first_column(g, h, t):
            return PASS * h + P * t if g == 0 else 2 * P * t + P * h

        def comp_group_half(h):
            if h == 0:
                comp_grouped[0] = rotating.tile(
                    [P, CHANNEL_PASSES, WORD, P // RUN, RUN, WORD], BF16, name="comp_grouped", align_bytes=64
                )
            source = half_rows[h][:].rearrange("p v (q t e i) -> p t q e v i", t=WORD, e=2, i=4)
            target = comp_grouped[0][:, h].rearrange("p t q (e i) v -> p t q e v i", i=4)
            for t in range(WORD):
                nc.vector.tensor_copy(out=target[:, t], in_=source[:, t])

        def comp_quantize_half(h):
            columns = slice(PASS * h, PASS * (h + 1))
            nc.vector.quantize_mx(
                out=comp_codes[:, 0, columns].bitcast(MXFP8),
                scales=comp_scales[:, 0, columns],
                in_=comp_grouped[0][:, h].rearrange("p t q e v -> p (t q e v)"),
            )

        def comp_group(g, first, count, copy):
            if g not in comp_grouped:
                comp_grouped[g] = rotating.tile(
                    [P, WORD, CHANNELS // (WORD * RUN), RUN, WORD], BF16, name="comp_grouped", align_bytes=64
                )
            source = comp_rows[g][:].rearrange("p v (hq t e i) -> p t hq e v i", t=WORD, e=2, i=4)
            target = comp_grouped[g][:].rearrange("p t hq (e i) v -> p t hq e v i", i=4)
            for t in range(first, first + count):
                copy(out=target[:, t], in_=source[:, t])

        def comp_quantize(g, first, count):
            columns = slice(2 * P * first, 2 * P * (first + count))
            nc.vector.quantize_mx(
                out=comp_codes[:, g, columns].bitcast(MXFP8),
                scales=comp_scales[:, g, columns],
                in_=comp_grouped[g][:, first : first + count].rearrange("p t hq e v -> p (t hq e v)"),
            )

        def widen_gains():
            nc.scalar.copy(out=gain_square[:], in_=gain_rows[:])

        def turn_gains():
            bank = psum.tile([P, 4, P], F32, name="sums_ps", bufs=SUM_BANKS)
            for h in range(CHANNEL_PASSES):
                nc.tensor.transpose(bank[:, h, :], gain_square[:, h, :], identity[:])
            nc.scalar.copy(out=gain_columns[:], in_=bank[:, 0:CHANNEL_PASSES, 0:GAIN_ROWS])

        e_grouped = {}

        def permute_a_scales(h, quadrants=range(4)):
            for quadrant in quadrants:
                rows = slice(32 * quadrant, 32 * quadrant + SCALE_ROWS)
                nc.vector.tensor_copy(
                    out=a_scales_sb[h][rows].bitcast(I32).rearrange("p g (t q i) -> p g t q i", t=WORD, i=2),
                    in_=a_scales_raw[rows, :, PASS * h : PASS * (h + 1)].bitcast(I32).rearrange("p g (q t i) -> p g t q i", t=WORD, i=2),
                )

        def permute_a(h):
            nc.vector.tensor_copy(
                out=a_codes[h][:].bitcast(I32).rearrange("p g (t q i) -> p g t q i", t=WORD, i=4),
                in_=a_codes_raw[h][:].bitcast(I32).rearrange("p g (q t i) -> p g t q i", t=WORD, i=4),
            )

        def e_matmul(part, b, tag="direct_ps", bufs=DIRECT_BANKS):
            j, h = divmod(part, CHANNEL_PASSES)
            if b == 0 and h == 0:
                e_grouped[j] = rotating.tile(
                    [P, CHANNEL_PASSES, HALF, WORD], BF16, name="e_grouped", tag="e_then_sums", bufs=E_BUFS, align_bytes=64
                )
            n = P * b
            bank = psum.tile([P, WORD, P], F32, name=tag, bufs=bufs)
            for t in range(WORD):
                m = P * t
                for g in range(CHANNEL_PASSES):
                    nc.tensor.matmul_mx(
                        out=bank[:, t, :],
                        lhsT=a_codes[h][:, g, 2 * m : 2 * (m + P)].bitcast(MXFP4),
                        lhsT_scale=a_scales_sb[h][:, g, m : m + P],
                        rhs=d_codes[j][:, g, 2 * n : 2 * (n + P)].bitcast(MXFP4),
                        rhs_scale=d_scales_sb[:, g, HALF * j + n : HALF * j + n + P],
                        start=(g == 0),
                        stop=(g == CHANNEL_PASSES - 1),
                    )
            nc.scalar.copy(out=e_grouped[j][:, h, n : n + P, :], in_=bank[:].rearrange("p t n -> p n t"))

        def e_part(part):
            for b in range(BLOCKS):
                e_matmul(part, b)

        def e_quantize(j):
            nc.vector.quantize_mx(
                out=e_codes[:, j].rearrange("p h n -> p (h n)").bitcast(MXFP8),
                scales=e_scales[:, j].rearrange("p h n -> p (h n)"),
                in_=e_grouped[j][:].rearrange("p h n t -> p (h n t)"),
            )

        z_rounded, z_grouped, z_mx, z_tile = {}, {}, {}, {}

        def z_matmul(s, h, tag="sums_ps", bufs=SUM_BANKS, banks=range(WORD // 2)):
            codes, scales = x_mx[s]
            if (s, h) not in z_rounded:
                z_rounded[(s, h)] = small([P, WORD, PAIR], BF16, "z_rounded")
            for i in banks:
                bank = psum.tile([P, 2, PAIR], F32, name=tag, bufs=bufs)
                for t in (2 * i, 2 * i + 1):
                    for g in range(FEATURE_PASSES):
                        m = first_column(g, h, t)
                        nc.tensor.matmul_mx(
                            out=bank[:, t - 2 * i, :],
                            lhsT=comp_codes[:, g, m : m + P].bitcast(MXFP8),
                            lhsT_scale=comp_scales[:, g, m : m + P],
                            rhs=codes[:, g, :].bitcast(MXFP8),
                            rhs_scale=scales[:, g, :],
                            start=(g == 0),
                            stop=(g == FEATURE_PASSES - 1),
                        )
                for t in (2 * i, 2 * i + 1):
                    nc.scalar.activation(
                        out=z_rounded[(s, h)][:, t, :],
                        in_=bank[:, t - 2 * i, :],
                        func=COPY,
                        scale=gain_columns[:, h, t : t + 1],
                    )

        open_banks = {}

        def z_pass(s, g):
            codes, scales = x_mx[s]
            for place in range(2):
                tokens = slice(P * place, P * (place + 1))
                for h in range(CHANNEL_PASSES):
                    if g == 0:
                        open_banks[(place, h)] = psum.tile([P, WORD, P], F32, name="direct_ps", bufs=DIRECT_BANKS)
                    for t in range(WORD):
                        m = first_column(g, h, t)
                        nc.tensor.matmul_mx(
                            out=open_banks[(place, h)][:, t, :],
                            lhsT=comp_codes[:, g, m : m + P].bitcast(MXFP8),
                            lhsT_scale=comp_scales[:, g, m : m + P],
                            rhs=codes[:, g, tokens].bitcast(MXFP8),
                            rhs_scale=scales[:, g, tokens],
                            start=(g == 0 and t == 0),
                            stop=(g == FEATURE_PASSES - 1 and t == WORD - 1),
                        )

        def z_narrow(i, h):
            s, place = divmod(i, 2)
            codes, scales = x_mx[s]
            tokens = slice(P * place, P * (place + 1))
            open_banks[(place, h)] = psum.tile([P, WORD, P], F32, name="sums_ps", bufs=SUM_BANKS)
            for t in range(WORD):
                for g in range(FEATURE_PASSES):
                    m = first_column(g, h, t)
                    nc.tensor.matmul_mx(
                        out=open_banks[(place, h)][:, t, :],
                        lhsT=comp_codes[:, g, m : m + P].bitcast(MXFP8),
                        lhsT_scale=comp_scales[:, g, m : m + P],
                        rhs=codes[:, g, tokens].bitcast(MXFP8),
                        rhs_scale=scales[:, g, tokens],
                        start=(g == 0),
                        stop=(g == FEATURE_PASSES - 1),
                    )

        def z_leave_narrow(i, h):
            s, place = divmod(i, 2)
            nc.vector.tensor_tensor(
                out=z_grouped[s][:, h, P * place : P * (place + 1), :],
                in0=open_banks[(place, h)][:].rearrange("p t n -> p n t"),
                in1=gain_columns[:, h, 0:WORD].unsqueeze(1).to_broadcast([P, P, WORD]),
                op=MULT,
            )

        tile_grouped = {}

        def z_leave_bank(i, h):
            if i not in tile_grouped:
                tile_grouped[i] = small([P, CHANNEL_PASSES, P, WORD], BF16, "tile_grouped")
            nc.vector.tensor_tensor(
                out=tile_grouped[i][:, h],
                in0=open_banks[(i % 2, h)][:].rearrange("p t n -> p n t"),
                in1=gain_columns[:, h, 0:WORD].unsqueeze(1).to_broadcast([P, P, WORD]),
                op=MULT,
            )

        def z_quantize_tile(i):
            codes = rotating.tile([P, CHANNEL_PASSES, P], U32, name="z_codes", bufs=4, align_bytes=64)
            scales = rotating.tile([P, CHANNEL_PASSES, P], U8, name="z_scales", bufs=4, align_bytes=64)
            nc.vector.quantize_mx(
                out=codes[:].rearrange("p h r -> p (h r)").bitcast(MXFP8),
                scales=scales[:].rearrange("p h r -> p (h r)"),
                in_=tile_grouped[i][:].rearrange("p h r t -> p (h r t)"),
            )
            for h in range(CHANNEL_PASSES):
                z_tile[(i, h)] = (codes[:, h], scales[:, h])

        def z_group_pool(s, h):
            if h == 0:
                z_grouped[s] = rotating.tile([P, CHANNEL_PASSES, PAIR, WORD], BF16, name="z_grouped", align_bytes=64)
            pool_copy(out=z_grouped[s][:, h], in_=z_rounded[(s, h)][:].rearrange("p t n -> p n t"))

        def z_group(s, h, copy):
            if h == 0:
                z_grouped[s] = rotating.tile([P, CHANNEL_PASSES, PAIR, WORD], BF16, name="z_grouped", align_bytes=64)
            copy(
                out=z_grouped[s][:, h].rearrange("p (k i) t -> p k t i", i=4),
                in_=z_rounded[(s, h)][:].rearrange("p t (k i) -> p k t i", i=4),
            )

        z_codes, z_scales = {}, {}

        def z_quantize(s, first, count):
            if first == 0:
                z_codes[s] = rotating.tile([P, CHANNEL_PASSES, PAIR], U32, name="z_codes", bufs=4, align_bytes=64)
                z_scales[s] = rotating.tile([P, CHANNEL_PASSES, PAIR], U8, name="z_scales", bufs=4, align_bytes=64)
            passes = slice(first, first + count)
            nc.vector.quantize_mx(
                out=z_codes[s][:, passes].rearrange("p h r -> p (h r)").bitcast(MXFP8),
                scales=z_scales[s][:, passes].rearrange("p h r -> p (h r)"),
                in_=z_grouped[s][:, passes].rearrange("p h r t -> p (h r t)"),
            )
            for h in range(first, first + count):
                z_mx[(s, h)] = (z_codes[s][:, h], z_scales[s][:, h])
                for place in range(2):
                    tokens = slice(P * place, P * (place + 1))
                    z_tile[(2 * s + place, h)] = (z_codes[s][:, h, tokens], z_scales[s][:, h, tokens])

        y_banks, results = {}, {}

        def y_direct(i, j):
            bank = psum.tile([P, HALF], F32, name="direct_ps", bufs=DIRECT_BANKS)
            for h in range(CHANNEL_PASSES):
                codes, scales = z_tile[(i, h)]
                nc.tensor.matmul_mx(
                    out=bank[:],
                    lhsT=codes.bitcast(MXFP8),
                    lhsT_scale=scales,
                    rhs=e_codes[:, j, h, :].bitcast(MXFP8),
                    rhs_scale=e_scales[:, j, h, :],
                    start=(h == 0),
                    stop=(h == CHANNEL_PASSES - 1),
                )
            y_banks[(i, j)] = bank

        def result(i):
            if i not in results:
                results[i] = rotating.tile(
                    [P, COPIES, COLUMNS], F32, name="result", tag="comp_then_products", bufs=RESULT_BUFS, align_bytes=64
                )
            return results[i]

        def multiply(i, j):
            columns = slice(HALF * j, HALF * (j + 1))
            nc.vector.tensor_tensor(
                out=result(i)[:, :, columns],
                in0=y_banks[(i, j)][:].unsqueeze(1).to_broadcast([P, COPIES, HALF]),
                in1=copy_gain_sb[:, :, columns],
                op=MULT,
            )

        def add_base(engine, i, c, first, last):
            part = results[i][:, c, first:last]
            engine.tensor_tensor(out=part, in0=part, in1=base_rows[i][:, c, first:last], op=ADD)

        def add_aside(i, c, first, last, target):
            nc.gpsimd.tensor_tensor(out=target, in0=results[i][:, c, first:last], in1=base_rows[i][:, c, first:last], op=ADD)

        def store_aside(i, c, first, last, target):
            nc.sync.dma_start(out=out[P * i : P * (i + 1), COLUMNS * c + first : COLUMNS * c + last], in_=target)

        def store_columns(i, c, first, last):
            store_aside(i, c, first, last, results[i][:, c, first:last])

        def store(i, c, first=0, count=2):
            columns = slice(HALF * first, HALF * (first + count))
            rows = out[P * i : P * (i + 1), :].rearrange("p (c n) -> p c n", c=COPIES)
            nc.sync.dma_start(out=rows[:, c, columns], in_=results[i][:, c, columns])

        turned_products = {}

        turned_banks = {}

        def y_transposed_mm(s, j, tag="direct_ps", bufs=DIRECT_BANKS, blocks=range(BLOCKS)):
            banks = turned_banks.setdefault((s, j), [])
            for b in blocks:
                if b % 2 == 0:
                    banks.append(psum.tile([P, 2, PAIR], F32, name=tag, bufs=bufs))
                columns = slice(P * b, P * (b + 1))
                for h in range(CHANNEL_PASSES):
                    codes, scales = z_mx[(s, h)]
                    nc.tensor.matmul_mx(
                        out=banks[b // 2][:, b % 2, :],
                        lhsT=e_codes[:, j, h, columns].bitcast(MXFP8),
                        lhsT_scale=e_scales[:, j, h, columns],
                        rhs=codes.bitcast(MXFP8),
                        rhs_scale=scales,
                        start=(h == 0),
                        stop=(h == CHANNEL_PASSES - 1),
                    )

        def turned_out(s, j, c):
            banks = turned_banks[(s, j)]
            turned = rotating.tile([P, BLOCKS, PAIR], F32, name="turned", tag="rows", bufs=ROW_BUFS, align_bytes=64)
            for b in range(BLOCKS):
                column = WORD + c * (COLUMNS // P) + BLOCKS * j + b
                nc.scalar.activation(
                    out=turned[:, b, :],
                    in_=banks[b // 2][:, b % 2, :],
                    func=COPY,
                    scale=gain_columns[:, 0, column : column + 1],
                )
            turned_products[(s, j, c)] = turned

        back_banks, totals = {}, {}

        def turn_back(i, j, c, tag="turned_ps", bufs=TURN_BANKS):
            s, place = divmod(i, 2)
            bank = psum.tile([P, BLOCKS, P], F32, name=tag, bufs=bufs)
            for b in range(BLOCKS):
                nc.tensor.transpose(
                    bank[:, b, :], turned_products[(s, j, c)][:, b, P * place : P * (place + 1)], identity[:]
                )
            back_banks[(i, j, c)] = bank

        def add_turned(i, j, c):
            columns = slice(HALF * j, HALF * (j + 1))
            nc.vector.tensor_tensor(
                out=result(i)[:, c, columns],
                in0=back_banks[(i, j, c)][:].rearrange("p b n -> p (b n)"),
                in1=base_rows[i][:, c, columns],
                op=ADD,
            )

        def pool_copy(out, in_):
            nc.gpsimd.tensor_scalar(out=out, in0=in_, scalar1=1.0, scalar2=0.0, op0=MULT, op1=ADD)


        fill_tiles()
        V, S = nc.vector.tensor_copy, nc.scalar.copy
        VE, G = nc.vector, nc.gpsimd
        load_scales(a_scales_raw, a_scales)
        load_codes(a_codes_raw, a_words, 0)
        load_codes(d_codes, d_words, 0)
        load_scales(d_scales_sb, d_scales)
        load_codes(a_codes_raw, a_words, 1)
        load_comp_half(0)
        load_comp_half(1)
        load_codes(d_codes, d_words, 1)
        load_comp(1)
        load_x(0)
        load_gains()
        load_x(1)
        load_comp(2)
        load_comp(3)
        for i in range(2, 6):
            load_x(i)
        load_copy_gain()
        load_x(6)
        load_base(0)
        load_x(7)
        for i in range(1, 8):
            load_base(i)

        permute_a_scales(0, range(1))
        warm_up()
        permute_a_scales(0, range(1, 4))
        permute_a(0)
        permute_a_scales(1)
        e_part(0)
        permute_a(1)
        comp_group_half(0)
        e_part(1)
        comp_group_half(1)
        comp_quantize_half(0)
        comp_quantize_half(1)
        e_part(2)
        comp_group(1, 0, 4, V)
        e_matmul(3, 0)
        x_transpose(0)
        x_transpose(1, "sums_ps", SUM_BANKS)
        e_matmul(3, 1)
        widen_gains()
        e_matmul(3, 2)
        e_matmul(3, 3)
        turn_gains()
        e_quantize(0)
        comp_quantize(1, 0, 4)
        x_quantize(0)
        comp_group(2, 0, 3, V)
        comp_group(2, 3, 1, S)
        comp_group(3, 2, 2, S)
        comp_group(3, 0, 2, V)
        comp_quantize(2, 0, 4)
        comp_quantize(3, 0, 4)
        x_sort(4, V)
        e_quantize(1)
        z_pass(0, 0)
        z_pass(0, 1)
        x_transpose(2)
        x_transpose(3, "sums_ps", SUM_BANKS)
        x_sort(5, S)
        z_pass(0, 2)
        z_pass(0, 3)
        x_transpose(4)
        x_quantize(1)
        for i in range(2):
            z_leave_bank(i, 0)
            z_leave_bank(i, 1)
        z_quantize_tile(0)
        z_quantize_tile(1)

        x_transpose(5, "sums_ps", SUM_BANKS)
        z_matmul(1, 0, "turned_ps", TURN_BANKS)
        x_sort(6, S)
        x_quantize(2)
        z_group_pool(1, 0)
        y_direct(0, 0)
        y_direct(1, 0)
        y_direct(0, 1)
        y_direct(1, 1)
        def multiply_pair(s):
            i = 2 * s
            multiply(i, 0)
            add_base(G, i, 0, 0, HALF)
            add_base(G, i, 1, 0, POOL_COLUMNS)
            multiply(i + 1, 0)
            multiply(i, 1)
            multiply(i + 1, 1)
        def turned(s, j):
            y_transposed_mm(s, j)
            turned_out(s, j, 0)
            turned_out(s, j, 1)
        multiply_pair(0)
        x_sort(7, S)
        z_matmul(1, 1)
        add_base(VE, 0, 0, HALF, COLUMNS)
        store(0, 0)
        add_base(VE, 1, 0, 0, COLUMNS)
        store(1, 0)
        z_group(1, 1, S)
        x_transpose(6)
        x_transpose(7, "direct_ps", DIRECT_BANKS)
        z_matmul(2, 0)
        z_quantize(1, 0, 2)
        add_base(VE, 0, 1, POOL_COLUMNS, COLUMNS)
        store(0, 1)
        add_base(VE, 1, 1, 0, HALF)
        store_columns(1, 1, 0, HALF)
        x_quantize(3)
        aside = x_grouped[3][:, 0].rearrange("p n t -> p (n t)").bitcast(F32)
        add_aside(1, 1, HALF, COLUMNS, aside)
        store_aside(1, 1, HALF, COLUMNS, aside)
        y_direct(2, 0)
        y_direct(3, 0)
        z_group(2, 0, S)
        z_matmul(2, 1, "turned_ps", TURN_BANKS)
        y_direct(2, 1)
        y_direct(3, 1)
        multiply_pair(1)
        store_columns(2, 0, 0, HALF)
        store_columns(2, 1, 0, POOL_COLUMNS)
        z_group(2, 1, S)
        z_matmul(3, 0, "direct_ps", DIRECT_BANKS)
        TU, SU, DI = ("turned_ps", TURN_BANKS), ("sums_ps", SUM_BANKS), ("direct_ps", DIRECT_BANKS)
        def back(s, j, c, tags):
            for i, tag in zip((2 * s, 2 * s + 1), tags):
                turn_back(i, j, c, *tag)
        def tadd(s, j, c):
            for i in (2 * s, 2 * s + 1):
                add_turned(i, j, c)
                store(i, c, j, 1)
        z_quantize(2, 0, 2)
        add_base(VE, 2, 0, HALF, COLUMNS)
        store_columns(2, 0, HALF, COLUMNS)
        add_base(VE, 3, 0, 0, COLUMNS)
        store(3, 0)
        add_base(VE, 2, 1, POOL_COLUMNS, COLUMNS)
        store_columns(2, 1, POOL_COLUMNS, COLUMNS)
        z_group(3, 0, S)
        z_narrow(6, 1)
        y_transposed_mm(2, 0, *TU)
        turned_out(2, 0, 0)
        turned_out(2, 0, 1)
        z_narrow(7, 1)
        y_transposed_mm(2, 1)
        turned_out(2, 1, 0)
        turned_out(2, 1, 1)
        add_base(VE, 3, 1, 0, HALF)
        store_columns(3, 1, 0, HALF)
        z_leave_narrow(6, 1)
        z_leave_narrow(7, 1)
        add_base(VE, 3, 1, HALF, COLUMNS)
        store_columns(3, 1, HALF, COLUMNS)
        z_quantize(3, 0, 2)
        back(2, 0, 0, (DI, DI))
        back(2, 0, 1, (TU, TU))
        tadd(2, 0, 0)
        tadd(2, 0, 1)
        y_transposed_mm(3, 0, *SU)
        turned_out(3, 0, 0)
        turned_out(3, 0, 1)
        back(2, 1, 0, (DI, DI))
        back(2, 1, 1, (TU, TU))
        tadd(2, 1, 0)
        tadd(2, 1, 1)
        y_transposed_mm(3, 1)
        turned_out(3, 1, 0)
        turned_out(3, 1, 1)
        back(3, 0, 0, (DI, DI))
        back(3, 0, 1, (TU, TU))
        tadd(3, 0, 0)
        tadd(3, 0, 1)
        back(3, 1, 0, (SU, SU))
        back(3, 1, 1, (DI, DI))
        tadd(3, 1, 0)
        tadd(3, 1, 1)
